import numpy as np, ml_dtypes
CORES = [35,38,43,46]
N = 4
import mx_ref
BF = ml_dtypes.bfloat16
def entries(a):
    return np.ascontiguousarray(a.T).reshape(-1)
def table(e):
    return np.ascontiguousarray(np.reshape(e, (-1, 16)).T).astype(np.int32)
def pick(q, e):
    c = np.concatenate([q[0].reshape(128, -1, 4), np.zeros((128, 1, 4), np.uint8)], axis=1); s = np.concatenate([q[1], np.ones((16, 1), np.uint8)], axis=1)
    return (np.ascontiguousarray(c[:, e].reshape(128, -1)), np.ascontiguousarray(s[:, e]))
def join(*qs):
    return (np.concatenate([q[0] for q in qs], axis=1), np.concatenate([q[1] for q in qs], axis=1))
def put(q, e, v):
    c, s = q[0].reshape(128, -1, 4).copy(), q[1].copy(); c[:, e] = v[0].reshape(128, -1, 4); s[:, e] = v[1]
    return (c.reshape(128, -1), s)
def pk(c, s):
    return (np.ascontiguousarray(c), mx_ref.live(s))
def emit(q):
    return q[0], q[1]
def decode(q):
    o = []
    for b in range(4):
        e = np.zeros((128, 128, 4), np.float32); e[np.arange(128), np.arange(128), b] = 1
        o.append(mx_ref.matmul(mx_ref.quantize(e.reshape(128, 512).astype(BF)), q))
    return np.stack(o, axis=2).reshape(128, -1)
def f(rng, *shape):
    return mx_ref.flush((rng.standard_normal(shape, dtype=np.float32) * np.exp2(rng.integers(-2, 3, shape[:-1] + (1,)))).astype(BF))
def wide(rng, *shape, cols=0):
    v = rng.standard_normal(shape, dtype=np.float32) * np.exp2(rng.integers(-12, 13, shape)).astype(np.float32)
    if cols: v *= np.repeat(np.exp2(rng.integers(-cols, cols + 1, shape[:-2] + (1, shape[-1] // 4))) * (rng.random(shape[:-2] + (1, shape[-1] // 4)) > 0.0625), 4, axis=-1).astype(np.float32)
    return mx_ref.flush(v.astype(BF))
P, F, R = 256, 48, 3
def big(v):
    v = np.array(v, np.float32)
    v[np.abs(v) < np.float32(2.0 ** -16)] = 0
    return v.astype(BF)
def share(v):
    return big(np.ascontiguousarray(v.reshape(128, N, 4 * P).transpose(1, 0, 2)))
def links(nb):
    return np.concatenate([entries(nb[r]).reshape(P, 3) for r in range(N)])
def graph(rng, ends=False):
    to, far, n = np.zeros((N * P, 3), int), [], P - (N - 1) * F
    for r in range(N):
        a, i = P * r + rng.permutation(P), 0
        while i < P:
            m = min(2 * int(rng.integers(2, 17)), P - i)
            if P - i - m < 4: m = P - i
            for k in range(2):
                c = np.roll(a[i:i + m], -k)
                to[c[0::2], k], to[c[1::2], k] = c[1::2], c[0::2]
            i += m
        if ends:
            h = rng.permutation(a[a < to[a, 0]])[:n]
            e = np.where(rng.random(n) < 0.5, h, to[h, 0])
        else: e = rng.permutation(a)[:n]
        far.append(rng.permutation(np.setdiff1d(a, e)).reshape(N - 1, F))
        for i in range(0, n, 2):
            if e[i + 1] in to[e[i], :2]:
                for j in range(0, n, 2):
                    if j != i and e[j + 1] not in to[e[i], :2] and e[i + 1] not in to[e[j], :2]:
                        e[i + 1], e[j + 1] = e[j + 1], e[i + 1]
                        break
        to[e[0::2], 2], to[e[1::2], 2] = e[1::2], e[0::2]
    for r in range(N):
        for q in range(r + 1, N):
            u, v = far[r][q - 1], far[q][r]
            to[u, 2], to[v, 2] = v, u
    return to
def inputs(rng, x, to):
    return {"x": x, "nb": np.stack([table(to[P * r:P * r + P].reshape(-1)) for r in range(N)]), "w": f(rng, N, 128, 512)}
def setup_inputs(rng):
    return inputs(rng, big(f(rng, N, 128, 4 * P)), graph(rng))
def setup_inputs_far(rng):
    to, n = graph(rng), np.arange(N * P)
    v = (1 + 0.5 * rng.random((128, N * P, 4))) * rng.choice([-1.0, 1.0], (128, N * P, 4))
    a = n[(to[:, 2] // P != n // P) & (n < to[:, 2])]
    b = to[a, 2]
    v[:, b] = np.abs(v[:, b]) * np.sign(v[:, a]) * np.where(rng.random((128, a.size, 4)) < 0.125, -1.0, 1.0)
    return inputs(rng, share(v), to)
def setup_inputs_none(rng):
    to, n, z = graph(rng, ends=True), np.arange(N * P), int(rng.integers(0, N))
    own = n // P == z
    size = np.where(own & (to[:, 2] // P == z), 0.125, 1.0)
    color = np.full(N * P, -1)
    for a in n[n < to[:, 0]]:
        both = np.array([a, to[a, 0]])
        near = color[to[both, 1:]].reshape(-1).tolist()
        color[both] = next(int(c) for c in rng.permutation(5) if c not in near)
    v = rng.choice([-1.0, 1.0], (128, N * P, 4))
    a = n[(to[:, 2] // P != n // P) & (n < to[:, 2])]
    v[:, to[a, 2]] = v[:, a]
    v[:40] = np.where((np.arange(40) // 8)[:, None, None] == color[None, :, None], 8.0, 0.0)
    v[40:48] = 64.0
    v = np.where(own[None, :, None], (1 + 0.5 * rng.random((128, N * P, 4))) * size[None, :, None], 16.0 * v)
    return inputs(rng, share(v), to)
def setup_inputs_spread(rng):
    return inputs(rng, big(wide(rng, N, 128, 4 * P, cols=6)), graph(rng))
def setup_inputs_ties(rng):
    to = graph(rng)
    t = f(rng, 128, 12).astype(np.float32).reshape(128, 3, 4)
    five = np.concatenate([t, 0 - t[:, :1], np.zeros((128, 1, 4), np.float32)], axis=1)
    e = rng.integers(0, 5, N * P)
    for r in range(N):
        j = P * r + int(rng.integers(0, P))
        e[to[j]] = 0
        e[to[to[j]].reshape(-1)] = 0
    return inputs(rng, share(five[:, e]), to)
def setup_inputs_twice(rng):
    to, large = graph(rng), np.zeros(N * P, bool)
    v = np.abs(rng.standard_normal((128, N * P, 4))) * np.exp2(rng.integers(-1, 2, (1, N * P, 1)))
    for i in range(P // 32):
        for r in rng.permutation(N):
            for j in rng.permutation(P):
                n1 = P * r + j
                n2 = to[n1, 1]
                p = np.array([to[n1, 0], n1, n2, to[n2, 0]])
                if i == 0:
                    m = to[[n1, n2], 2]
                    q = np.concatenate([p, m])
                    if large[q].any() or large[to[q]].any() or np.count_nonzero(np.isin(to[q], q)) != 10: continue
                    size = np.concatenate([rng.choice([1.0, 1.25], (128, 4, 4)), rng.choice([3.5, 4.0], (128, 2, 4))], axis=1) * 2.0 ** 26
                    v[:, q] = size * rng.choice([-1.0, 1.0], (128, 1, 4)) * np.array([1.0, 1.0, -1.0, -1.0, -1.0, 1.0])[None, :, None]
                    large[q] = True
                    large[to[m]] = True
                    break
                if large[p].any() or large[to[p]].any() or np.isin(to[p, 2], p).any() or to[p[0], 1] == p[3]: continue
                large[p] = True
                v[:, p] = (1 + 0.5 * rng.random((128, 4, 4))) * np.array([256.0, 64.0, 64.0, 256.0])[None, :, None]
                break
    return inputs(rng, share(v), to)
def check_inputs(d):
    b = []
    for k, low, high in (("x", -16, 28), ("w", -30, 30)):
        v = np.abs(d[k].astype(np.float32))
        if not (np.isfinite(v).all() and ((v == 0) | (v >= 2.0 ** low) & (v <= 2.0 ** high)).all()): b.append("a value of " + k)
    to, n = links(d["nb"]), np.arange(N * P)
    if to.min() < 0 or to.max() >= N * P: return b + ["range of nb"]
    for k in range(3):
        if (to[to[:, k], k] != n).any() or (to[:, k] == n).any(): b.append("edges k = %d are no pairs" % k)
    if (to[:, :2] // P != n[:, None] // P).any(): b.append("an edge k = 0 or 1 leaves its rank")
    if (to[:, 0] == to[:, 1]).any() or (to[:, 0] == to[:, 2]).any() or (to[:, 1] == to[:, 2]).any(): b.append("two edges of a node lead to the same node")
    c = np.zeros((N, N), int)
    np.add.at(c, (n // P, to[:, 2] // P), 1)
    if (c[~np.eye(N, dtype=bool)] != F).any(): b.append("number of edges between two ranks")
    return b
def scores(h, to):
    s = np.zeros((N * P, 3), np.float32)
    for i in range(0, N * P, 128):
        a = pick(h, np.arange(i, i + 128))
        for k in range(3): s[i:i + 128, k] = np.diagonal(mx_ref.matmul(a, pick(h, to[i:i + 128, k]))) + np.float32(0)
    return s
def reference(x, nb, w):
    to, n = links(nb), np.arange(N * P)
    h = join(*[mx_ref.quantize(np.ascontiguousarray(x[r])) for r in range(N)])
    merged, pr = np.zeros((N * P, 3), bool), np.zeros((N, R, P), np.float32)
    for t in range(R):
        s = scores(h, to)
        s[merged] = -np.inf
        c = np.argmax(s, axis=1)
        v = to[n, c]
        met = c[v] == c
        merged[n[met], c[met]] = True
        pr[:, t] = np.where(met, v, -1).reshape(N, P)
        d = decode(h).reshape(128, N * P, 4)
        m = np.float32(0.5) * d + np.float32(0.5) * d[:, np.where(met, v, n)]
        new = mx_ref.quantize(np.ascontiguousarray(m.reshape(128, -1).astype(BF)))
        h = pick(join(h, new), np.where(met, N * P + n, n))
    oc, osc, y = np.zeros((N, 128, 4 * P), np.uint8), np.zeros((N, 16, P), np.uint8), np.zeros((N, 128, P), np.float32)
    for r in range(N):
        own = pick(h, np.arange(P * r, P * r + P))
        oc[r], osc[r] = emit(own)
        y[r] = mx_ref.matmul(mx_ref.quantize(np.ascontiguousarray(w[r])), own)
    return {"oc": oc, "osc": osc, "pr": pr, "y": y}

@@ -1,0 +1,494 @@
+from concourse.bass import DstId, RemoteDMATransfer
+from concourse.mybir import dt, AluOpType as A, AxisListType, ActivationFunctionType as AF
+
+P, F, R = 256, 48, 3
+FAR = {1: (0, 48), 3: (160, 208), 2: (208, 256)}
+LOC = (48, 160)
+BIG = 1e29
+BANKS = ((4, 5, 6, 7), (4, 5, 6, 7), (2, 3, 0, 1))
+VPARTS = (0, 1)
+AHEAD = (("u", 0, 0), ("u", 0, 1), ("u", 0, 2), ("u", 0, 3))
+BESIDE = (("q", 0), ("u", 2, 0), ("u", 2, 1), ("u", 1, 0), ("u", 1, 1), ("u", 1, 2), ("u", 1, 3), ("q", 1), ("l",), ("u", 2, 2), ("u", 2, 3))
+AFTER = (("q", 2),)
+
+
+def _bufs():
+    b = {}
+    def sb(name, n, d="float32"): b[name] = ("sbuf", [128, n], d)
+    def mx(name, n):
+        sb(name + "c", n, "float8_e4m3fn_x4")
+        sb(name + "s", n, "uint8")
+    sb("nbT", 48, "int32"); sb("xb", 1024, "bfloat16"); sb("wb", 512, "bfloat16")
+    mx("X", 256); mx("wq", 128); mx("E", 512); mx("H", 256); mx("Z", 256)
+    for t in range(R):
+        mx("W%d" % t, 1024); mx("N%d" % t, 512); mx("M%d" % t, 256)
+        sb("fl%d" % t, 4); sb("m01_%d" % t, 2); sb("RC%d" % t, 272, "bfloat16"); sb("U%d" % t, 16, "uint16")
+        for name in ("S0_", "S1_", "Ls"): sb("%s%d" % (name, t), 64)
+        sb("PRp%d" % t, 256); sb("PRn%d" % t, 256)
+    for k in range(3): sb("h%d" % k, 1024, "bfloat16")
+    sb("hE", 516, "bfloat16"); sb("Ho", 1024, "bfloat16")
+    for name, n in (("pI", 1), ("rI", 1), ("gI", 1), ("uI", 1), ("aP", 1), ("yI", 256), ("wI", 256), ("rhoI", 1), ("zI", 48),
+                    ("lP", 48), ("aI", 48), ("nbI", 48), ("kI", 32), ("kA", 32)): sb(name, n, "int32")
+    for name, n in (("pF", 1), ("I", 128), ("mF", 256), ("rF", 1), ("g16", 1), ("gG", 1), ("rho", 1), ("o48", 48), ("z48", 48), ("z3", 48), ("M48", 48),
+                    ("Fw", 1024), ("mk", 48), ("t2a", 16), ("T2", 16), ("RK", 256), ("dk", 256), ("nK", 2), ("sg", 2), ("jk", 512), ("Tn", 16), ("c0", 32),
+                    ("kh", 32), ("k1", 32), ("kap", 32), ("hP", 48), ("kP", 48), ("lQ", 64), ("kP0", 1), ("mk0", 2), ("MS", 3), ("NP", 6), ("dN", 2), ("Bm", 48), ("c8", 48),
+                    ("dg", 792), ("dh", 792), ("Sc", 6), ("ge", 2), ("c01", 2), ("d2c", 2), ("gt", 2), ("ga", 2), ("A2", 2), ("Qf", 3), ("Tf", 3), ("ckB", 6), ("ngB", 2), ("mB", 16), ("mP", 2), ("ckm", 6),
+                    ("EB", 48), ("io", 1032), ("Rn", 768), ("NR", 1024), ("yo", 256)): sb(name, n)
+    for name, n in (("TS", 64), ("TT", 64), ("Rp", 256), ("dA", 256), ("tA", 256), ("iJ", 256), ("Rpi", 256), ("tI", 256), ("dB", 256), ("tB", 256), ("Rpn", 256), ("Rq", 768), ("d2", 768), ("t2", 768),
+                    ("TC", 64), ("TD", 64), ("RO", 256), ("ROt", 256), ("RT", 256), ("RV", 256), ("RVt", 256)): sb(name, n, "bfloat16")
+    for name, n in (("T2u", 16), ("lA", 16), ("lB", 16), ("lM", 16), ("posU", 16), ("piU", 16), ("nbL", 48), ("nbU", 48), ("lG", 48), ("lN", 48), ("nU", 32), ("n2U", 8), ("LV", 16), ("CLd", 16)): sb(name, n, "uint16")
+    for i in range(8): b["ps%d" % i] = ("psum", [128, 512], "float32")
+    return b
+
+
+def _pack(b):
+    out, place, fill = {}, {}, {"float32": 0, "int32": 0, "uint16": 0, "bfloat16": 0}
+    fixed = ("nbT", "xb", "wb", "hE", "pF", "mF", "I", "Ho", "h0", "h1", "h2", "fl0", "fl1", "fl2", "m01_0", "m01_1", "m01_2")
+    for name, (where, shape, d) in b.items():
+        place[name] = (name, 0)
+        if where != "sbuf" or d not in fill or name in fixed: out[name] = (where, shape, d)
+        else:
+            place[name] = ("pool_" + d, fill[d])
+            fill[d] += (shape[1] + 31) // 32 * 32
+    for d, n in fill.items(): out["pool_" + d] = ("sbuf", [128, n], d)
+    return out, place
+
+
+SCRATCH, PLACE = _pack(_bufs())
+WIDTH = {k: v[1][1] for k, v in _bufs().items()}
+SEMAPHORES = ["qv", "qs", "qt", "qg", "ldn", "ldx", "ldw", "ls", "st"] + ["x%s%d" % (k, t) for k in "csm" for t in range(R)]
+
+
+def shares(T, topo, core):
+    peer = {d: T.cores[T.rank_of(core) ^ d] for d in FAR}
+    may = {d: topo.engines(core, c) for d, c in peer.items()}
+    away = [d for d in FAR if topo.chip(peer[d]) != topo.chip(core)]
+    eng, used = {}, []
+    for d in sorted(FAR, key=lambda d: (d not in away, d)):
+        free = [e for e in may[d] if e not in used]
+        eng[d] = free[:len(may[d]) // len(away)] if d in away else free[::2][:4]
+        used += eng[d]
+    return peer, eng
+
+
+def rank_program(g, core, T, topo):
+    rank = T.rank_of(core)
+    if rank is None: return
+    queues = {"v": g.vector, "s": g.scalar, "t": g.tensor, "g": g, "y": g.sync}
+    qsem = {"v": "qv", "s": "qs", "t": "qt", "g": "qg"}
+    count = {k: 0 for k in qsem.values()}
+    known = {q: {} for q in queues}
+    writes, reads = {}, {}
+
+    def norm(r): return (r[0], r[1], r[2], r[3] if len(r) > 3 else 1)
+
+    def clash(x, y):
+        if x[2] <= y[1] or y[2] <= x[1]: return False
+        if x[3] == y[3]: return x[3] == 1 or (x[1] - y[1]) % x[3] == 0
+        if x[3] > 1 and y[3] > 1: return True
+        (s, a, b), (c, e) = ((x[3], x[1], x[2]), y[1:3]) if x[3] > 1 else ((y[3], y[1], y[2]), x[1:3])
+        return a + max(0, -((a - c) // s)) * s < min(b, e)
+
+    def need(q, rd, wr, acc=False):
+        evs = []
+        for r in map(norm, rd): evs += [e for w, e in writes.get(r[0], []) if clash(w, r)]
+        for r in map(norm, wr):
+            evs += [e for w, e in writes.get(r[0], []) if clash(w, r) and not (acc and e[3] == "t")]
+            evs += [e for w, e in reads.get(r[0], []) if clash(w, r)]
+        evs.sort(key=lambda e: -e[1])
+        for sem, val, snap, _q in evs:
+            if known[q].get(sem, 0) >= val: continue
+            queues[q].wait_ge(T.sem[sem], val)
+            known[q][sem] = val
+            for k, v in snap.items(): known[q][k] = max(known[q].get(k, 0), v)
+
+    def note(ev, rd, wr):
+        for r in rd: reads.setdefault(r[0], []).append((norm(r), ev))
+        for r in map(norm, wr):
+            inside = lambda w: w[1] >= r[1] and w[2] <= r[2] and r[3] == 1
+            writes[r[0]] = [(w, e) for w, e in writes.get(r[0], []) if not inside(w)] + [(r, ev)]
+            reads[r[0]] = [(w, e) for w, e in reads.get(r[0], []) if not inside(w)]
+
+    def run(q, fn, rd, wr, acc=False):
+        need(q, rd, wr, acc)
+        sem = qsem[q]
+        count[sem] += 1
+        fn(queues[q]).then_inc(T.sem[sem], 1)
+        note((sem, count[sem], dict(known[q]), q), rd, wr)
+
+    def arrives(sem, val, wr): note((sem, val, {}, "d"), [], wr)
+
+    def ap(r, p=None):
+        name, a, b, st = norm(r)
+        buf, o = PLACE[name]
+        rows = slice(p[0], p[1]) if p else slice(None)
+        return T[buf][rows, o + a:o + b:st] if st != 1 else T[buf][rows, o + a:o + b]
+
+    def words(r): return ap(r).bitcast(dt.uint32)
+    def octets(r): return ap(r).bitcast(dt.uint8)
+    def W(n): return (n, 0, WIDTH[n])
+    def sc(s): return ap(s) if isinstance(s, tuple) else s
+    def tt(out, in0, in1, op): run("v", lambda e: e.tensor_tensor(ap(out), ap(in0), ap(in1), op), [in0, in1], [out])
+    def ts(out, in0, s1, op0, s2=None, op1=None):
+        rd = [in0] + [s for s in (s1, s2) if isinstance(s, tuple)]
+        if op1 is None: run("v", lambda e: e.tensor_scalar(ap(out), ap(in0), sc(s1), None, op0), rd, [out])
+        else: run("v", lambda e: e.tensor_scalar(ap(out), ap(in0), sc(s1), sc(s2), op0, op1), rd, [out])
+    def cp(out, in_, q="v"):
+        if q == "v": run("v", lambda e: e.tensor_copy(ap(out), ap(in_)), [in_], [out])
+        else: run("s", lambda e: e.activation(ap(out), ap(in_), AF.Copy), [in_], [out])
+    def plus(out, in_, bias, scale=1.0):
+        rd = [in_] + [x for x in (bias, scale) if isinstance(x, tuple)]
+        run("s", lambda e: e.activation(ap(out), ap(in_), AF.Identity, bias=sc(bias), scale=sc(scale)), rd, [out])
+    def times(out, in_, col): run("s", lambda e: e.activation(ap(out), ap(in_), AF.Copy, scale=ap(col)), [in_, col], [out])
+    def ms(out, c): run("v", lambda e: e.memset(ap(out), c), [], [out])
+    def rsum(out, in_, negate=False): run("v", lambda e: e.tensor_reduce(ap(out), ap(in_), AxisListType.X, A.add, negate=negate), [in_], [out])
+    def tp(out, in_): run("v", lambda e: e.transpose(ap(out), ap(in_)), [in_], [out])
+    def gather(out, win, off, q="v"):
+        if q == "v": run("v", lambda e: e.tensor_copy(ap(out), ap(win).indirect(ap(off))), [win, off], [out])
+        else: run("s", lambda e: e.activation(ap(out), ap(win).indirect(ap(off)), AF.Copy), [win, off], [out])
+    def pick(out, win, off, what="cs"):
+        oc, wc, os_, ws = [(r[0] + x, r[1], r[2]) for x in "cs" for r in (out, win)]
+        if "c" in what: run("v", lambda e: e.tensor_copy(words(oc), words(wc).indirect(ap(off))), [wc, off], [oc])
+        if "s" in what: run("s", lambda e: e.activation(ap(os_), ap(ws).indirect(ap(off)), AF.Copy), [ws, off], [os_])
+    def quant(out, in_):
+        c, s = (out[0] + "c", out[1], out[2]), (out[0] + "s", out[1], out[2])
+        run("v", lambda e: e.quantize_mx(ap(c), ap(s), ap(in_)), [in_], [c, s])
+    def mm(bank, n, w, x, start=True, stop=True):
+        wc, ws, xc, xs = (w[0] + "c", w[1], w[2]), (w[0] + "s", w[1], w[2]), (x[0] + "c", x[1], x[2]), (x[0] + "s", x[1], x[2])
+        run("t", lambda e: e.matmul_mx(ap(("ps%d" % bank, 0, n)), ap(wc), ap(ws), ap(xc), ap(xs), start, stop), [wc, ws, xc, xs], [("ps%d" % bank, 0, 512)], acc=not start)
+    def iota(out, pattern, base, cm):
+        if PLACE[out[0]][0] == "pool_int32": run("g", lambda e: e.iota(ap(out), pattern, base, cm), [], [out])
+        else: run("g", lambda e: e.iota(ap(out), pattern, base, cm, allow_small_or_imprecise_dtypes=True), [], [out])
+    def settle():
+        if known["g"].get("qg", 0) < count["qg"]: g.wait_ge(T.sem.qg, count["qg"])
+        known["g"]["qg"] = count["qg"]
+    def pb(out, in_, p): run("g", lambda e: e.partition_broadcast(ap(out), ap(in_, (p, p + 1)), 128), [in_], [out])
+    def spread(row, col):
+        settle()
+        for a in range(4): pb((row, 64 * a, 64 * a + 64), (col, 0, 64), 32 * a)
+    def D(f, *a): return lambda: f(*a)
+    def weave(*chains):
+        for i in range(max(map(len, chains))):
+            for c in chains:
+                if i < len(c): c[i]()
+
+    peer, eng = shares(T, topo, core)
+    incoming = sum(len(shares(T, topo, c)[1][d]) for d, c in peer.items())
+    sent = [0]
+
+    def send(what, sem):
+        tr = []
+        for d in eng:
+            src, dst, region = what(d)
+            need("g", [region], [])
+            rid, pid, _s = topo.addr(peer[d])
+            tr.append(RemoteDMATransfer(dst_ids=[DstId(rid=rid, pnc=pid)], dma_engine_mask=sum(1 << e for e in eng[d]), remote_sem=T.sem[sem], src=src, dst=dst))
+            sent[0] += len(eng[d])
+        g.remote_dma_fused(tr, local_sem=T.sem.ls)
+
+    for i in range(8):
+        q = g.sync if i % 2 == 0 else g.scalar
+        q.dma_start(T.nbT[16 * i:16 * i + 16, :], T.nb[:, :]).then_inc(T.sem.ldn, 16)
+    arrives("ldn", 128, [W("nbT")])
+    g.sync.dma_start(T.xb[:, :], T.x[:, :]).then_inc(T.sem.ldx, 16)
+    arrives("ldx", 16, [W("xb")])
+    g.sync.dma_start(T.wb[:, :], T.w[:, :]).then_inc(T.sem.ldw, 16)
+    arrives("ldw", 16, [W("wb")])
+
+    iota(W("pI"), [[0, 1]], 0, 1)
+    iota(W("o48"), [[0, 16], [1, 3]], 0, 0)
+    iota(W("pF"), [[0, 1]], 0, 1)
+    iota(W("mF"), [[1, 256]], 0, 0)
+    iota(W("yI"), [[256, 16], [11, 16]], 10, 0)
+    iota(W("c8"), [[0, 6], [1, 8]], 0, 0)
+    for q in (3, 0, 1, 2):
+        c, r = q ^ rank ^ 1, ("Fw", 256 * q, 256 * q + 256)
+        if q == 3: ms(r, 1048576.0 * c)
+        elif q < rank: plus(r, W("mF"), 1048576.0 * c, 4096.0)
+        else: plus(r, W("mF"), 1048576.0 * c, 0.0)
+    cp(W("iJ"), W("mF"), "s")
+    for q in range(4): plus(("io", 256 * q, 256 * q + 256), W("mF"), 256.0 * q)
+    plus(("io", 1024, 1032), ("mF", 0, 8), 1024.0)
+    plus(("NR", 0, 256), W("mF"), -1.0, 0.0)
+
+    def kappa(v, ai, h, s, out):
+        return [D(ts, h, v, 128.0, A.is_ge, 96.0, A.mult), D(ts, ai, v, 96, A.bitwise_and), D(tt, s, v, ai, A.add), D(tt, out, s, h, A.subtract)]
+
+    ts(W("rI"), W("pI"), 15, A.bitwise_and)
+    ts(W("gI"), W("pI"), 4, A.logical_shift_right)
+    cp(W("rF"), W("rI"))
+    ts(W("uI"), W("gI"), 1, A.bitwise_and)
+    weave([D(ts, W("z48"), W("o48"), W("rF"), A.add, 1.0, A.add), D(ts, W("zI"), W("z48"), 1.0 / 3.0, A.mult), D(ts, W("z3"), W("zI"), 3.0, A.mult), D(tt, W("M48"), W("z3"), W("z48"), A.is_equal)],
+          [D(ts, W("rhoI"), W("rF"), 3.0, A.mult, 2.0, A.add), D(ts, W("rhoI"), W("rhoI"), 15, A.bitwise_and), D(cp, W("rho"), W("rhoI"))],
+          [D(ts, W("g16"), W("uI"), 16.0, A.mult), D(ms, W("TS"), 0.0), D(ms, W("TC"), 0.0)])
+
+    weave([D(tt, W("mk"), W("nbT"), W("M48"), A.mult), D(tt, W("t2a"), ("mk", 0, 48, 3), ("mk", 1, 48, 3), A.add), D(tt, W("T2"), W("t2a"), ("mk", 2, 48, 3), A.add), D(cp, W("T2u"), W("T2"))],
+          [D(ts, W("wI"), W("yI"), 3855, A.bitwise_and), D(ts, W("I"), ("mF", 0, 128), W("pF"), A.is_equal)])
+    run("v", lambda e: e.tensor_tensor(ap(W("RK")), ap(W("Fw")).indirect(ap(W("T2u"))), ap(W("wI")), A.add), [W("Fw"), W("T2u"), W("wI")], [W("RK")])
+    cp(W("nbU"), W("nbT"))
+    for h in range(2): tt(("dk", 128 * h, 128 * h + 128), ("RK", 128 * h, 128 * h + 128), W("I"), A.mult)
+    for h in range(2):
+        rsum(("nK", h, h + 1), ("dk", 128 * h, 128 * h + 128), negate=True)
+        jk, b, o = ("jk", 256 * h, 256 * h + 256), ("nK", h, h + 1), ("sg", h, h + 1)
+        run("s", lambda e: e.activation(ap(jk), ap(W("RK")), AF.Sign, bias=ap(b), accum_out=ap(o)), [W("RK"), b], [jk, o])
+    ms(W("hE"), 0.0)
+    run("s", lambda e: e.activation(ap(("hE", 3, 515, 4)), ap(W("I")), AF.Copy, scale=0.5), [W("I")], [("hE", 3, 515, 4)])
+    gather(W("Rn"), W("io"), W("nbU"), "s")
+    ts(W("nbI"), W("nbT"), 255, A.bitwise_and)
+    quant(("X", 0, 256), W("xb"))
+    cp(W("nbL"), W("nbI"))
+    ts(("TS", 0, 64, 32), W("sg"), -0.5, A.mult, 127.5, A.add)
+    tp(W("TT"), W("TS"))
+    spread("Rp", "TT")
+    cp(("c0", 0, 16), ("mF", 0, 256, 16))
+    for i in range(2): ts(("c0", 16 + i, 32, 2), ("mF", 0, 256, 32), W("g16"), A.add)
+    weave([D(cp, W("kI"), W("c0"))] + kappa(W("kI"), W("kA"), W("kh"), W("k1"), W("kap")),
+          [D(quant, ("E", 128 * b, 128 * b + 128), ("hE", 3 - b, 515 - b)) for b in range(4)])
+    ts(W("aP"), W("pI"), 96, A.bitwise_and)
+    ts(W("lA"), ("kap", 16, 32), W("rho"), A.add)
+    ts(W("lM"), ("kap", 0, 16), W("rho"), A.add)
+    ts(W("lB"), ("c0", 16, 32), W("rF"), A.add)
+    tt(W("kP0"), W("pI"), W("aP"), A.add)
+    gather(W("dA"), W("Rp"), W("lA"))
+    ts(("mk0", 0, 1), W("kP0"), -256.0, A.add)
+    tp(W("tA"), W("dA"))
+    ts(("mk0", 1, 2), W("kP0"), -224.0, A.add)
+    cp(W("posU"), ("tA", 0, 256, 16))
+    ts(W("CLd"), ("kap", 16, 32), W("rF"), A.add)
+    run("v", lambda e: e.tensor_copy(ap(W("Rpi")).indirect(ap(W("posU"))), ap(W("iJ"))), [W("posU"), W("iJ")], [W("Rpi")])
+    def within(out, src, cm, base): run("g", lambda e: e.affine_select(ap(out), ap(src), [[0, 1]], A.is_ge, 0.0, base, cm), [src], [out])
+    settle()
+    within(("MS", 0, 1), ("mk0", 0, 1), -1, 47)
+    within(("MS", 2, 3), ("mk0", 1, 2), 1, -80)
+    within(("MS", 1, 2), ("mk0", 1, 2), 1, -32)
+    settle()
+    within(("MS", 1, 2), ("MS", 1, 2), -1, 79)
+    gather(W("Rpn"), W("Rp"), W("lM"), "s")
+    gather(W("Rq"), W("Rpn"), W("nbL"), "s")
+    tp(W("tI"), W("Rpi"))
+    gather(W("dB"), W("Rpi"), W("lB"), "s")
+    def where(k):
+        for i in range(2): ts(("lG", 16 * k + i, 16 * k + 16, 2), ("tI", 0, 256, 32), 3.0, A.mult, float(k), A.add)
+    def find(k): gather(("d2", 256 * k, 256 * k + 256), W("Rq"), ("lG", 16 * k, 16 * k + 16), "s")
+    def turn(k):
+        tp(("t2", 256 * k, 256 * k + 256), ("d2", 256 * k, 256 * k + 256))
+        cp(("nU", 16 * k, 16 * k + 16), ("t2", 256 * k, 256 * k + 256, 16))
+    where(0)
+    find(0)
+    where(1)
+    quant(("wq", 0, 128), W("wb"))
+    tp(W("tB"), W("dB"))
+    ts(("lQ", 48, 64), ("kap", 0, 16), W("rF"), A.add)
+    cp(W("piU"), ("tB", 0, 256, 16))
+    ts(W("Tn"), ("mF", 0, 256, 16), W("rF"), A.add)
+    pick(("W0", 0, 256), ("X", 0, 256), W("piU"))
+
+    def exchange(t):
+        for kind in "cs":
+            def what(d):
+                own, far = [("%s%d%s" % (n, t, kind),) + FAR[d] for n in "WM"]
+                return (octets(own), octets(far), own) if kind == "c" else (ap(own), ap(far), own)
+            send(what, "x%s%d" % (kind, t))
+            arrives("x%s%d" % (kind, t), incoming, [("M%d%s" % (t, kind), a, b) for a, b in FAR.values()])
+
+    def neighbours(t, k): pick(("N%d" % t, 256 * k, 256 * k + 256), ("W%d" % t, 0, 256), ("nU", 16 * k, 16 * k + 16))
+
+    def neighbours2(t, what="cs"): pick(("M%d" % t,) + LOC, ("W%d" % t, 0, 256), ("n2U", 0, 7), what)
+
+    def product(t, k, h, bank):
+        mov = ("N%d" % t, 256 * k + 128 * h, 256 * k + 128 * h + 128) if k < 2 else ("M%d" % t, 128 * h, 128 * h + 128)
+        mm(bank, 128, ("W%d" % t, 128 * h, 128 * h + 128), mov)
+
+    def mask(k, h, bank): tt(("dg", 132 * (2 * k + h), 132 * (2 * k + h) + 128), ("ps%d" % bank, 0, 128), W("I"), A.mult)
+
+    def total(k, h, q):
+        i = 2 * k + h
+        d, s, j = ("dg", 132 * i, 132 * i + 129), ("Sc", i, i + 1), ("dh", 132 * i, 132 * i + 129)
+        if q == "s": run("s", lambda e: e.activation(ap(j), ap(d), AF.Copy, accum_out=ap(s)), [d], [j, s])
+        else: rsum(s, d)
+
+    def halves(t, parts):
+        for b in parts: mm(BANKS[0][b], 256, ("E", 128 * b, 128 * b + 128), ("W%d" % t, 0, 256), True, b in VPARTS)
+
+    def keep():
+        for b in VPARTS: cp(("Ho", b, 1024, 4), ("ps%d" % BANKS[0][b], 0, 256), "s")
+
+    def unpack(t, k, b):
+        mov = ("N%d" % t, 256 * k, 256 * k + 256) if k < 2 else ("M%d" % t, 0, 256)
+        e, bank, alone = ("E", 128 * b, 128 * b + 128), BANKS[k][b], b in VPARTS
+        if k and not alone: mm(bank, 256, e, ("W%d" % t, 0, 256), True, False)
+        mm(bank, 256, e, mov, alone, True)
+        out, half = ("h%d" % k, b, 1024, 4), ("ps%d" % bank, 0, 256)
+        if alone: tt(out, half, ("Ho", b, 1024, 4), A.add)
+        else: cp(out, half, "s")
+
+    def candidate(t, k): quant(("W%d" % t, 256 * (k + 1), 256 * (k + 2)), W("h%d" % k))
+
+    def lists(t):
+        tp(W("RT"), ("RC%d" % t, 0, 256))
+        for h in range(2):
+            for s in range(2): cp(("LV", 8 * h + s, 8 * h + 8, 2), ("RT", 32 * h, 256, 64))
+
+    def shadow(t, items):
+        for i in items:
+            if i[0] == "u": unpack(t, i[1], i[2])
+            elif i[0] == "q": candidate(t, i[1])
+            else: lists(t)
+
+    def local(t, middle=()):
+        halves(t, (0, 1))
+        for k in range(2):
+            for h in range(2): product(t, k, h, 2 * k + h)
+        halves(t, (2, 3))
+        keep()
+        for h in range(2): mask(0, h, h)
+        if t:
+            cl = ("dg", 128, 792, 132)
+            tt(cl, cl, W("ckm"), A.add)
+            neighbours2(t, "c")
+        for h in range(2): total(0, h, "s")
+        mask(1, 0, 2)
+        total(1, 0, "s")
+        mask(1, 1, 3)
+        if t: neighbours2(t, "s")
+        total(1, 1, "v")
+        for f in middle: f()
+        m, fl = "m01_%d" % t, "fl%d" % t
+        tt(W(m), ("Sc", 0, 2), ("Sc", 2, 4), A.max)
+        def what(d):
+            r = (m, FAR[d][0] // 128, FAR[d][0] // 128 + 1)
+            return ap(r), ap((fl, d, d + 1)), r
+        send(what, "xm%d" % t)
+        arrives("xm%d" % t, incoming, [W(fl)])
+        tt(W("ge"), ("Sc", 0, 2), ("Sc", 2, 4), A.is_ge)
+
+    def prefer():
+        for h in range(2): plus(("c01", h, h + 1), ("ge", h, h + 1), ("NP", 2 + h, 3 + h), ("dN", h, h + 1))
+        for h in range(2): plus(("d2c", h, h + 1), ("c01", h, h + 1), ("NP", 4 + h, 5 + h), -1.0)
+
+    def choose(t):
+        fl, m = "fl%d" % t, "m01_%d" % t
+        if t:
+            prefer()
+            shadow(t, AHEAD)
+        for h in range(2): product(t, 2, h, h)
+        ready(t)
+        if t == 0:
+            for k in range(3): numbers(k)
+            prefer()
+        for h in range(2): mask(2, h, h)
+        for h in range(2): total(2, h, "v")
+        tt(W("gt"), ("Sc", 4, 6), W(m), A.is_gt)
+        tt(W("ga"), W("gt"), W("d2c"), A.mult)
+        ts(("Qf", 1, 3), ("MS", 1, 3), ("gt", 1, 2), A.mult)
+        ts(("Qf", 0, 1), ("MS", 0, 1), ("gt", 0, 1), A.mult)
+        tt(W("A2"), W("ga"), W("c01"), A.add)
+        for i, d, h in ((1, 3, 1), (2, 2, 1), (0, 1, 0)): ts(("Tf", i, i + 1), (fl, d, d + 1), ("Sc", 4 + h, 5 + h), A.is_lt, ("Qf", i, i + 1), A.mult)
+        ts(("TC", 32, 33), ("A2", 1, 2), ("Tf", 1, 2), A.add, ("Tf", 2, 3), A.add)
+        tt(("TC", 0, 1), ("A2", 0, 1), ("Tf", 0, 1), A.add)
+        tp(W("TD"), W("TC"))
+        spread("RC%d" % t, "TD")
+        shadow(t, BESIDE)
+
+    def ready(t):
+        for i, c in enumerate((0.0, 0.5, 512.0)): plus(("S0_%d" % t, i, 64, 4), ("mF", 0, 16), c, 0.0)
+        plus(("S1_%d" % t, 2, 64, 4), ("mF", 0, 16), 256.0, 0.0)
+        cp(("S1_%d" % t, 3, 64, 4), W("Tn"), "s")
+        plus(("RC%d" % t, 256, 272), ("mF", 0, 16), -1.0, 0.0)
+
+    def decide(t):
+        rc, d0, d1, ls = ["%s%d" % (n, t) for n in ("RC", "S0_", "S1_", "Ls")]
+        gather(W("RO"), (rc, 0, 256), W("CLd"), "s")
+        gather(W("RV"), (rc, 0, 272), W("LV"), "s")
+        shadow(t, AFTER)
+        if t < R - 1: bars()
+        else:
+            rows(1, "s")
+            store(1)
+        tp(W("ROt"), W("RO"))
+        v = ("ROt", 0, 256, 16)
+        tt((d1, 0, 64, 4), v, ("lQ", 16, 32), A.is_equal)
+        tt((d1, 1, 64, 4), v, ("lQ", 32, 48), A.is_equal)
+        tp(W("RVt"), W("RV"))
+        tt((d0, 3, 64, 4), ("RVt", 0, 256, 16), ("lQ", 48, 64), A.is_equal)
+        run("v", lambda e: e.tensor_tensor_scan(ap(W(ls)), ap(W(d0)), ap(W(d1)), 0.0, A.mult, A.add), [W(d0), W(d1)], [W(ls)])
+        cp(W("U%d" % t), (ls, 3, 64, 4))
+        if t < R - 1: tt(W("mB"), (d0, 3, 64, 4), ("Bm", 0, 16), A.mult)
+
+    def bars():
+        plus(("ckB", 4, 6), W("gt"), 0.0, -BIG)
+        plus(W("ngB"), W("gt"), -BIG, BIG)
+        for h in range(2): times(("ckB", h, h + 1), ("ge", h, h + 1), ("ngB", h, h + 1))
+        for h in range(2): plus(("ckB", 2 + h, 3 + h), ("ckB", h, h + 1), ("ngB", h, h + 1), -1.0)
+
+    def caps():
+        for h in range(2): times(("ckm", h, 6, 2), ("ckB", h, 6, 2), ("mP", h, h + 1))
+
+    def numbers(k): gather(("NR", 256 * k + 256, 256 * k + 512), W("Rn"), ("lN", 16 * k, 16 * k + 16), "s")
+
+    def rows(t, q):
+        gather(W("PRp%d" % t), W("NR"), W("U%d" % t), q)
+        gather(W("PRn%d" % t), W("PRp%d" % t), W("posU"), q)
+
+    def store(t):
+        need("y", [W("PRn%d" % t)], [])
+        g.sync.dma_start(T.pr[t:t + 1, :], ap(W("PRn%d" % t), (0, 1))).then_inc(T.sem.st, 16)
+
+    exchange(0)
+    find(1)
+    turn(0)
+    neighbours(0, 0)
+    turn(1)
+    neighbours(0, 1)
+    where(2)
+    find(2)
+    ts(("dg", 128, 792, 132), ("mF", 0, 6), 0.0, A.mult)
+    for k in range(3): ts(("lN", 16 * k, 16 * k + 16), ("tB", 0, 256, 16), 3.0, A.mult, float(k), A.add)
+    l0, l1 = LOC[0] // 16, LOC[1] // 16
+    local(0, [D(tp, ("t2", 512, 768), ("d2", 512, 768)), D(cp, ("lP", 0, 32), ("t2", 0, 512, 16)), D(cp, W("gG"), W("gI")), D(cp, ("n2U", 0, 7), ("t2", 512 + LOC[0], 512 + LOC[1], 16)),
+        D(cp, ("lP", 32 + l0, 32 + l1), ("t2", 512 + LOC[0], 512 + LOC[1], 16)), D(cp, ("lP", 32, 32 + l0), ("Tn", 0, l0)), D(cp, ("lP", 32 + l1, 48), ("Tn", l1, 16))])
+    ts(W("Bm"), W("c8"), W("gG"), A.is_equal)
+    weave(kappa(W("lP"), W("aI"), W("hP"), W("kP"), ("lQ", 0, 48)), [D(neighbours2, 0)] + [D(shadow, 0, (i,)) for i in AHEAD])
+    tt(W("EB"), ("lQ", 0, 48), W("Bm"), A.mult)
+    for i in range(6): rsum(("NP", i, i + 1), ("EB", 8 * i, 8 * i + 8))
+    tt(("NP", 4, 6), ("NP", 4, 6), ("MS", 0, 2), A.subtract)
+    tt(W("dN"), ("NP", 0, 2), ("NP", 2, 4), A.subtract)
+    tt(("NP", 5, 6), ("NP", 5, 6), ("MS", 2, 3), A.subtract)
+    choose(0)
+
+    for t in range(R):
+        decide(t)
+        if t == R - 1: break
+        u = t + 1
+        pick(("W%d" % u, 0, 256), ("W%d" % t, 0, 1024), W("U%d" % t))
+        exchange(u)
+        for h in range(2): rsum(("mP", h, h + 1), ("mB", 8 * h, 8 * h + 8))
+        neighbours(u, 0)
+        neighbours(u, 1)
+        caps()
+        local(u)
+        if u == R - 1:
+            rows(0, "s")
+            store(0)
+        choose(u)
+
+    t = R - 1
+    pick(("H", 0, 256), ("W%d" % t, 0, 1024), W("U%d" % t))
+    pick(("Z", 0, 256), ("H", 0, 256), W("posU"))
+    gather(W("PRp%d" % t), W("NR"), W("U%d" % t))
+    need("y", [("Zc", 0, 256)], [])
+    g.sync.dma_start(T.oc[:, :], octets(("Zc", 0, 256))).then_inc(T.sem.st, 16)
+    for h in range(2): mm(h, 128, ("wq", 0, 128), ("Z", 128 * h, 128 * h + 128))
+    need("y", [("Zs", 0, 256)], [])
+    for k in range(4): g.sync.dma_start(T.osc[4 * k:4 * k + 4, :], T.Zs[32 * k:32 * k + 4, 0:256]).then_inc(T.sem.st, 16)
+    for h in range(2):
+        half = ("yo", 128 * h, 128 * h + 128)
+        cp(half, ("ps%d" % h, 0, 128), "sv"[h])
+        need("sy"[h], [half], [])
+        queues["sy"[h]].dma_start(T.y[:, 128 * h:128 * h + 128], ap(half)).then_inc(T.sem.st, 16)
+    gather(W("PRn%d" % t), W("PRp%d" % t), W("posU"))
+    store(t)
+    g.sync.wait_ge(T.sem.st, 16 * (7 + R))
+    g.wait_ge(T.sem.ls, sent[0])
+    for q, sem in qsem.items():
+        if known["g"].get(sem, 0) < count[sem]: g.wait_ge(T.sem[sem], count[sem])

@@ -2,14 +2,16 @@ from concourse.bass import DstId, RemoteDMATransfer
 from concourse.mybir import dt, AluOpType as A, AxisListType, ActivationFunctionType as AF
 
 P, F, R = 256, 48, 3
-FAR = {1: (0, 48), 3: (160, 208), 2: (208, 256)}
-LOC = (48, 160)
+FAR = {1: (80, 128), 2: (128, 176), 3: (176, 224)}
+F0, F1 = 80, 224
 BIG = 1e29
-BANKS = ((4, 5, 6, 7), (4, 5, 6, 7), (2, 3, 0, 1))
-VPARTS = (0, 1)
-AHEAD = (("u", 0, 0), ("u", 0, 1), ("u", 0, 2), ("u", 0, 3))
-BESIDE = (("q", 0), ("u", 2, 0), ("u", 2, 1), ("u", 1, 0), ("u", 1, 1), ("u", 1, 2), ("u", 1, 3), ("q", 1), ("l",), ("u", 2, 2), ("u", 2, 3))
-AFTER = (("q", 2),)
+HUGE = 5e29
+OWN = 2048.0
+GAIN = (512.0, 768.0, 1024.0, 256.0)
+PACES = [dict(cyc=0.001, pe=0.0013, gat=1.5, sca=3.5, wake=0.06, issue=0.6, first=1.6, way=(1.4, 2.2), store=1.5),
+         dict(cyc=0.001, pe=0.0010, gat=1.2, sca=2.5, wake=0.06, issue=0.5, first=1.2, way=(1.0, 1.7), store=1.5),
+         dict(cyc=0.001, pe=0.0015, gat=1.9, sca=5.0, wake=0.1, issue=0.7, first=2.0, way=(2.0, 3.0), store=1.5)]
+PLAN = dict(load=(1.45, 1.6), seed=1, tries=300, moves=4, noise=2.0, lean=1.0)
 
 
 def _bufs():
@@ -19,31 +21,29 @@ def _bufs():
         sb(name + "c", n, "float8_e4m3fn_x4")
         sb(name + "s", n, "uint8")
     sb("nbT", 48, "int32"); sb("xb", 1024, "bfloat16"); sb("wb", 512, "bfloat16")
-    mx("X", 256); mx("wq", 128); mx("E", 512); mx("H", 256); mx("Z", 256)
+    mx("X", 256); mx("wq", 128); mx("E", 512); mx("H", 256); mx("Z", 256); mx("B", 256); mx("D", 272); mx("L", 144); mx("SQ", 128); mx("SR", 128)
     for t in range(R):
-        mx("W%d" % t, 1024); mx("N%d" % t, 512); mx("M%d" % t, 256)
-        sb("fl%d" % t, 4); sb("m01_%d" % t, 2); sb("RC%d" % t, 272, "bfloat16"); sb("U%d" % t, 16, "uint16")
-        for name in ("S0_", "S1_", "Ls"): sb("%s%d" % (name, t), 64)
-        sb("PRp%d" % t, 256); sb("PRn%d" % t, 256)
-    for k in range(3): sb("h%d" % k, 1024, "bfloat16")
-    sb("hE", 516, "bfloat16"); sb("Ho", 1024, "bfloat16")
-    for name, n in (("pI", 1), ("rI", 1), ("gI", 1), ("uI", 1), ("aP", 1), ("yI", 256), ("wI", 256), ("rhoI", 1), ("zI", 48),
-                    ("lP", 48), ("aI", 48), ("nbI", 48), ("kI", 32), ("kA", 32)): sb(name, n, "int32")
-    for name, n in (("pF", 1), ("I", 128), ("mF", 256), ("rF", 1), ("g16", 1), ("gG", 1), ("rho", 1), ("o48", 48), ("z48", 48), ("z3", 48), ("M48", 48),
-                    ("Fw", 1024), ("mk", 48), ("t2a", 16), ("T2", 16), ("RK", 256), ("dk", 256), ("nK", 2), ("sg", 2), ("jk", 512), ("Tn", 16), ("c0", 32),
-                    ("kh", 32), ("k1", 32), ("kap", 32), ("hP", 48), ("kP", 48), ("lQ", 64), ("kP0", 1), ("mk0", 2), ("MS", 3), ("NP", 6), ("dN", 2), ("Bm", 48), ("c8", 48),
-                    ("dg", 792), ("dh", 792), ("Sc", 6), ("ge", 2), ("c01", 2), ("d2c", 2), ("gt", 2), ("ga", 2), ("A2", 2), ("Qf", 3), ("Tf", 3), ("ckB", 6), ("ngB", 2), ("mB", 16), ("mP", 2), ("ckm", 6),
-                    ("EB", 48), ("io", 1032), ("Rn", 768), ("NR", 1024), ("yo", 256)): sb(name, n)
-    for name, n in (("TS", 64), ("TT", 64), ("Rp", 256), ("dA", 256), ("tA", 256), ("iJ", 256), ("Rpi", 256), ("tI", 256), ("dB", 256), ("tB", 256), ("Rpn", 256), ("Rq", 768), ("d2", 768), ("t2", 768),
-                    ("TC", 64), ("TD", 64), ("RO", 256), ("ROt", 256), ("RT", 256), ("RV", 256), ("RVt", 256)): sb(name, n, "bfloat16")
-    for name, n in (("T2u", 16), ("lA", 16), ("lB", 16), ("lM", 16), ("posU", 16), ("piU", 16), ("nbL", 48), ("nbU", 48), ("lG", 48), ("lN", 48), ("nU", 32), ("n2U", 8), ("LV", 16), ("CLd", 16)): sb(name, n, "uint16")
+        mx("W%d" % t, 768); mx("M%d" % t, 144)
+        sb("fl%d" % t, 4); sb("m01_%d" % t, 2); sb("U%d" % t, 16, "uint16")
+    for name, n in (("hn", 1024), ("hf", 576), ("Ho", 1024), ("Hp", 1024), ("hE", 516), ("hB", 1024), ("hM", 576), ("hL", 512), ("hP", 512), ("hQ", 512)): sb(name, n, "bfloat16")
+    for name, n in (("pI", 1), ("rI", 1), ("gI", 1), ("uI", 1), ("aI", 1), ("bI", 1), ("yI", 256), ("wI", 256), ("rhoI", 1), ("rh", 1), ("zI", 48),
+                    ("nbG", 16), ("nbH", 12), ("posI", 2), ("rgI", 4), ("npI", 6), ("nsI", 12)): sb(name, n, "int32")
+    for name, n in (("pF", 1), ("I", 128), ("mF", 256), ("rF", 1), ("gF", 1), ("o48", 48), ("z48", 48), ("z3", 48), ("M48", 48), ("Fw", 1024), ("mk", 48), ("t2a", 16), ("T2", 16),
+                    ("RK", 256), ("KG", 32), ("KT", 32), ("sg", 2), ("jk", 512), ("rg", 4), ("ns", 12), ("nh", 6), ("dn", 4), ("c1", 1), ("c2", 1), ("c3", 1), ("c4", 1), ("c5", 1), ("c6", 1),
+                    ("c8", 1), ("c9", 1), ("r1", 1), ("rB", 1), ("rT", 1), ("vr", 16), ("HB", 16), ("gt", 16), ("gt0", 16), ("NE", 24), ("EQ", 24), ("MK", 192), ("D48", 48), ("T16", 16),
+                    ("tg", 16), ("tq", 2), ("one", 8), ("nil", 1), ("top", 1), ("loc", 2), ("wc", 2), ("m1", 8), ("m3", 8), ("m4", 8), ("m2", 1), ("b0", 1), ("b1", 1), ("i17", 17), ("wR", 64),
+                    ("K96", 96), ("KF", 96), ("S96", 96), ("nm", 96), ("np", 96), ("MV", 64), ("G", 512), ("gm", 96), ("gs", 96), ("SL", 600), ("jr", 256), ("S2", 2), ("GL", 4), ("th", 4),
+                    ("e2", 2), ("n2", 2), ("sel", 4), ("cl", 12), ("CF", 16), ("ls", 48), ("lu", 16), ("NR", 1280), ("PRp", 256), ("PRn", 256), ("yo", 256), ("FX", 1), ("FL", 16)): sb(name, n)
+    for name, n in (("CR", 256), ("GN", 192), ("VT", 256), ("VR", 256), ("mr", 256), ("idF", 64), ("iJ", 256), ("Rp", 256), ("d3", 256), ("t3", 256)): sb(name, n, "bfloat16")
+    for name, n in (("T2u", 16), ("lKG", 2), ("lNG", 1), ("nbO", 12), ("lVR", 16), ("idT", 64), ("lG", 1), ("gI0", 16), ("gU0", 6), ("gU", 6), ("lC", 1), ("lB", 16), ("posU", 16),
+                    ("lst", 16), ("UA", 16), ("off", 16)): sb(name, n, "uint16")
     for i in range(8): b["ps%d" % i] = ("psum", [128, 512], "float32")
     return b
 
 
 def _pack(b):
     out, place, fill = {}, {}, {"float32": 0, "int32": 0, "uint16": 0, "bfloat16": 0}
-    fixed = ("nbT", "xb", "wb", "hE", "pF", "mF", "I", "Ho", "h0", "h1", "h2", "fl0", "fl1", "fl2", "m01_0", "m01_1", "m01_2")
+    fixed = ("nbT", "xb", "wb", "hn", "hf", "Ho", "Hp", "hE", "hB", "hM", "hL", "hP", "hQ", "fl0", "fl1", "fl2", "m01_0", "m01_1", "m01_2", "FX", "FL", "off", "yo")
     for name, (where, shape, d) in b.items():
         place[name] = (name, 0)
         if where != "sbuf" or d not in fill or name in fixed: out[name] = (where, shape, d)
@@ -56,7 +56,8 @@ def _pack(b):
 
 SCRATCH, PLACE = _pack(_bufs())
 WIDTH = {k: v[1][1] for k, v in _bufs().items()}
-SEMAPHORES = ["qv", "qs", "qt", "qg", "ldn", "ldx", "ldw", "ls", "st"] + ["x%s%d" % (k, t) for k in "csm" for t in range(R)]
+KIND = {k: v[2] for k, v in _bufs().items()}
+SEMAPHORES = ["qv", "qs", "qt", "qg", "ldn", "ldx", "ldb", "ldw", "ls", "st"] + ["x%s%d" % (k, t) for k in "csm" for t in range(R)]
 
 
 def shares(T, topo, core):
@@ -71,52 +72,90 @@ def shares(T, topo, core):
     return peer, eng
 
 
+def norm(r): return (r[0], r[1], r[2], r[3] if len(r) > 3 else 1)
+def size(r): return len(range(*norm(r)[1:]))
+def bank(r): return r[0][:2] == "ps"
+
+
+def clash(x, y):
+    if x[2] <= y[1] or y[2] <= x[1]: return False
+    return x[3] == y[3] == 1 or not set(range(*x[1:])).isdisjoint(range(*y[1:]))
+
+
+def arrange(calls, loaded):
+    n = len(calls)
+    before, seen = [dict() for _ in calls], {}
+    for i, c in enumerate(calls):
+        for r, w in [(norm(r), False) for r in c["rd"]] + [(norm(r), True) for r in c["wr"]]:
+            for j, s, v in seen.get(r[0], ()):
+                if j == i: continue
+                if (w or v) and clash(r, s): before[i][j] = not (c["acc"] and v and bank(r)) or before[i].get(j, False)
+                elif bank(r): before[i].setdefault(j, False)
+            seen.setdefault(r[0], []).append((i, r, w))
+    after = [[] for _ in calls]
+    for i in range(n):
+        for j in before[i]: after[j].append(i)
+    wake, chain = PACES[0]["wake"], [0.0] * n
+    for i in reversed(range(n)): chain[i] = min(w[1][0] for w in calls[i]["ways"]) + calls[i]["lat"][0] + max([wake + chain[k] for k in after[i]] + [0.0])
+    early = [max([loaded.get(r[0], 0.0) for r in c["rd"]] + [0.0]) for c in calls]
+    state = [PLAN["seed"]]
+
+    def draw():
+        state[0] = (state[0] * 1103515245 + 12345) % 2147483648
+        return state[0] / 2147483648
+
+    def lay(shift, lean):
+        left, ready, busy, at = [len(b) for b in before], [i for i in range(n) if not before[i]], {"s": [(0.0, 0.25)], "y": [(0.0, 0.4)]}, [None] * n
+        while ready:
+            i = max(ready, key=lambda k: chain[k] + shift[k])
+            ready.remove(i)
+            pick = None
+            for w in calls[i]["ways"]:
+                t = max([early[i]] + [at[j][1] + calls[j]["lat"][0] + (wake if hard or at[j][2][0] != w[0] else 0.0) for j, hard in before[i].items()])
+                for a, b in busy.setdefault(w[0], []):
+                    if t + w[1][0] <= a: break
+                    t = max(t, b)
+                e = t + w[1][0] + (lean[i] if w[0] == "v" else 0.0)
+                if pick is None or e < pick[3]: pick = (t, t + w[1][0], w, e)
+            at[i] = pick
+            busy[pick[2][0]].append(pick[:2])
+            busy[pick[2][0]].sort()
+            for k in after[i]:
+                left[k] -= 1
+                if not left[k]: ready.append(k)
+        order = sorted(range(n), key=lambda i: (at[i][0], i))
+        ends = []
+        for s, pace in enumerate(PACES):
+            free, end = {"s": 0.25, "y": 0.4}, [0.0] * n
+            for i in order:
+                q = at[i][2][0]
+                t = max([early[i], free.get(q, 0.0)] + [end[j] + (pace["wake"] if hard or at[j][2][0] != q else 0.0) for j, hard in before[i].items()])
+                free[q] = t + at[i][2][1][s]
+                end[i] = free[q] + calls[i]["lat"][s]
+            ends.append(max(end))
+        return sum(ends), [(calls[i], at[i][2]) for i in order]
+
+    shift, lean = [0.0] * n, [PLAN["lean"]] * n
+    best = lay(shift, lean)
+    for trial in range(PLAN["tries"]):
+        s, l = list(shift), list(lean)
+        for _ in range(PLAN["moves"]):
+            i = int(draw() * n)
+            if len(calls[i]["ways"]) > 1 and draw() < 0.5: l[i] = (draw() - 0.3) * 2.0
+            else: s[i] = (draw() - 0.5) * PLAN["noise"]
+        now = lay(s, l)
+        if now[0] <= best[0]: best, shift, lean = now, s, l
+    return best[1]
+
+
 def rank_program(g, core, T, topo):
     rank = T.rank_of(core)
     if rank is None: return
-    queues = {"v": g.vector, "s": g.scalar, "t": g.tensor, "g": g, "y": g.sync}
-    qsem = {"v": "qv", "s": "qs", "t": "qt", "g": "qg"}
-    count = {k: 0 for k in qsem.values()}
-    known = {q: {} for q in queues}
-    writes, reads = {}, {}
+    calls = []
 
-    def norm(r): return (r[0], r[1], r[2], r[3] if len(r) > 3 else 1)
-
-    def clash(x, y):
-        if x[2] <= y[1] or y[2] <= x[1]: return False
-        if x[3] == y[3]: return x[3] == 1 or (x[1] - y[1]) % x[3] == 0
-        if x[3] > 1 and y[3] > 1: return True
-        (s, a, b), (c, e) = ((x[3], x[1], x[2]), y[1:3]) if x[3] > 1 else ((y[3], y[1], y[2]), x[1:3])
-        return a + max(0, -((a - c) // s)) * s < min(b, e)
-
-    def need(q, rd, wr, acc=False):
-        evs = []
-        for r in map(norm, rd): evs += [e for w, e in writes.get(r[0], []) if clash(w, r)]
-        for r in map(norm, wr):
-            evs += [e for w, e in writes.get(r[0], []) if clash(w, r) and not (acc and e[3] == "t")]
-            evs += [e for w, e in reads.get(r[0], []) if clash(w, r)]
-        evs.sort(key=lambda e: -e[1])
-        for sem, val, snap, _q in evs:
-            if known[q].get(sem, 0) >= val: continue
-            queues[q].wait_ge(T.sem[sem], val)
-            known[q][sem] = val
-            for k, v in snap.items(): known[q][k] = max(known[q].get(k, 0), v)
-
-    def note(ev, rd, wr):
-        for r in rd: reads.setdefault(r[0], []).append((norm(r), ev))
-        for r in map(norm, wr):
-            inside = lambda w: w[1] >= r[1] and w[2] <= r[2] and r[3] == 1
-            writes[r[0]] = [(w, e) for w, e in writes.get(r[0], []) if not inside(w)] + [(r, ev)]
-            reads[r[0]] = [(w, e) for w, e in reads.get(r[0], []) if not inside(w)]
-
-    def run(q, fn, rd, wr, acc=False):
-        need(q, rd, wr, acc)
-        sem = qsem[q]
-        count[sem] += 1
-        fn(queues[q]).then_inc(T.sem[sem], 1)
-        note((sem, count[sem], dict(known[q]), q), rd, wr)
-
-    def arrives(sem, val, wr): note((sem, val, {}, "d"), [], wr)
+    def each(f): return tuple(f(p) for p in PACES)
+    def cycles(n): return each(lambda p: n * p["cyc"])
+    def put(ways, rd, wr, acc=False, lat=None, kind="c", parts=None): calls.append(dict(ways=ways, rd=rd, wr=wr, acc=acc, lat=lat or cycles(0), kind=kind, parts=parts))
 
     def ap(r, p=None):
         name, a, b, st = norm(r)
@@ -127,368 +166,359 @@ def rank_program(g, core, T, topo):
     def words(r): return ap(r).bitcast(dt.uint32)
     def octets(r): return ap(r).bitcast(dt.uint8)
     def W(n): return (n, 0, WIDTH[n])
+    def C(n, i): return (n, i, i + 1)
     def sc(s): return ap(s) if isinstance(s, tuple) else s
-    def tt(out, in0, in1, op): run("v", lambda e: e.tensor_tensor(ap(out), ap(in0), ap(in1), op), [in0, in1], [out])
+    def cols(*x): return [s for s in x if isinstance(s, tuple)]
+    def real(*x): return all(KIND[r[0]] in ("float32", "bfloat16") for r in x)
+    def plain(n, k=1.0, more=0): return cycles(max(64, n * k) + more)
+    def narrow(*x): return 0.5 if all(KIND[r[0]] in ("bfloat16", "uint16") for r in x) else 1.0
+    def picked(n, q="v"): return each(lambda p: ((60 if q == "v" else 78) + n * p["gat"]) * p["cyc"])
+    def tt(out, in0, in1, op, off=None):
+        if off is None: put([("v", plain(size(out), 1 if bank(in0) else 2), lambda e: e.tensor_tensor(ap(out), ap(in0), ap(in1), op))], [in0, in1], [out])
+        else: put([("v", picked(size(out)), lambda e: e.tensor_tensor(ap(out), ap(in0).indirect(ap(off)), ap(in1), op))], [in0, off, in1], [out])
     def ts(out, in0, s1, op0, s2=None, op1=None):
-        rd = [in0] + [s for s in (s1, s2) if isinstance(s, tuple)]
-        if op1 is None: run("v", lambda e: e.tensor_scalar(ap(out), ap(in0), sc(s1), None, op0), rd, [out])
-        else: run("v", lambda e: e.tensor_scalar(ap(out), ap(in0), sc(s1), sc(s2), op0, op1), rd, [out])
-    def cp(out, in_, q="v"):
-        if q == "v": run("v", lambda e: e.tensor_copy(ap(out), ap(in_)), [in_], [out])
-        else: run("s", lambda e: e.activation(ap(out), ap(in_), AF.Copy), [in_], [out])
+        t = plain(size(out), narrow(out, in0))
+        if op1 is None: put([("v", t, lambda e: e.tensor_scalar(ap(out), ap(in0), sc(s1), None, op0))], [in0] + cols(s1), [out])
+        else: put([("v", t, lambda e: e.tensor_scalar(ap(out), ap(in0), sc(s1), sc(s2), op0, op1))], [in0] + cols(s1, s2), [out])
+    def cp(out, in_, p=None):
+        ways = [("v", plain(size(out), narrow(out, in_)), lambda e: e.tensor_copy(ap(out, p), ap(in_, p)))]
+        if real(out, in_): ways.append(("s", plain(size(out)), lambda e: e.activation(ap(out, p), ap(in_, p), AF.Copy)))
+        put(ways, [in_], [out])
     def plus(out, in_, bias, scale=1.0):
-        rd = [in_] + [x for x in (bias, scale) if isinstance(x, tuple)]
-        run("s", lambda e: e.activation(ap(out), ap(in_), AF.Identity, bias=sc(bias), scale=sc(scale)), rd, [out])
-    def times(out, in_, col): run("s", lambda e: e.activation(ap(out), ap(in_), AF.Copy, scale=ap(col)), [in_, col], [out])
-    def ms(out, c): run("v", lambda e: e.memset(ap(out), c), [], [out])
-    def rsum(out, in_, negate=False): run("v", lambda e: e.tensor_reduce(ap(out), ap(in_), AxisListType.X, A.add, negate=negate), [in_], [out])
-    def tp(out, in_): run("v", lambda e: e.transpose(ap(out), ap(in_)), [in_], [out])
-    def gather(out, win, off, q="v"):
-        if q == "v": run("v", lambda e: e.tensor_copy(ap(out), ap(win).indirect(ap(off))), [win, off], [out])
-        else: run("s", lambda e: e.activation(ap(out), ap(win).indirect(ap(off)), AF.Copy), [win, off], [out])
-    def pick(out, win, off, what="cs"):
+        ways = [("v", plain(size(out), narrow(out, in_)), lambda e: e.tensor_scalar(ap(out), ap(in_), sc(scale), sc(bias), A.mult, A.add))]
+        if real(out, in_): ways.append(("s", plain(size(out)), lambda e: e.activation(ap(out), ap(in_), AF.Identity, bias=sc(bias), scale=sc(scale))))
+        put(ways, [in_] + cols(bias, scale), [out])
+    def count(out, pattern, base, cm):
+        if KIND[out[0]] == "int32": return lambda e: e.iota(ap(out), pattern, base, cm)
+        return lambda e: e.iota(ap(out), pattern, base, cm, allow_small_or_imprecise_dtypes=True)
+    def iota(out, pattern, base, cm): put([("g", cycles(157 + 2 * size(out)), count(out, pattern, base, cm))], [], [out], kind="iota")
+    def ms(out, c): put([("v", plain(size(out), narrow(out)), lambda e: e.memset(ap(out), c)), ("g", cycles(157 + 2 * size(out)), count(out, [[0, size(out)]], int(c), 0))], [], [out], kind="iota")
+    def within(out, src, cm, base, fill):
+        put([("g", cycles(205 + 2 * size(out)), lambda e: e.affine_select(ap(out), ap(src), [[0, size(out)]], A.is_ge, fill, base, cm))], [src], [out], kind="select")
+    def rsum(out, in_, junk):
+        put([("v", plain(size(in_)), lambda e: e.tensor_reduce(ap(out), ap(in_), AxisListType.X, A.add)),
+             ("s", plain(size(in_), 1, 24), lambda e: e.activation(ap(junk), ap(in_), AF.Copy, accum_out=ap(out)))], [in_], [out, junk])
+    def tp(out, in_): put([("v", plain(size(out), narrow(out, in_)), lambda e: e.transpose(ap(out), ap(in_)))], [in_], [out])
+    def scan(out, d0, d1, op0, op1): put([("v", plain(size(out)), lambda e: e.tensor_tensor_scan(ap(out), ap(d0), ap(d1), 0.0, op0, op1))], [d0, d1], [out])
+    def gather(out, win, off, bias=None):
+        if bias is None: ways = [("v", picked(size(out)), lambda e: e.tensor_copy(ap(out), ap(win).indirect(ap(off)))), ("s", picked(size(out), "s"), lambda e: e.activation(ap(out), ap(win).indirect(ap(off)), AF.Copy))]
+        else: ways = [("v", picked(size(out)), lambda e: e.tensor_scalar(ap(out), ap(win).indirect(ap(off)), bias, None, A.add)),
+                      ("s", picked(size(out), "s"), lambda e: e.activation(ap(out), ap(win).indirect(ap(off)), AF.Identity, bias=bias))]
+        put(ways if real(out, win) else ways[:1], [win, off], [out])
+    def pick(out, win, off):
         oc, wc, os_, ws = [(r[0] + x, r[1], r[2]) for x in "cs" for r in (out, win)]
-        if "c" in what: run("v", lambda e: e.tensor_copy(words(oc), words(wc).indirect(ap(off))), [wc, off], [oc])
-        if "s" in what: run("s", lambda e: e.activation(ap(os_), ap(ws).indirect(ap(off)), AF.Copy), [ws, off], [os_])
+        put([("v", picked(size(oc)), lambda e: e.tensor_copy(words(oc), words(wc).indirect(ap(off))))], [wc, off], [oc])
+        put([("s", picked(size(oc), "s"), lambda e: e.activation(ap(os_), ap(ws).indirect(ap(off)), AF.Copy))], [ws, off], [os_])
     def quant(out, in_):
         c, s = (out[0] + "c", out[1], out[2]), (out[0] + "s", out[1], out[2])
-        run("v", lambda e: e.quantize_mx(ap(c), ap(s), ap(in_)), [in_], [c, s])
-    def mm(bank, n, w, x, start=True, stop=True):
+        put([("v", cycles(15 + 0.265 * size(in_)), lambda e: e.quantize_mx(ap(c), ap(s), ap(in_)))], [in_], [c, s])
+    def mm(b, w, x, start=True, stop=True):
+        n = x[2] - x[1]
         wc, ws, xc, xs = (w[0] + "c", w[1], w[2]), (w[0] + "s", w[1], w[2]), (x[0] + "c", x[1], x[2]), (x[0] + "s", x[1], x[2])
-        run("t", lambda e: e.matmul_mx(ap(("ps%d" % bank, 0, n)), ap(wc), ap(ws), ap(xc), ap(xs), start, stop), [wc, ws, xc, xs], [("ps%d" % bank, 0, 512)], acc=not start)
-    def iota(out, pattern, base, cm):
-        if PLACE[out[0]][0] == "pool_int32": run("g", lambda e: e.iota(ap(out), pattern, base, cm), [], [out])
-        else: run("g", lambda e: e.iota(ap(out), pattern, base, cm, allow_small_or_imprecise_dtypes=True), [], [out])
-    def settle():
-        if known["g"].get("qg", 0) < count["qg"]: g.wait_ge(T.sem.qg, count["qg"])
-        known["g"]["qg"] = count["qg"]
-    def pb(out, in_, p): run("g", lambda e: e.partition_broadcast(ap(out), ap(in_, (p, p + 1)), 128), [in_], [out])
-    def spread(row, col):
-        settle()
-        for a in range(4): pb((row, 64 * a, 64 * a + 64), (col, 0, 64), 32 * a)
-    def D(f, *a): return lambda: f(*a)
-    def weave(*chains):
-        for i in range(max(map(len, chains))):
-            for c in chains:
-                if i < len(c): c[i]()
+        put([("t", each(lambda p: (n + 16) * p["pe"]), lambda e: e.matmul_mx(ap(("ps%d" % b, 0, n)), ap(wc), ap(ws), ap(xc), ap(xs), start, stop))], [wc, ws, xc, xs], [("ps%d" % b, 0, 512)], acc=not start)
+    stores = [0]
+    def store(q, out, in_, view):
+        stores[0] += 16
+        put([(q, cycles(50), lambda e: e.dma_start(out, view))], [in_], [], lat=each(lambda p: p["store"]), kind="store")
 
     peer, eng = shares(T, topo, core)
     incoming = sum(len(shares(T, topo, c)[1][d]) for d, c in peer.items())
     sent = [0]
 
-    def send(what, sem):
-        tr = []
-        for d in eng:
-            src, dst, region = what(d)
-            need("g", [region], [])
-            rid, pid, _s = topo.addr(peer[d])
-            tr.append(RemoteDMATransfer(dst_ids=[DstId(rid=rid, pnc=pid)], dma_engine_mask=sum(1 << e for e in eng[d]), remote_sem=T.sem[sem], src=src, dst=dst))
-            sent[0] += len(eng[d])
-        g.remote_dma_fused(tr, local_sem=T.sem.ls)
-
-    for i in range(8):
-        q = g.sync if i % 2 == 0 else g.scalar
-        q.dma_start(T.nbT[16 * i:16 * i + 16, :], T.nb[:, :]).then_inc(T.sem.ldn, 16)
-    arrives("ldn", 128, [W("nbT")])
-    g.sync.dma_start(T.xb[:, :], T.x[:, :]).then_inc(T.sem.ldx, 16)
-    arrives("ldx", 16, [W("xb")])
-    g.sync.dma_start(T.wb[:, :], T.w[:, :]).then_inc(T.sem.ldw, 16)
-    arrives("ldw", 16, [W("wb")])
+    def send(way, *parts):
+        made = []
+        for what, sem, lands in parts:
+            tr, rd = [], []
+            for d in eng:
+                src, dst, region = what(d)
+                rid, pid, _s = topo.addr(peer[d])
+                tr.append(RemoteDMATransfer(dst_ids=[DstId(rid=rid, pnc=pid)], dma_engine_mask=sum(1 << e for e in eng[d]), remote_sem=T.sem[sem], src=src, dst=dst))
+                rd.append(region)
+            made.append((tr, rd, sem, lands))
+        put([("g", each(lambda p: p["issue"] * len(parts) + (0.0 if sent[0] else p["first"])), None)], [r for m in made for r in m[1]], [m[3] for m in made],
+            lat=each(lambda p: p["way"][way]), kind="send", parts=made)
+        sent[0] += len(parts) * sum(len(e) for e in eng.values())
 
     iota(W("pI"), [[0, 1]], 0, 1)
-    iota(W("o48"), [[0, 16], [1, 3]], 0, 0)
-    iota(W("pF"), [[0, 1]], 0, 1)
     iota(W("mF"), [[1, 256]], 0, 0)
+    iota(W("o48"), [[0, 16], [1, 3]], 0, 0)
     iota(W("yI"), [[256, 16], [11, 16]], 10, 0)
-    iota(W("c8"), [[0, 6], [1, 8]], 0, 0)
-    for q in (3, 0, 1, 2):
-        c, r = q ^ rank ^ 1, ("Fw", 256 * q, 256 * q + 256)
-        if q == 3: ms(r, 1048576.0 * c)
-        elif q < rank: plus(r, W("mF"), 1048576.0 * c, 4096.0)
-        else: plus(r, W("mF"), 1048576.0 * c, 0.0)
-    cp(W("iJ"), W("mF"), "s")
-    for q in range(4): plus(("io", 256 * q, 256 * q + 256), W("mF"), 256.0 * q)
-    plus(("io", 1024, 1032), ("mF", 0, 8), 1024.0)
-    plus(("NR", 0, 256), W("mF"), -1.0, 0.0)
-
-    def kappa(v, ai, h, s, out):
-        return [D(ts, h, v, 128.0, A.is_ge, 96.0, A.mult), D(ts, ai, v, 96, A.bitwise_and), D(tt, s, v, ai, A.add), D(tt, out, s, h, A.subtract)]
-
+    iota(W("vr"), [[16, 2], [64, 4], [0, 2]], 0, 0)
+    iota(W("CR"), [[0, 8], [1, 16], [0, 2]], 0, 0)
+    iota(W("HB"), [[0, 8], [256, 2]], 0, 0)
+    iota(W("i17"), [[1, 17]], -1, 0)
+    iota(W("tg"), [[128, 16]], int(GAIN[0]), 1)
+    iota(W("tq"), [[128, 2]], 0, 1)
+    ms(W("one"), 1.0)
+    ms(W("nil"), 0.0)
+    ms(W("top"), GAIN[2])
+    within(C("loc", 0), C("one", 0), -1, F0 - 1, 0.0)
+    within(C("loc", 1), C("one", 0), 1, 128 - F1, 0.0)
+    within(C("wc", 0), W("top"), -1, F0 - 1, GAIN[3])
+    within(C("wc", 1), W("top"), 1, 128 - F1, GAIN[3])
+    within(W("m1"), W("one"), 1, -FAR[1][0], 0.0)
+    within(W("m4"), W("one"), 1, 128 - FAR[3][0], 0.0)
+    within(W("m2"), C("one", 0), -1, FAR[2][1] - 129, 0.0)
+    within(W("b0"), W("nil"), 1, -F0, -HUGE)
+    within(W("b1"), W("nil"), -1, F1 - 129, -HUGE)
+    within(W("m3"), W("m4"), -1, FAR[3][1] - 129, 0.0)
     ts(W("rI"), W("pI"), 15, A.bitwise_and)
     ts(W("gI"), W("pI"), 4, A.logical_shift_right)
+    ts(W("aI"), W("pI"), 96, A.bitwise_and)
+    ts(W("bI"), W("pI"), 1, A.bitwise_and)
+    ts(W("uI"), W("pI"), 4, A.logical_shift_right, 1, A.bitwise_and)
     cp(W("rF"), W("rI"))
-    ts(W("uI"), W("gI"), 1, A.bitwise_and)
-    weave([D(ts, W("z48"), W("o48"), W("rF"), A.add, 1.0, A.add), D(ts, W("zI"), W("z48"), 1.0 / 3.0, A.mult), D(ts, W("z3"), W("zI"), 3.0, A.mult), D(tt, W("M48"), W("z3"), W("z48"), A.is_equal)],
-          [D(ts, W("rhoI"), W("rF"), 3.0, A.mult, 2.0, A.add), D(ts, W("rhoI"), W("rhoI"), 15, A.bitwise_and), D(cp, W("rho"), W("rhoI"))],
-          [D(ts, W("g16"), W("uI"), 16.0, A.mult), D(ms, W("TS"), 0.0), D(ms, W("TC"), 0.0)])
-
-    weave([D(tt, W("mk"), W("nbT"), W("M48"), A.mult), D(tt, W("t2a"), ("mk", 0, 48, 3), ("mk", 1, 48, 3), A.add), D(tt, W("T2"), W("t2a"), ("mk", 2, 48, 3), A.add), D(cp, W("T2u"), W("T2"))],
-          [D(ts, W("wI"), W("yI"), 3855, A.bitwise_and), D(ts, W("I"), ("mF", 0, 128), W("pF"), A.is_equal)])
-    run("v", lambda e: e.tensor_tensor(ap(W("RK")), ap(W("Fw")).indirect(ap(W("T2u"))), ap(W("wI")), A.add), [W("Fw"), W("T2u"), W("wI")], [W("RK")])
-    cp(W("nbU"), W("nbT"))
-    for h in range(2): tt(("dk", 128 * h, 128 * h + 128), ("RK", 128 * h, 128 * h + 128), W("I"), A.mult)
-    for h in range(2):
-        rsum(("nK", h, h + 1), ("dk", 128 * h, 128 * h + 128), negate=True)
-        jk, b, o = ("jk", 256 * h, 256 * h + 256), ("nK", h, h + 1), ("sg", h, h + 1)
-        run("s", lambda e: e.activation(ap(jk), ap(W("RK")), AF.Sign, bias=ap(b), accum_out=ap(o)), [W("RK"), b], [jk, o])
+    cp(W("gF"), W("gI"))
+    cp(W("pF"), W("pI"))
+    plus(W("r1"), W("rF"), 1.0)
+    plus(W("rB"), W("rF"), -OWN)
+    plus(W("rT"), W("rF"), GAIN[0])
+    plus(W("c6"), W("rF"), W("gF"), 8.0)
+    cp(W("iJ"), W("mF"))
+    ts(W("I"), ("mF", 0, 128), W("pF"), A.is_equal)
     ms(W("hE"), 0.0)
-    run("s", lambda e: e.activation(ap(("hE", 3, 515, 4)), ap(W("I")), AF.Copy, scale=0.5), [W("I")], [("hE", 3, 515, 4)])
-    gather(W("Rn"), W("io"), W("nbU"), "s")
-    ts(W("nbI"), W("nbT"), 255, A.bitwise_and)
-    quant(("X", 0, 256), W("xb"))
-    cp(W("nbL"), W("nbI"))
-    ts(("TS", 0, 64, 32), W("sg"), -0.5, A.mult, 127.5, A.add)
-    tp(W("TT"), W("TS"))
-    spread("Rp", "TT")
-    cp(("c0", 0, 16), ("mF", 0, 256, 16))
-    for i in range(2): ts(("c0", 16 + i, 32, 2), ("mF", 0, 256, 32), W("g16"), A.add)
-    weave([D(cp, W("kI"), W("c0"))] + kappa(W("kI"), W("kA"), W("kh"), W("k1"), W("kap")),
-          [D(quant, ("E", 128 * b, 128 * b + 128), ("hE", 3 - b, 515 - b)) for b in range(4)])
-    ts(W("aP"), W("pI"), 96, A.bitwise_and)
-    ts(W("lA"), ("kap", 16, 32), W("rho"), A.add)
-    ts(W("lM"), ("kap", 0, 16), W("rho"), A.add)
-    ts(W("lB"), ("c0", 16, 32), W("rF"), A.add)
-    tt(W("kP0"), W("pI"), W("aP"), A.add)
-    gather(W("dA"), W("Rp"), W("lA"))
-    ts(("mk0", 0, 1), W("kP0"), -256.0, A.add)
-    tp(W("tA"), W("dA"))
-    ts(("mk0", 1, 2), W("kP0"), -224.0, A.add)
-    cp(W("posU"), ("tA", 0, 256, 16))
-    ts(W("CLd"), ("kap", 16, 32), W("rF"), A.add)
-    run("v", lambda e: e.tensor_copy(ap(W("Rpi")).indirect(ap(W("posU"))), ap(W("iJ"))), [W("posU"), W("iJ")], [W("Rpi")])
-    def within(out, src, cm, base): run("g", lambda e: e.affine_select(ap(out), ap(src), [[0, 1]], A.is_ge, 0.0, base, cm), [src], [out])
-    settle()
-    within(("MS", 0, 1), ("mk0", 0, 1), -1, 47)
-    within(("MS", 2, 3), ("mk0", 1, 2), 1, -80)
-    within(("MS", 1, 2), ("mk0", 1, 2), 1, -32)
-    settle()
-    within(("MS", 1, 2), ("MS", 1, 2), -1, 79)
-    gather(W("Rpn"), W("Rp"), W("lM"), "s")
-    gather(W("Rq"), W("Rpn"), W("nbL"), "s")
-    tp(W("tI"), W("Rpi"))
-    gather(W("dB"), W("Rpi"), W("lB"), "s")
-    def where(k):
-        for i in range(2): ts(("lG", 16 * k + i, 16 * k + 16, 2), ("tI", 0, 256, 32), 3.0, A.mult, float(k), A.add)
-    def find(k): gather(("d2", 256 * k, 256 * k + 256), W("Rq"), ("lG", 16 * k, 16 * k + 16), "s")
-    def turn(k):
-        tp(("t2", 256 * k, 256 * k + 256), ("d2", 256 * k, 256 * k + 256))
-        cp(("nU", 16 * k, 16 * k + 16), ("t2", 256 * k, 256 * k + 256, 16))
-    where(0)
-    find(0)
-    where(1)
-    quant(("wq", 0, 128), W("wb"))
-    tp(W("tB"), W("dB"))
-    ts(("lQ", 48, 64), ("kap", 0, 16), W("rF"), A.add)
-    cp(W("piU"), ("tB", 0, 256, 16))
-    ts(W("Tn"), ("mF", 0, 256, 16), W("rF"), A.add)
-    pick(("W0", 0, 256), ("X", 0, 256), W("piU"))
-
-    def exchange(t):
-        for kind in "cs":
-            def what(d):
-                own, far = [("%s%d%s" % (n, t, kind),) + FAR[d] for n in "WM"]
-                return (octets(own), octets(far), own) if kind == "c" else (ap(own), ap(far), own)
-            send(what, "x%s%d" % (kind, t))
-            arrives("x%s%d" % (kind, t), incoming, [("M%d%s" % (t, kind), a, b) for a, b in FAR.values()])
-
-    def neighbours(t, k): pick(("N%d" % t, 256 * k, 256 * k + 256), ("W%d" % t, 0, 256), ("nU", 16 * k, 16 * k + 16))
-
-    def neighbours2(t, what="cs"): pick(("M%d" % t,) + LOC, ("W%d" % t, 0, 256), ("n2U", 0, 7), what)
-
-    def product(t, k, h, bank):
-        mov = ("N%d" % t, 256 * k + 128 * h, 256 * k + 128 * h + 128) if k < 2 else ("M%d" % t, 128 * h, 128 * h + 128)
-        mm(bank, 128, ("W%d" % t, 128 * h, 128 * h + 128), mov)
-
-    def mask(k, h, bank): tt(("dg", 132 * (2 * k + h), 132 * (2 * k + h) + 128), ("ps%d" % bank, 0, 128), W("I"), A.mult)
-
-    def total(k, h, q):
-        i = 2 * k + h
-        d, s, j = ("dg", 132 * i, 132 * i + 129), ("Sc", i, i + 1), ("dh", 132 * i, 132 * i + 129)
-        if q == "s": run("s", lambda e: e.activation(ap(j), ap(d), AF.Copy, accum_out=ap(s)), [d], [j, s])
-        else: rsum(s, d)
-
-    def halves(t, parts):
-        for b in parts: mm(BANKS[0][b], 256, ("E", 128 * b, 128 * b + 128), ("W%d" % t, 0, 256), True, b in VPARTS)
-
-    def keep():
-        for b in VPARTS: cp(("Ho", b, 1024, 4), ("ps%d" % BANKS[0][b], 0, 256), "s")
-
-    def unpack(t, k, b):
-        mov = ("N%d" % t, 256 * k, 256 * k + 256) if k < 2 else ("M%d" % t, 0, 256)
-        e, bank, alone = ("E", 128 * b, 128 * b + 128), BANKS[k][b], b in VPARTS
-        if k and not alone: mm(bank, 256, e, ("W%d" % t, 0, 256), True, False)
-        mm(bank, 256, e, mov, alone, True)
-        out, half = ("h%d" % k, b, 1024, 4), ("ps%d" % bank, 0, 256)
-        if alone: tt(out, half, ("Ho", b, 1024, 4), A.add)
-        else: cp(out, half, "s")
-
-    def candidate(t, k): quant(("W%d" % t, 256 * (k + 1), 256 * (k + 2)), W("h%d" % k))
-
-    def lists(t):
-        tp(W("RT"), ("RC%d" % t, 0, 256))
+    plus(("hE", 3, 515, 4), W("I"), 0.0, 0.5)
+    def Eb(b): return ("E", 128 * b, 128 * b + 128)
+    for b in range(4): quant(Eb(b), ("hE", 3 - b, 515 - b))
+    for i in range(2): ts(("hP", i, 512, 2), W("CR"), W("rF"), A.is_equal, OWN, A.mult)
+    quant(("D", 144, 272), W("hP"))
+    ms(W("hL"), 0.0)
+    quant(("L", 16, 144), W("hL"))
+    ms(W("hM"), 0.0)
+    ts(W("NE"), ("mF", 0, 24), -8.0, A.add, W("gF"), A.not_equal)
+    plus(W("EQ"), W("NE"), 1.0 / OWN, -1.0 / OWN)
+    for k in range(3):
         for h in range(2):
-            for s in range(2): cp(("LV", 8 * h + s, 8 * h + 8, 2), ("RT", 32 * h, 256, 64))
+            a = 32 * (2 * k + h) + (16 if k == 2 else 0)
+            plus(("MK", a, a + 16), ("NE", 8 - 8 * h, 24 - 8 * h), 0.0, HUGE if k == 2 else -HUGE)
+    ts(W("KF"), ("CR", 0, 192, 2), W("rF"), A.is_equal)
+    cp(("K96", 0, 64), ("KF", 0, 64))
+    for h in range(2): plus(("K96", 64 + 16 * h, 80 + 16 * h), ("KF", 0, 16), 0.0, C("loc", h))
+    ts(W("S96"), ("CR", 0, 192, 2), 0.0, A.not_equal)
+    ms(("cl", 0, 6), 0.0)
+    ms(W("D48"), 0.0)
+    plus(("D48", 2, 48, 3), ("mF", 0, 256, 16), W("rB"))
+    plus(W("T16"), ("mF", 0, 256, 16), W("rT"))
+    plus(W("c9"), W("gF"), 2.0, 3.0)
+    ts(W("lC"), W("bI"), 24.0, A.mult, W("c9"), A.add)
+    tt(("tg", 4, 6), W("tq"), W("wc"), A.add)
+    ts(W("lG"), W("c6"), 16.0, A.add, 63.0, A.min)
+    ts(W("c8"), W("uI"), 16.0, A.mult, W("rF"), A.add)
+    for i in range(2): ts(("lB", i, 16, 2), ("mF", 0, 256, 32), W("c8"), A.add)
+    quant(("X", 0, 256), W("xb"))
+    quant(("wq", 0, 128), W("wb"))
 
-    def shadow(t, items):
-        for i in items:
-            if i[0] == "u": unpack(t, i[1], i[2])
-            elif i[0] == "q": candidate(t, i[1])
-            else: lists(t)
+    for q in range(4): plus(("Fw", 256 * q, 256 * q + 256), W("mF"), 1048576.0 * (q ^ rank), 4096.0 if q < rank else 0.0)
+    ts(W("z48"), W("o48"), W("rF"), A.add, 1.0, A.add)
+    ts(W("zI"), W("z48"), 1.0 / 3.0, A.mult)
+    ts(W("z3"), W("zI"), 3.0, A.mult)
+    tt(W("M48"), W("z3"), W("z48"), A.is_equal)
+    ts(W("wI"), W("yI"), 3855, A.bitwise_and)
+    tt(W("mk"), W("nbT"), W("M48"), A.mult)
+    tt(W("t2a"), ("mk", 0, 48, 3), ("mk", 1, 48, 3), A.add)
+    tt(W("T2"), W("t2a"), ("mk", 2, 48, 3), A.add)
+    cp(W("T2u"), W("T2"))
+    tt(W("RK"), W("Fw"), W("wI"), A.add, W("T2u"))
+    ts(W("rh"), W("rF"), 3.0, A.mult, 2.0, A.add)
+    ts(W("rhoI"), W("rh"), 15, A.bitwise_and)
+    plus(W("c2"), W("gF"), 0.0, 32.0)
+    ts(W("c1"), W("rhoI"), W("c2"), A.add)
+    ts(W("lKG"), ("mF", 0, 32, 16), W("c1"), A.add)
+    gather(W("KG"), W("RK"), W("lKG"))
+    tp(W("KT"), W("KG"))
+    for u in range(2):
+        def sign(jk, b, o): put([("s", plain(256, 1, 24), lambda e: e.activation(ap(jk), ap(W("RK")), AF.Sign, bias=ap(b), scale=-1.0, accum_out=ap(o)))], [W("RK"), b], [jk, o])
+        sign(("jk", 256 * u, 256 * u + 256), C("KT", 16 * u), C("sg", u))
+    ts(W("posI"), W("sg"), 0.5, A.mult, 127.5 + F1, A.add)
+    ts(("rgI", 0, 2), W("posI"), 15, A.bitwise_and)
+    ts(("rgI", 2, 4), W("posI"), 4, A.logical_shift_right, 15, A.bitwise_and)
+    cp(W("rg"), W("rgI"))
+    plus(W("c3"), W("gF"), W("rF"), 6.0)
+    ts(W("lNG"), W("c3"), 47.0, A.min)
+    gather(W("nbG"), W("nbT"), W("lNG"))
+    ts(("nbH", 0, 6), ("nbG", 0, 6), 240, A.bitwise_and)
+    ts(("nbH", 6, 12), ("nbG", 0, 6), 15, A.bitwise_and)
+    cp(W("nbO"), W("nbH"))
+    gather(W("GN"), W("mF"), W("nbO"))
+    ms(("VT", 0, 64), 0.0)
+    ts(W("c4"), W("aI"), W("pF"), A.add, W("rF"), A.subtract)
+    plus(("VT", 0, 32, 16), ("mF", 0, 64, 32), W("c4"))
+    plus(("VT", 32, 64, 16), ("mF", 0, 2), W("rF"), 0.0)
+    for k in range(3): tp(("VT", 64 * k + 64, 64 * k + 128), ("GN", k, 192, 3))
+    ts(W("c5"), W("bI"), 32.0, A.mult)
+    ts(W("lVR"), W("vr"), W("c5"), A.add)
+    gather(W("VR"), W("VT"), W("lVR"))
+    for u in range(2): ts(("mr", 128 * u, 128 * u + 128), ("CR", 0, 128), C("rg", 2 + u), A.is_equal)
+    for u in range(2): ts(("hB", u, 512, 2), W("CR"), C("rg", u), A.is_equal)
+    for u in range(2): tt(("hB", 512 + u, 768, 2), ("mr", 128 * u, 128 * u + 128), ("VR", 128 * u, 128 * u + 128), A.mult)
+    quant(("B", 0, 128), ("hB", 0, 512))
+    quant(("B", 128, 256), ("hB", 512, 1024))
+    mm(2, ("B", 0, 128), ("B", 128, 256))
+    cp(W("idT"), ("ps2", 0, 64))
+    cp(W("idF"), ("ps2", 0, 64))
+    cp(("idF", 48 + F0 // 16, 48 + F1 // 16), ("ps2", F0 // 16, F1 // 16))
+    pick(("W0", 0, 256), ("X", 0, 256), ("idT", 0, 16))
+    tt(W("gt0"), W("idF"), W("HB"), A.add, W("lG"))
+    cp(W("gU0"), ("gt0", 0, 6))
 
-    def local(t, middle=()):
-        halves(t, (0, 1))
-        for k in range(2):
-            for h in range(2): product(t, k, h, 2 * k + h)
-        halves(t, (2, 3))
-        keep()
-        for h in range(2): mask(0, h, h)
-        if t:
-            cl = ("dg", 128, 792, 132)
-            tt(cl, cl, W("ckm"), A.add)
-            neighbours2(t, "c")
-        for h in range(2): total(0, h, "s")
-        mask(1, 0, 2)
-        total(1, 0, "s")
-        mask(1, 1, 3)
-        if t: neighbours2(t, "s")
-        total(1, 1, "v")
-        for f in middle: f()
-        m, fl = "m01_%d" % t, "fl%d" % t
-        tt(W(m), ("Sc", 0, 2), ("Sc", 2, 4), A.max)
-        def what(d):
-            r = (m, FAR[d][0] // 128, FAR[d][0] // 128 + 1)
-            return ap(r), ap((fl, d, d + 1)), r
-        send(what, "xm%d" % t)
-        arrives("xm%d" % t, incoming, [W(fl)])
-        tt(W("ge"), ("Sc", 0, 2), ("Sc", 2, 4), A.is_ge)
+    put([("v", each(lambda p: (60 + 256 * p["sca"]) * p["cyc"]), lambda e: e.tensor_copy(ap(W("Rp")).indirect(ap(("idT", 0, 16))), ap(W("iJ"))))], [("idT", 0, 16), W("iJ")], [W("Rp")])
+    gather(W("gI0"), W("idF"), W("lG"))
+    tt(W("nm"), W("Rp"), W("KF"), A.mult, ("gI0", 0, 6))
+    scan(W("np"), W("S96"), W("nm"), A.mult, A.add)
+    cp(W("npI"), ("np", 15, 96, 16))
+    tt(("gt", 0, 6), ("np", 15, 96, 16), ("HB", 0, 6), A.add)
+    cp(W("gU"), ("gt", 0, 6))
+    ts(("nsI", 0, 6), W("npI"), 15, A.bitwise_and)
+    ts(("nsI", 6, 12), W("npI"), 4, A.logical_shift_right)
+    cp(W("ns"), W("nsI"))
+    plus(W("nh"), ("ns", 6, 12), 0.0, 16.0)
+    for i in range(2): tt(("dn", 2 * i, 2 * i + 2), (("ns", "nh")[i], 0, 2), (("ns", "nh")[i], 2, 4), A.subtract)
+    for i in range(4): plus(("MV", 32 * (i % 2) + i // 2, 32 * (i % 2) + 32, 2), ("EQ", 8 - 8 * (i % 2), 24 - 8 * (i % 2)), 0.0, C(("nh", "ns")[i // 2], 4 + i % 2))
+    for i in range(4): ts(("hQ", i, 512, 4), ("CR", 0, 256, 2), C("ns", i), A.is_equal, GAIN[i // 2], A.mult)
+    quant(("SQ", 0, 128), W("hQ"))
+    for i in range(6):
+        a = 32 * i + (0 if i >= 4 else 16)
+        ts(("MK", a, a + 16), ("mF", 0, 16), C("ns", 6 + i), A.not_equal, HUGE if i >= 4 else -HUGE, A.mult)
+    for h in range(2): ts(("wR", 32 * h, 32 * h + 17), W("i17"), C("ns", 4 + h), A.is_equal, C("wc", h), A.mult)
+    gather(W("d3"), W("Rp"), W("lB"))
+    tp(W("t3"), W("d3"))
+    cp(W("posU"), ("t3", 0, 256, 16))
+    for i in range(2): plus(("NR", 256 * i, 256 * i + 256), W("mF"), -1.0, 0.0)
+    for k in range(3): gather(("NR", 512 + 256 * k, 768 + 256 * k), W("mF"), ("idT", 16 + 16 * k, 32 + 16 * k), 256.0 * rank)
+    for d, (a, b) in FAR.items(): plus(("NR", 256 + a, 256 + b), ("NR", 1024 + a, 1024 + b), 256.0 * ((rank ^ d) - rank))
 
-    def prefer():
-        for h in range(2): plus(("c01", h, h + 1), ("ge", h, h + 1), ("NP", 2 + h, 3 + h), ("dN", h, h + 1))
-        for h in range(2): plus(("d2c", h, h + 1), ("c01", h, h + 1), ("NP", 4 + h, 5 + h), -1.0)
-
-    def choose(t):
-        fl, m = "fl%d" % t, "m01_%d" % t
-        if t:
-            prefer()
-            shadow(t, AHEAD)
-        for h in range(2): product(t, 2, h, h)
-        ready(t)
-        if t == 0:
-            for k in range(3): numbers(k)
-            prefer()
-        for h in range(2): mask(2, h, h)
-        for h in range(2): total(2, h, "v")
-        tt(W("gt"), ("Sc", 4, 6), W(m), A.is_gt)
-        tt(W("ga"), W("gt"), W("d2c"), A.mult)
-        ts(("Qf", 1, 3), ("MS", 1, 3), ("gt", 1, 2), A.mult)
-        ts(("Qf", 0, 1), ("MS", 0, 1), ("gt", 0, 1), A.mult)
-        tt(W("A2"), W("ga"), W("c01"), A.add)
-        for i, d, h in ((1, 3, 1), (2, 2, 1), (0, 1, 0)): ts(("Tf", i, i + 1), (fl, d, d + 1), ("Sc", 4 + h, 5 + h), A.is_lt, ("Qf", i, i + 1), A.mult)
-        ts(("TC", 32, 33), ("A2", 1, 2), ("Tf", 1, 2), A.add, ("Tf", 2, 3), A.add)
-        tt(("TC", 0, 1), ("A2", 0, 1), ("Tf", 0, 1), A.add)
-        tp(W("TD"), W("TC"))
-        spread("RC%d" % t, "TD")
-        shadow(t, BESIDE)
-
-    def ready(t):
-        for i, c in enumerate((0.0, 0.5, 512.0)): plus(("S0_%d" % t, i, 64, 4), ("mF", 0, 16), c, 0.0)
-        plus(("S1_%d" % t, 2, 64, 4), ("mF", 0, 16), 256.0, 0.0)
-        cp(("S1_%d" % t, 3, 64, 4), W("Tn"), "s")
-        plus(("RC%d" % t, 256, 272), ("mF", 0, 16), -1.0, 0.0)
-
-    def decide(t):
-        rc, d0, d1, ls = ["%s%d" % (n, t) for n in ("RC", "S0_", "S1_", "Ls")]
-        gather(W("RO"), (rc, 0, 256), W("CLd"), "s")
-        gather(W("RV"), (rc, 0, 272), W("LV"), "s")
-        shadow(t, AFTER)
-        if t < R - 1: bars()
-        else:
-            rows(1, "s")
-            store(1)
-        tp(W("ROt"), W("RO"))
-        v = ("ROt", 0, 256, 16)
-        tt((d1, 0, 64, 4), v, ("lQ", 16, 32), A.is_equal)
-        tt((d1, 1, 64, 4), v, ("lQ", 32, 48), A.is_equal)
-        tp(W("RVt"), W("RV"))
-        tt((d0, 3, 64, 4), ("RVt", 0, 256, 16), ("lQ", 48, 64), A.is_equal)
-        run("v", lambda e: e.tensor_tensor_scan(ap(W(ls)), ap(W(d0)), ap(W(d1)), 0.0, A.mult, A.add), [W(d0), W(d1)], [W(ls)])
-        cp(W("U%d" % t), (ls, 3, 64, 4))
-        if t < R - 1: tt(W("mB"), (d0, 3, 64, 4), ("Bm", 0, 16), A.mult)
-
-    def bars():
-        plus(("ckB", 4, 6), W("gt"), 0.0, -BIG)
-        plus(W("ngB"), W("gt"), -BIG, BIG)
-        for h in range(2): times(("ckB", h, h + 1), ("ge", h, h + 1), ("ngB", h, h + 1))
-        for h in range(2): plus(("ckB", 2 + h, 3 + h), ("ckB", h, h + 1), ("ngB", h, h + 1), -1.0)
-
-    def caps():
-        for h in range(2): times(("ckm", h, 6, 2), ("ckB", h, 6, 2), ("mP", h, h + 1))
-
-    def numbers(k): gather(("NR", 256 * k + 256, 256 * k + 512), W("Rn"), ("lN", 16 * k, 16 * k + 16), "s")
-
-    def rows(t, q):
-        gather(W("PRp%d" % t), W("NR"), W("U%d" % t), q)
-        gather(W("PRn%d" % t), W("PRp%d" % t), W("posU"), q)
-
-    def store(t):
-        need("y", [W("PRn%d" % t)], [])
-        g.sync.dma_start(T.pr[t:t + 1, :], ap(W("PRn%d" % t), (0, 1))).then_inc(T.sem.st, 16)
-
-    exchange(0)
-    find(1)
-    turn(0)
-    neighbours(0, 0)
-    turn(1)
-    neighbours(0, 1)
-    where(2)
-    find(2)
-    ts(("dg", 128, 792, 132), ("mF", 0, 6), 0.0, A.mult)
-    for k in range(3): ts(("lN", 16 * k, 16 * k + 16), ("tB", 0, 256, 16), 3.0, A.mult, float(k), A.add)
-    l0, l1 = LOC[0] // 16, LOC[1] // 16
-    local(0, [D(tp, ("t2", 512, 768), ("d2", 512, 768)), D(cp, ("lP", 0, 32), ("t2", 0, 512, 16)), D(cp, W("gG"), W("gI")), D(cp, ("n2U", 0, 7), ("t2", 512 + LOC[0], 512 + LOC[1], 16)),
-        D(cp, ("lP", 32 + l0, 32 + l1), ("t2", 512 + LOC[0], 512 + LOC[1], 16)), D(cp, ("lP", 32, 32 + l0), ("Tn", 0, l0)), D(cp, ("lP", 32 + l1, 48), ("Tn", l1, 16))])
-    ts(W("Bm"), W("c8"), W("gG"), A.is_equal)
-    weave(kappa(W("lP"), W("aI"), W("hP"), W("kP"), ("lQ", 0, 48)), [D(neighbours2, 0)] + [D(shadow, 0, (i,)) for i in AHEAD])
-    tt(W("EB"), ("lQ", 0, 48), W("Bm"), A.mult)
-    for i in range(6): rsum(("NP", i, i + 1), ("EB", 8 * i, 8 * i + 8))
-    tt(("NP", 4, 6), ("NP", 4, 6), ("MS", 0, 2), A.subtract)
-    tt(W("dN"), ("NP", 0, 2), ("NP", 2, 4), A.subtract)
-    tt(("NP", 5, 6), ("NP", 5, 6), ("MS", 2, 3), A.subtract)
-    choose(0)
+    def S(i): return C("SL", 100 * i + 99)
+    def SS(k): return ("SL", 200 * k + 99, 200 * k + 200, 100)
 
     for t in range(R):
-        decide(t)
-        if t == R - 1: break
-        u = t + 1
-        pick(("W%d" % u, 0, 256), ("W%d" % t, 0, 1024), W("U%d" % t))
-        exchange(u)
-        for h in range(2): rsum(("mP", h, h + 1), ("mB", 8 * h, 8 * h + 8))
-        neighbours(u, 0)
-        neighbours(u, 1)
-        caps()
-        local(u)
-        if u == R - 1:
-            rows(0, "s")
-            store(0)
-        choose(u)
+        w, far, m, fl = "W%d" % t, "M%d" % t, "m01_%d" % t, "fl%d" % t
+        def columns(kind, view):
+            def what(d):
+                own, there = (w + kind,) + FAR[d], (far + kind, FAR[d][0] - F0, FAR[d][1] - F0)
+                return view(own), view(there), own
+            return what, "x%s%d" % (kind, t), W(far + kind)
+        send(1, columns("c", octets), columns("s", ap))
+        for h in range(2): mm(h, (w, 128 * h, 128 * h + 128), (w, 0, 256) if t else ("X", 0, 256))
+        for h in range(2): cp(("G", 256 * h, 256 * h + 256), ("ps%d" % h, 0, 256))
+        tt(W("gm"), W("G"), W("K96"), A.mult, W("gU" if t else "gU0"))
+        scan(W("gs"), W("S96"), W("gm"), A.mult, A.add)
+        tt(("SL", 99, 600, 100), ("gs", 15, 96, 16), ("cl", 0, 6), A.add)
+        tt(W(m), SS(0), SS(1), A.max)
+        send(0, (lambda d: (ap(C(m, FAR[d][0] // 128)), ap(C(fl, d)), C(m, FAR[d][0] // 128)), "xm%d" % t, W(fl)))
+        tt(("GL", 0, 2), SS(0), SS(1), A.is_lt)
+        tt(("GL", 2, 4), SS(0), SS(1), A.is_ge)
+        for h in range(2): ts(C("e2", h), S(4 + h), C(m, h), A.is_gt, C("loc", h), A.mult)
+        plus(W("n2"), W("e2"), 1.0, -1.0)
+        for i in range(4): plus(C("sel", i), C("GL", 2 + i % 2), C(("ns", "nh")[i // 2], 2 + i % 2), C("dn", i))
+        for i in range(4): plus(C("th", i), C("GL", i), S(i), -HUGE)
+        for h in range(2): plus(("hL", 64 + h, 128, 2), ("MV", 32 * h, 32 * h + 32), 0.0, C("e2", h))
+        for i in range(4):
+            h, lo = i % 2, 1 - i // 2
+            ts(("hL", h + 2 * lo, 64, 4), ("EQ", 8 - 8 * h, 24 - 8 * h), C("sel", i), A.mult, C("n2", h), A.mult)
+        quant(("L", 0, 128), W("hL"))
+        mm(2, ("D", 144, 272), ("L", 0, 128), True, False)
+        mm(2, ("D", 144, 272), ("L", 16, 144), False, True)
+        cp(W("lst"), ("ps2", 0, 16))
+        for b in range(4): mm(4 + b, Eb(b), (w, 0, 256))
+        for b in range(4):
+            half, again = ("Ho", 256 * b, 256 * b + 256), ("Hp", 256 * b, 256 * b + 256)
+            cp(half, ("ps%d" % (4 + b), 0, 256))
+            cp(again, half)
+            tt(("hn", b, 1024, 4), half, again, A.add, W("lst"))
+        quant((w, 512, 768), W("hn"))
+        for b in range(4): mm(4 + b, Eb(b), (w, F0, F1), True, False)
+        for h in range(2): mm(h, (w, 128 * h, 128 * h + 128), (far, 16 * h, 16 * h + 128))
+        for b in range(4): mm(4 + b, Eb(b), (far, 0, 144), False, True)
+        for b in range(4): cp(("hf", b, 576, 4), ("ps%d" % (4 + b), 0, 144))
+        quant((w, 256 + F0, 256 + F1), W("hf"))
+        tt(("SL", 451, 499), ("ps0", 0, 48), ("I", F0, 128), A.mult)
+        tt(("SL", 503, 599), ("ps1", 32, 128), ("I", 0, 96), A.mult)
+        rsum(C("S2", 0), ("SL", 451, 500), ("jr", 0, 49))
+        rsum(C("S2", 1), ("SL", 503, 600), ("jr", 128, 225))
+        for h in range(2):
+            for k in range(3):
+                a, mk = (192 + h, 198 + h, 8 + h)[k], ("MK", 32 * (2 * k + h), 32 * (2 * k + h) + 32)
+                if k < 2: ts(("hM", a, a + 373, 12), mk, C("th", 2 * k + h), A.add, C("S2", h), A.is_ge)
+                else: ts(("hM", a, a + 373, 12), mk, C(m, h), A.add, C("S2", h), A.is_lt)
+        quant(("D", 0, 144), W("hM"))
+        mm(3, ("D", 144, 272), ("D", 48, 176), True, False)
+        mm(3, ("SQ", 0, 128), ("D", 96, 224), False, False)
+        plus(W("FX"), W("m2"), W("b1"), C(fl, 2))
+        plus(("FL", 0, 8), W("m1"), W("b0"), C(fl, 1))
+        plus(("FL", 8, 16), W("m3"), W("FX"), C(fl, 3))
+        for h in range(2): ts(("off", 8 * h, 8 * h + 8), ("FL", 8 * h, 8 * h + 8), C("S2", h), A.is_lt, W("r1"), A.mult)
+        for h in range(2): gather(("hB", h, 512, 4), ("wR", 32 * h, 32 * h + 17), ("off", 8 * h, 8 * h + 8))
+        quant(("SR", 0, 128), ("hB", 0, 512))
+        mm(3, ("SR", 0, 128), ("D", 0, 128), False, True)
+        scan(W("ls"), ("ps3", 0, 48), W("D48"), A.max, A.add)
+        tt(W("lu"), ("ls", 2, 48, 3), W("T16"), A.min)
+        cp(W("U%d" % t), W("lu"))
+        pick(("W%d" % (t + 1) if t < R - 1 else "H", 0, 256), (w, 0, 768), W("U%d" % t))
+        cp(W("UA"), ("ls", 2, 48, 3), ((0, 32), (32, 64), (64, 128))[t])
+        if t < R - 1:
+            tt(W("CF"), W("ls"), W("tg"), A.is_equal, W("lC"))
+            plus(("cl", 6 * t, 6 * t + 6), ("CF", 0, 6), 0.0, -BIG)
+        if t == 1: tt(("cl", 0, 6), ("cl", 0, 6), ("cl", 6, 12), A.add)
 
-    t = R - 1
-    pick(("H", 0, 256), ("W%d" % t, 0, 1024), W("U%d" % t))
     pick(("Z", 0, 256), ("H", 0, 256), W("posU"))
-    gather(W("PRp%d" % t), W("NR"), W("U%d" % t))
-    need("y", [("Zc", 0, 256)], [])
-    g.sync.dma_start(T.oc[:, :], octets(("Zc", 0, 256))).then_inc(T.sem.st, 16)
-    for h in range(2): mm(h, 128, ("wq", 0, 128), ("Z", 128 * h, 128 * h + 128))
-    need("y", [("Zs", 0, 256)], [])
-    for k in range(4): g.sync.dma_start(T.osc[4 * k:4 * k + 4, :], T.Zs[32 * k:32 * k + 4, 0:256]).then_inc(T.sem.st, 16)
+    store("y", T.oc[:, :], ("Zc", 0, 256), octets(("Zc", 0, 256)))
+    for k in range(4): store("y", T.osc[4 * k:4 * k + 4, :], ("Zs", 0, 256), T.Zs[32 * k:32 * k + 4, 0:256])
     for h in range(2):
         half = ("yo", 128 * h, 128 * h + 128)
-        cp(half, ("ps%d" % h, 0, 128), "sv"[h])
-        need("sy"[h], [half], [])
-        queues["sy"[h]].dma_start(T.y[:, 128 * h:128 * h + 128], ap(half)).then_inc(T.sem.st, 16)
-    gather(W("PRn%d" % t), W("PRp%d" % t), W("posU"))
-    store(t)
-    g.sync.wait_ge(T.sem.st, 16 * (7 + R))
+        mm(h, ("wq", 0, 128), ("Z", 128 * h, 128 * h + 128))
+        cp(half, ("ps%d" % h, 0, 128))
+        store("sy"[h], T.y[:, 128 * h:128 * h + 128], half, ap(half))
+    gather(W("PRp"), W("NR"), W("UA"))
+    gather(W("PRn"), W("PRp"), W("posU"))
+    for i in range(R): store("y", T.pr[i:i + 1, :], W("PRn"), ap(W("PRn"), (32 * i, 32 * i + 1)))
+
+    queues = {"v": g.vector, "s": g.scalar, "t": g.tensor, "g": g, "y": g.sync}
+    done = {q: 0 for q in "vstg"}
+    known = {q: {} for q in queues}
+    writes, reads, last = {}, {}, [None]
+
+    def wait(q, evs):
+        for sem, val, snap, _q in sorted(evs, key=lambda e: -e[1]):
+            if known[q].get(sem, 0) >= val: continue
+            queues[q].wait_ge(T.sem[sem], val)
+            known[q][sem] = val
+            for k, v in snap.items(): known[q][k] = max(known[q].get(k, 0), v)
+
+    def made(rd): return [e for r in map(norm, rd) for w, e in writes.get(r[0], []) if clash(w, r)]
+
+    def note(ev, rd, wr):
+        for r in rd: reads.setdefault(r[0], []).append((norm(r), ev))
+        for r in map(norm, wr):
+            inside = lambda w: w == r or w[1] >= r[1] and w[2] <= r[2] and r[3] == 1
+            writes[r[0]] = [(w, e) for w, e in writes.get(r[0], []) if not inside(w)] + [(r, ev)]
+            reads[r[0]] = [(w, e) for w, e in reads.get(r[0], []) if not inside(w)]
+
+    for i in range(8): queues["ys"[i % 2]].dma_start(T.nbT[16 * i:16 * i + 16, :], T.nb[:, :]).then_inc(T.sem.ldn, 16)
+    note(("ldn", 128, {}, "d"), [], [W("nbT")])
+    for sem, region, src in (("ldx", W("xb"), T.x[:, :]), ("ldb", ("hB", 768, 1024), T.x[:, 0:256]), ("ldw", W("wb"), T.w[:, :])):
+        g.sync.dma_start(ap(region), src).then_inc(T.sem[sem], 16)
+        note((sem, 16, {}, "d"), [], [region])
+
+    for c, (q, _t, call) in arrange(calls, {"nbT": PLAN["load"][0], "xb": PLAN["load"][1], "wb": PLAN["load"][1]}):
+        if c["kind"] == "send":
+            for tr, rd, sem, lands in c["parts"]:
+                wait("g", made(rd))
+                g.remote_dma_fused(tr, local_sem=T.sem.ls)
+                note((sem, incoming, {}, "d"), [], [lands])
+            continue
+        evs = made(c["rd"]) + [e for r in c["rd"] if bank(r) for w, e in reads.get(r[0], []) if e[3] != q]
+        for r in map(norm, c["wr"]):
+            evs += [e for w, e in writes.get(r[0], []) if clash(w, r) and not (c["acc"] and e[3] == "t")]
+            evs += [e for w, e in reads.get(r[0], []) if clash(w, r)]
+        if q == "g":
+            if last[0] not in (None, c["kind"]): evs.append(("qg", done["g"], {}, "g"))
+            last[0] = c["kind"]
+        wait(q, evs)
+        if c["kind"] == "store": call(queues[q]).then_inc(T.sem.st, 16)
+        else:
+            done[q] += 1
+            call(queues[q]).then_inc(T.sem["q" + q], 1)
+            note(("q" + q, done[q], dict(known[q]), q), c["rd"], c["wr"])
+    g.sync.wait_ge(T.sem.st, stores[0])
     g.wait_ge(T.sem.ls, sent[0])
-    for q, sem in qsem.items():
-        if known["g"].get(sem, 0) < count[sem]: g.wait_ge(T.sem[sem], count[sem])
+    wait("g", [("q" + q, done[q], {}, q) for q in done])

@@ -8,10 +8,10 @@ BIG = 1e29
 HUGE = 5e29
 OWN = 2048.0
 GAIN = (512.0, 768.0, 1024.0, 256.0)
-PACES = [dict(cyc=0.001, pe=0.0013, gat=1.5, sca=3.5, wake=0.06, issue=0.6, first=1.6, way=(1.4, 2.2), store=1.5),
-         dict(cyc=0.001, pe=0.0010, gat=1.2, sca=2.5, wake=0.06, issue=0.5, first=1.2, way=(1.0, 1.7), store=1.5),
-         dict(cyc=0.001, pe=0.0015, gat=1.9, sca=5.0, wake=0.1, issue=0.7, first=2.0, way=(2.0, 3.0), store=1.5)]
-PLAN = dict(load=(1.45, 1.6), seed=1, tries=300, moves=4, noise=2.0, lean=1.0)
+PACES = [dict(cyc=0.00104, pe=0.00075, gat=1.5, sca=3.5, wake=0.06, issue=0.6, first=1.6, way=(1.5, 2.3), store=1.5),
+         dict(cyc=0.00095, pe=0.0006, gat=1.2, sca=2.5, wake=0.06, issue=0.6, first=1.6, way=(2.2, 3.2), store=1.5),
+         dict(cyc=0.00104, pe=0.0011, gat=1.9, sca=5.0, wake=0.06, issue=0.6, first=1.6, way=(1.1, 1.9), store=1.5)]
+PLAN = dict(load=(1.45, 1.6), seed=1, tries=40000, lean=1.0, reach=25, heat=0.05, mean=0.05)
 
 
 def _bufs():
@@ -23,9 +23,9 @@ def _bufs():
     sb("nbT", 48, "int32"); sb("xb", 1024, "bfloat16"); sb("wb", 512, "bfloat16")
     mx("X", 256); mx("wq", 128); mx("E", 512); mx("H", 256); mx("Z", 256); mx("B", 256); mx("D", 272); mx("L", 144); mx("SQ", 128); mx("SR", 128)
     for t in range(R):
-        mx("W%d" % t, 768); mx("M%d" % t, 144)
+        mx("W%d" % t, 768); mx("M%d" % t, 144); mx("N%d" % t, 256)
         sb("fl%d" % t, 4); sb("m01_%d" % t, 2); sb("U%d" % t, 16, "uint16")
-    for name, n in (("hn", 1024), ("hf", 576), ("Ho", 1024), ("Hp", 1024), ("hE", 516), ("hB", 1024), ("hM", 576), ("hL", 512), ("hP", 512), ("hQ", 512)): sb(name, n, "bfloat16")
+    for name, n in (("hn", 1024), ("hf", 576), ("hE", 516), ("hB", 1024), ("hM", 576), ("hL", 512), ("hP", 512), ("hQ", 512)): sb(name, n, "bfloat16")
     for name, n in (("pI", 1), ("rI", 1), ("gI", 1), ("uI", 1), ("aI", 1), ("bI", 1), ("yI", 256), ("wI", 256), ("rhoI", 1), ("rh", 1), ("zI", 48),
                     ("nbG", 16), ("nbH", 12), ("posI", 2), ("rgI", 4), ("npI", 6), ("nsI", 12)): sb(name, n, "int32")
     for name, n in (("pF", 1), ("I", 128), ("mF", 256), ("rF", 1), ("gF", 1), ("o48", 48), ("z48", 48), ("z3", 48), ("M48", 48), ("Fw", 1024), ("mk", 48), ("t2a", 16), ("T2", 16),
@@ -43,7 +43,7 @@ def _bufs():
 
 def _pack(b):
     out, place, fill = {}, {}, {"float32": 0, "int32": 0, "uint16": 0, "bfloat16": 0}
-    fixed = ("nbT", "xb", "wb", "hn", "hf", "Ho", "Hp", "hE", "hB", "hM", "hL", "hP", "hQ", "fl0", "fl1", "fl2", "m01_0", "m01_1", "m01_2", "FX", "FL", "off", "yo")
+    fixed = ("nbT", "xb", "wb", "hn", "hf", "hE", "hB", "hM", "hL", "hP", "hQ", "fl0", "fl1", "fl2", "m01_0", "m01_1", "m01_2", "FX", "FL", "off", "yo")
     for name, (where, shape, d) in b.items():
         place[name] = (name, 0)
         if where != "sbuf" or d not in fill or name in fixed: out[name] = (where, shape, d)
@@ -82,7 +82,11 @@ def clash(x, y):
     return x[3] == y[3] == 1 or not set(range(*x[1:])).isdisjoint(range(*y[1:]))
 
 
+LAID = []
+
+
 def arrange(calls, loaded):
+    if LAID: return [(calls[i], calls[i]["ways"][w]) for i, w in LAID]
     n = len(calls)
     before, seen = [dict() for _ in calls], {}
     for i, c in enumerate(calls):
@@ -92,60 +96,77 @@ def arrange(calls, loaded):
                 if (w or v) and clash(r, s): before[i][j] = not (c["acc"] and v and bank(r)) or before[i].get(j, False)
                 elif bank(r): before[i].setdefault(j, False)
             seen.setdefault(r[0], []).append((i, r, w))
+    above = [set() for _ in calls]
+    for i in range(n):
+        for j in before[i]: above[i] |= above[j] | {j}
+        for j in [j for j in before[i] if any(j in above[k] for k in before[i])]: del before[i][j]
     after = [[] for _ in calls]
     for i in range(n):
         for j in before[i]: after[j].append(i)
     wake, chain = PACES[0]["wake"], [0.0] * n
     for i in reversed(range(n)): chain[i] = min(w[1][0] for w in calls[i]["ways"]) + calls[i]["lat"][0] + max([wake + chain[k] for k in after[i]] + [0.0])
     early = [max([loaded.get(r[0], 0.0) for r in c["rd"]] + [0.0]) for c in calls]
-    state = [PLAN["seed"]]
+    left, ready, busy, at = [len(b) for b in before], [i for i in range(n) if not before[i]], {"s": [(0.0, 0.25)], "y": [(0.0, 0.4)]}, [None] * n
+    while ready:
+        i = max(ready, key=lambda k: chain[k])
+        ready.remove(i)
+        pick = None
+        for x, w in enumerate(calls[i]["ways"]):
+            t = max([early[i]] + [at[j][1] + calls[j]["lat"][0] + (wake if hard or at[j][2] != w[0] else 0.0) for j, hard in before[i].items()])
+            for a, b in busy.setdefault(w[0], []):
+                if t + w[1][0] <= a: break
+                t = max(t, b)
+            e = t + w[1][0] + (PLAN["lean"] if w[0] == "v" else 0.0)
+            if pick is None or e < pick[4]: pick = (t, t + w[1][0], w[0], x, e)
+        at[i] = pick
+        busy[pick[2]].append(pick[:2])
+        busy[pick[2]].sort()
+        for k in after[i]:
+            left[k] -= 1
+            if not left[k]: ready.append(k)
+    order, way = sorted(range(n), key=lambda i: (at[i][0], i)), [a[3] for a in at]
+    edges = [tuple(b.items()) for b in before]
 
-    def draw():
-        state[0] = (state[0] * 1103515245 + 12345) % 2147483648
-        return state[0] / 2147483648
-
-    def lay(shift, lean):
-        left, ready, busy, at = [len(b) for b in before], [i for i in range(n) if not before[i]], {"s": [(0.0, 0.25)], "y": [(0.0, 0.4)]}, [None] * n
-        while ready:
-            i = max(ready, key=lambda k: chain[k] + shift[k])
-            ready.remove(i)
-            pick = None
-            for w in calls[i]["ways"]:
-                t = max([early[i]] + [at[j][1] + calls[j]["lat"][0] + (wake if hard or at[j][2][0] != w[0] else 0.0) for j, hard in before[i].items()])
-                for a, b in busy.setdefault(w[0], []):
-                    if t + w[1][0] <= a: break
-                    t = max(t, b)
-                e = t + w[1][0] + (lean[i] if w[0] == "v" else 0.0)
-                if pick is None or e < pick[3]: pick = (t, t + w[1][0], w, e)
-            at[i] = pick
-            busy[pick[2][0]].append(pick[:2])
-            busy[pick[2][0]].sort()
-            for k in after[i]:
-                left[k] -= 1
-                if not left[k]: ready.append(k)
-        order = sorted(range(n), key=lambda i: (at[i][0], i))
-        ends = []
+    def span(order, way):
+        total = 0.0
+        queue = [calls[i]["ways"][way[i]][0] for i in range(n)]
         for s, pace in enumerate(PACES):
-            free, end = {"s": 0.25, "y": 0.4}, [0.0] * n
+            free, end, wake = {"v": 0.0, "s": 0.25, "t": 0.0, "g": 0.0, "y": 0.4}, [0.0] * n, pace["wake"]
             for i in order:
-                q = at[i][2][0]
-                t = max([early[i], free.get(q, 0.0)] + [end[j] + (pace["wake"] if hard or at[j][2][0] != q else 0.0) for j, hard in before[i].items()])
-                free[q] = t + at[i][2][1][s]
-                end[i] = free[q] + calls[i]["lat"][s]
-            ends.append(max(end))
-        return sum(ends), [(calls[i], at[i][2]) for i in order]
+                q = queue[i]
+                t = max(early[i], free[q])
+                for j, hard in edges[i]:
+                    e = end[j] + wake if hard or queue[j] != q else end[j]
+                    if e > t: t = e
+                c = calls[i]
+                free[q] = t = t + c["ways"][way[i]][1][s]
+                end[i] = t + c["lat"][s]
+            total += max(end) + PLAN["mean"] * sum(end) / n
+        return total
 
-    shift, lean = [0.0] * n, [PLAN["lean"]] * n
-    best = lay(shift, lean)
+    state = [PLAN["seed"]]
+    def draw(k):
+        state[0] = (state[0] * 1103515245 + 12345) % 2147483648
+        return (state[0] >> 8) * k >> 23
+    now = best = span(order, way)
+    kept = (list(order), list(way))
     for trial in range(PLAN["tries"]):
-        s, l = list(shift), list(lean)
-        for _ in range(PLAN["moves"]):
-            i = int(draw() * n)
-            if len(calls[i]["ways"]) > 1 and draw() < 0.5: l[i] = (draw() - 0.3) * 2.0
-            else: s[i] = (draw() - 0.5) * PLAN["noise"]
-        now = lay(s, l)
-        if now[0] <= best[0]: best, shift, lean = now, s, l
-    return best[1]
+        a = draw(n)
+        i, o, w = order[a], list(order), way
+        if len(calls[i]["ways"]) > 1 and draw(3) == 0:
+            w = list(way)
+            w[i] = 1 - w[i]
+        else:
+            lo, hi = a, a
+            while lo > max(0, a - PLAN["reach"]) and o[lo - 1] not in before[i]: lo -= 1
+            while hi < min(n - 1, a + PLAN["reach"]) and i not in before[o[hi + 1]]: hi += 1
+            o.insert(lo + draw(hi - lo + 1), o.pop(a))
+        new = span(o, w)
+        if new <= now + PLAN["heat"] * (1 - trial / PLAN["tries"]) * draw(1000) / 1000:
+            now, order, way = new, o, w
+            if new < best: best, kept = new, (o, w)
+    LAID.extend((i, kept[1][i]) for i in kept[0])
+    return arrange(calls, loaded)
 
 
 def rank_program(g, core, T, topo):
@@ -170,7 +191,7 @@ def rank_program(g, core, T, topo):
     def sc(s): return ap(s) if isinstance(s, tuple) else s
     def cols(*x): return [s for s in x if isinstance(s, tuple)]
     def real(*x): return all(KIND[r[0]] in ("float32", "bfloat16") for r in x)
-    def plain(n, k=1.0, more=0): return cycles(max(64, n * k) + more)
+    def plain(n, k=1.0, more=0): return cycles(64 + n * k + more)
     def narrow(*x): return 0.5 if all(KIND[r[0]] in ("bfloat16", "uint16") for r in x) else 1.0
     def picked(n, q="v"): return each(lambda p: ((60 if q == "v" else 78) + n * p["gat"]) * p["cyc"])
     def tt(out, in0, in1, op, off=None):
@@ -191,10 +212,10 @@ def rank_program(g, core, T, topo):
     def count(out, pattern, base, cm):
         if KIND[out[0]] == "int32": return lambda e: e.iota(ap(out), pattern, base, cm)
         return lambda e: e.iota(ap(out), pattern, base, cm, allow_small_or_imprecise_dtypes=True)
-    def iota(out, pattern, base, cm): put([("g", cycles(157 + 2 * size(out)), count(out, pattern, base, cm))], [], [out], kind="iota")
-    def ms(out, c): put([("v", plain(size(out), narrow(out)), lambda e: e.memset(ap(out), c)), ("g", cycles(157 + 2 * size(out)), count(out, [[0, size(out)]], int(c), 0))], [], [out], kind="iota")
+    def iota(out, pattern, base, cm): put([("g", cycles(200 + 2 * size(out)), count(out, pattern, base, cm))], [], [out], kind="iota")
+    def ms(out, c): put([("v", plain(size(out), narrow(out)), lambda e: e.memset(ap(out), c)), ("g", cycles(200 + 2 * size(out)), count(out, [[0, size(out)]], int(c), 0))], [], [out], kind="iota")
     def within(out, src, cm, base, fill):
-        put([("g", cycles(205 + 2 * size(out)), lambda e: e.affine_select(ap(out), ap(src), [[0, size(out)]], A.is_ge, fill, base, cm))], [src], [out], kind="select")
+        put([("g", cycles(250 + 2 * size(out)), lambda e: e.affine_select(ap(out), ap(src), [[0, size(out)]], A.is_ge, fill, base, cm))], [src], [out], kind="select")
     def rsum(out, in_, junk):
         put([("v", plain(size(in_)), lambda e: e.tensor_reduce(ap(out), ap(in_), AxisListType.X, A.add)),
              ("s", plain(size(in_), 1, 24), lambda e: e.activation(ap(junk), ap(in_), AF.Copy, accum_out=ap(out)))], [in_], [out, junk])
@@ -391,7 +412,7 @@ def rank_program(g, core, T, topo):
     def SS(k): return ("SL", 200 * k + 99, 200 * k + 200, 100)
 
     for t in range(R):
-        w, far, m, fl = "W%d" % t, "M%d" % t, "m01_%d" % t, "fl%d" % t
+        w, far, near, m, fl = "W%d" % t, "M%d" % t, "N%d" % t, "m01_%d" % t, "fl%d" % t
         def columns(kind, view):
             def what(d):
                 own, there = (w + kind,) + FAR[d], (far + kind, FAR[d][0] - F0, FAR[d][1] - F0)
@@ -416,23 +437,23 @@ def rank_program(g, core, T, topo):
             h, lo = i % 2, 1 - i // 2
             ts(("hL", h + 2 * lo, 64, 4), ("EQ", 8 - 8 * h, 24 - 8 * h), C("sel", i), A.mult, C("n2", h), A.mult)
         quant(("L", 0, 128), W("hL"))
-        mm(2, ("D", 144, 272), ("L", 0, 128), True, False)
-        mm(2, ("D", 144, 272), ("L", 16, 144), False, True)
-        cp(W("lst"), ("ps2", 0, 16))
-        for b in range(4): mm(4 + b, Eb(b), (w, 0, 256))
+        mm(0, ("D", 144, 272), ("L", 0, 128), True, False)
+        mm(0, ("D", 144, 272), ("L", 16, 144), False, True)
+        cp(W("lst"), ("ps0", 0, 16))
+        pick((near, 0, 256), (w, 0, 256), W("lst"))
         for b in range(4):
-            half, again = ("Ho", 256 * b, 256 * b + 256), ("Hp", 256 * b, 256 * b + 256)
-            cp(half, ("ps%d" % (4 + b), 0, 256))
-            cp(again, half)
-            tt(("hn", b, 1024, 4), half, again, A.add, W("lst"))
+            mm(4 + b, Eb(b), (w, 0, 256), True, False)
+            mm(4 + b, Eb(b), (near, 0, 256), False, True)
+            cp(("hn", b, 1024, 4), ("ps%d" % (4 + b), 0, 256))
         quant((w, 512, 768), W("hn"))
-        for b in range(4): mm(4 + b, Eb(b), (w, F0, F1), True, False)
-        for h in range(2): mm(h, (w, 128 * h, 128 * h + 128), (far, 16 * h, 16 * h + 128))
-        for b in range(4): mm(4 + b, Eb(b), (far, 0, 144), False, True)
-        for b in range(4): cp(("hf", b, 576, 4), ("ps%d" % (4 + b), 0, 144))
+        for h in range(2): mm(2 + h, (w, 128 * h, 128 * h + 128), (far, 16 * h, 16 * h + 128))
+        tt(("SL", 451, 499), ("ps2", 0, 48), ("I", F0, 128), A.mult)
+        tt(("SL", 503, 599), ("ps3", 32, 128), ("I", 0, 96), A.mult)
+        for b, k in enumerate((1, 0, 3, 1)):
+            mm(k, Eb(b), (w, F0, F1), True, False)
+            mm(k, Eb(b), (far, 0, 144), False, True)
+            cp(("hf", b, 576, 4), ("ps%d" % k, 0, 144))
         quant((w, 256 + F0, 256 + F1), W("hf"))
-        tt(("SL", 451, 499), ("ps0", 0, 48), ("I", F0, 128), A.mult)
-        tt(("SL", 503, 599), ("ps1", 32, 128), ("I", 0, 96), A.mult)
         rsum(C("S2", 0), ("SL", 451, 500), ("jr", 0, 49))
         rsum(C("S2", 1), ("SL", 503, 600), ("jr", 128, 225))
         for h in range(2):
@@ -441,16 +462,16 @@ def rank_program(g, core, T, topo):
                 if k < 2: ts(("hM", a, a + 373, 12), mk, C("th", 2 * k + h), A.add, C("S2", h), A.is_ge)
                 else: ts(("hM", a, a + 373, 12), mk, C(m, h), A.add, C("S2", h), A.is_lt)
         quant(("D", 0, 144), W("hM"))
-        mm(3, ("D", 144, 272), ("D", 48, 176), True, False)
-        mm(3, ("SQ", 0, 128), ("D", 96, 224), False, False)
+        mm(2, ("D", 144, 272), ("D", 48, 176), True, False)
+        mm(2, ("SQ", 0, 128), ("D", 96, 224), False, False)
         plus(W("FX"), W("m2"), W("b1"), C(fl, 2))
         plus(("FL", 0, 8), W("m1"), W("b0"), C(fl, 1))
         plus(("FL", 8, 16), W("m3"), W("FX"), C(fl, 3))
         for h in range(2): ts(("off", 8 * h, 8 * h + 8), ("FL", 8 * h, 8 * h + 8), C("S2", h), A.is_lt, W("r1"), A.mult)
         for h in range(2): gather(("hB", h, 512, 4), ("wR", 32 * h, 32 * h + 17), ("off", 8 * h, 8 * h + 8))
         quant(("SR", 0, 128), ("hB", 0, 512))
-        mm(3, ("SR", 0, 128), ("D", 0, 128), False, True)
-        scan(W("ls"), ("ps3", 0, 48), W("D48"), A.max, A.add)
+        mm(2, ("SR", 0, 128), ("D", 0, 128), False, True)
+        scan(W("ls"), ("ps2", 0, 48), W("D48"), A.max, A.add)
         tt(W("lu"), ("ls", 2, 48, 3), W("T16"), A.min)
         cp(W("U%d" % t), W("lu"))
         pick(("W%d" % (t + 1) if t < R - 1 else "H", 0, 256), (w, 0, 768), W("U%d" % t))

@@ -8,10 +8,10 @@ BIG = 1e29
 HUGE = 5e29
 OWN = 2048.0
 GAIN = (512.0, 768.0, 1024.0, 256.0)
-PACES = [dict(cyc=0.00104, pe=0.00075, gat=1.5, sca=3.5, wake=0.06, issue=0.6, first=1.6, way=(1.5, 2.3), store=1.5),
-         dict(cyc=0.00095, pe=0.0006, gat=1.2, sca=2.5, wake=0.06, issue=0.6, first=1.6, way=(2.2, 3.2), store=1.5),
-         dict(cyc=0.00104, pe=0.0011, gat=1.9, sca=5.0, wake=0.06, issue=0.6, first=1.6, way=(1.1, 1.9), store=1.5)]
-PLAN = dict(load=(1.45, 1.6), seed=1, tries=40000, lean=1.0, reach=25, heat=0.05, mean=0.05)
+PACES = [dict(cyc=0.000830, act=0.000, pe=0.00060, fill=0.00, gat=1.56, wake=0.25, own=0.17, issue=0.30, first=0.7, wire=(0.18, 0.35, 0.93), way=0.8, store=1.2),
+         dict(cyc=0.000913, act=0.000, pe=0.00042, fill=0.05, gat=1.10, wake=0.24, own=0.15, issue=0.60, first=1.7, wire=(0.18, 0.35, 0.93), way=0.3, store=1.2),
+         dict(cyc=0.000830, act=0.020, pe=0.00080, fill=0.02, gat=1.40, wake=0.19, own=0.19, issue=0.45, first=1.5, wire=(0.34, 0.51, 1.09), way=0.9, store=1.4)]
+PLAN = dict(load=(1.25, 1.5), seed=1, tries=40000, lean=0.0, reach=25, heat=0.15, mean=0.3)
 
 
 def _bufs():
@@ -21,21 +21,22 @@ def _bufs():
         sb(name + "c", n, "float8_e4m3fn_x4")
         sb(name + "s", n, "uint8")
     sb("nbT", 48, "int32"); sb("xb", 1024, "bfloat16"); sb("wb", 512, "bfloat16")
-    mx("X", 256); mx("wq", 128); mx("E", 512); mx("H", 256); mx("Z", 256); mx("B", 256); mx("D", 272); mx("L", 144); mx("SQ", 128); mx("SR", 128)
+    mx("X", 256); mx("wq", 128); mx("E", 512); mx("H", 256); mx("Z", 256); mx("B", 256); mx("D", 400); mx("SQ", 128); mx("SR", 128); mx("M", 128 + 144 * R)
     for t in range(R):
-        mx("W%d" % t, 768); mx("M%d" % t, 144); mx("N%d" % t, 256)
-        sb("fl%d" % t, 4); sb("m01_%d" % t, 2); sb("U%d" % t, 16, "uint16")
-    for name, n in (("hn", 1024), ("hf", 576), ("hE", 516), ("hB", 1024), ("hM", 576), ("hL", 512), ("hP", 512), ("hQ", 512)): sb(name, n, "bfloat16")
-    for name, n in (("pI", 1), ("rI", 1), ("gI", 1), ("uI", 1), ("aI", 1), ("bI", 1), ("yI", 256), ("wI", 256), ("rhoI", 1), ("rh", 1), ("zI", 48),
-                    ("nbG", 16), ("nbH", 12), ("posI", 2), ("rgI", 4), ("npI", 6), ("nsI", 12)): sb(name, n, "int32")
-    for name, n in (("pF", 1), ("I", 128), ("mF", 256), ("rF", 1), ("gF", 1), ("o48", 48), ("z48", 48), ("z3", 48), ("M48", 48), ("Fw", 1024), ("mk", 48), ("t2a", 16), ("T2", 16),
-                    ("RK", 256), ("KG", 32), ("KT", 32), ("sg", 2), ("jk", 512), ("rg", 4), ("ns", 12), ("nh", 6), ("dn", 4), ("c1", 1), ("c2", 1), ("c3", 1), ("c4", 1), ("c5", 1), ("c6", 1),
-                    ("c8", 1), ("c9", 1), ("r1", 1), ("rB", 1), ("rT", 1), ("vr", 16), ("HB", 16), ("gt", 16), ("gt0", 16), ("NE", 24), ("EQ", 24), ("MK", 192), ("D48", 48), ("T16", 16),
-                    ("tg", 16), ("tq", 2), ("one", 8), ("nil", 1), ("top", 1), ("loc", 2), ("wc", 2), ("m1", 8), ("m3", 8), ("m4", 8), ("m2", 1), ("b0", 1), ("b1", 1), ("i17", 17), ("wR", 64),
-                    ("K96", 96), ("KF", 96), ("S96", 96), ("nm", 96), ("np", 96), ("MV", 64), ("G", 512), ("gm", 96), ("gs", 96), ("SL", 600), ("jr", 256), ("S2", 2), ("GL", 4), ("th", 4),
-                    ("e2", 2), ("n2", 2), ("sel", 4), ("cl", 12), ("CF", 16), ("ls", 48), ("lu", 16), ("NR", 1280), ("PRp", 256), ("PRn", 256), ("yo", 256), ("FX", 1), ("FL", 16)): sb(name, n)
-    for name, n in (("CR", 256), ("GN", 192), ("VT", 256), ("VR", 256), ("mr", 256), ("idF", 64), ("iJ", 256), ("Rp", 256), ("d3", 256), ("t3", 256)): sb(name, n, "bfloat16")
-    for name, n in (("T2u", 16), ("lKG", 2), ("lNG", 1), ("nbO", 12), ("lVR", 16), ("idT", 64), ("lG", 1), ("gI0", 16), ("gU0", 6), ("gU", 6), ("lC", 1), ("lB", 16), ("posU", 16),
+        mx("W%d" % t, 768); mx("N%d" % t, 256)
+        sb("fl%d" % t, 16); sb("m01_%d" % t, 2); sb("U%d" % t, 16, "uint16")
+    for name, n in (("hn", 1024), ("hf", 576), ("hE", 516), ("hB", 1024), ("hM", 576), ("hL", 896), ("hP", 512), ("hQ", 512)): sb(name, n, "bfloat16")
+    for name, n in (("pI", 1), ("rI", 1), ("gI", 1), ("aI", 1), ("bI", 1), ("yI", 256), ("wI", 256), ("rhoI", 1), ("rh", 1), ("zI", 1),
+                    ("nbG", 16), ("nbH", 12), ("posI", 2), ("rgI", 6), ("npI", 6), ("nsI", 12)): sb(name, n, "int32")
+    for name, n in (("pF", 1), ("mF", 256), ("rF", 1), ("gF", 1), ("o48", 48), ("s48", 48), ("t48", 48), ("z1", 1), ("z3", 1), ("M48", 48), ("Fw", 1024), ("mk", 48),
+                    ("RK", 256), ("KG", 32), ("KT", 32), ("sg", 2), ("jk", 512), ("rg", 6), ("ns", 12), ("dn", 8), ("c1", 1), ("c2", 1), ("c3", 1), ("c4", 1), ("c5", 1), ("c6", 1),
+                    ("c9", 1), ("EJ", 32), ("r1", 1), ("rB", 1), ("rT", 1), ("vr", 16), ("HB", 16), ("gt", 16), ("gt0", 16), ("NE", 24), ("EQ", 24), ("EB", 24), ("NH", 24), ("MK", 192),
+                    ("D48", 48), ("T16", 16), ("tg", 16), ("tq", 2), ("one", 8), ("nil", 1), ("top", 1), ("loc", 2), ("wc", 2), ("m1", 8), ("m3", 8), ("m4", 8), ("m2", 1), ("b0", 1), ("b1", 1),
+                    ("i17", 17), ("wR", 64), ("K96", 96), ("KA", 96), ("KB", 96), ("R96", 96), ("x2", 2), ("KF", 96), ("S96", 96), ("nm", 96), ("np", 96), ("MV", 128), ("G", 512), ("gm", 96),
+                    ("gs", 96), ("SL", 600), ("jr", 256), ("ab", 256), ("S2", 2), ("GL", 4), ("e2", 2), ("th", 4), ("n2", 2), ("away", 2), ("cl", 12), ("CF", 16), ("ls", 48), ("lu", 16),
+                    ("NR", 1280), ("PRp", 256), ("PRn", 256), ("yo", 256), ("FX", 1), ("FL", 16)): sb(name, n)
+    for name, n in (("CR", 256), ("I", 128), ("GN", 192), ("VT", 256), ("VR", 256), ("mr", 256), ("idF", 64), ("Rp", 256)): sb(name, n, "bfloat16")
+    for name, n in (("T2u", 16), ("lKG", 2), ("lNG", 1), ("nbO", 12), ("lVR", 16), ("idT", 64), ("lG", 1), ("gI0", 16), ("gU0", 6), ("gU", 6), ("lC", 1), ("lK", 6), ("posU", 16),
                     ("lst", 16), ("UA", 16), ("off", 16)): sb(name, n, "uint16")
     for i in range(8): b["ps%d" % i] = ("psum", [128, 512], "float32")
     return b
@@ -57,7 +58,7 @@ def _pack(b):
 SCRATCH, PLACE = _pack(_bufs())
 WIDTH = {k: v[1][1] for k, v in _bufs().items()}
 KIND = {k: v[2] for k, v in _bufs().items()}
-SEMAPHORES = ["qv", "qs", "qt", "qg", "ldn", "ldx", "ldb", "ldw", "ls", "st"] + ["x%s%d" % (k, t) for k in "csm" for t in range(R)]
+SEMAPHORES = ["qv", "qs", "qt", "qg", "ldn", "ldx", "ldb", "ldc", "ldw", "ls", "st"] + ["x%s%d%s" % (k, t, s) for k in "csm" for t in range(R) for s in "ab"]
 
 
 def shares(T, topo, core):
@@ -67,7 +68,7 @@ def shares(T, topo, core):
     eng, used = {}, []
     for d in sorted(FAR, key=lambda d: (d not in away, d)):
         free = [e for e in may[d] if e not in used]
-        eng[d] = free[:len(may[d]) // len(away)] if d in away else free[::2][:4]
+        eng[d] = free[:len(may[d]) // len(away)] if d in away else free[::2]
         used += eng[d]
     return peer, eng
 
@@ -92,7 +93,7 @@ def arrange(calls, loaded):
     for i, c in enumerate(calls):
         for r, w in [(norm(r), False) for r in c["rd"]] + [(norm(r), True) for r in c["wr"]]:
             for j, s, v in seen.get(r[0], ()):
-                if j == i: continue
+                if j == i or r[0] == "issue" and w and not v: continue
                 if (w or v) and clash(r, s): before[i][j] = not (c["acc"] and v and bank(r)) or before[i].get(j, False)
                 elif bank(r): before[i].setdefault(j, False)
             seen.setdefault(r[0], []).append((i, r, w))
@@ -112,7 +113,7 @@ def arrange(calls, loaded):
         ready.remove(i)
         pick = None
         for x, w in enumerate(calls[i]["ways"]):
-            t = max([early[i]] + [at[j][1] + calls[j]["lat"][0] + (wake if hard or at[j][2] != w[0] else 0.0) for j, hard in before[i].items()])
+            t = max([early[i]] + [at[j][1] + calls[j]["lat"][0] + (wake if at[j][2] != w[0] else PACES[0]["own"] if hard else 0.0) for j, hard in before[i].items()])
             for a, b in busy.setdefault(w[0], []):
                 if t + w[1][0] <= a: break
                 t = max(t, b)
@@ -127,32 +128,39 @@ def arrange(calls, loaded):
     order, way = sorted(range(n), key=lambda i: (at[i][0], i)), [a[3] for a in at]
     edges = [tuple(b.items()) for b in before]
 
-    def span(order, way):
-        total = 0.0
+    def span(order, way, start, saved):
+        total, keep = 0.0, []
         queue = [calls[i]["ways"][way[i]][0] for i in range(n)]
         for s, pace in enumerate(PACES):
-            free, end, wake = {"v": 0.0, "s": 0.25, "t": 0.0, "g": 0.0, "y": 0.4}, [0.0] * n, pace["wake"]
-            for i in order:
+            wake, own = pace["wake"], pace["own"]
+            if start: marks, end = saved[s][0][:start // 16 + 1], list(saved[s][1])
+            else: marks, end = [{"v": 0.0, "s": 0.25, "t": 0.0, "g": 0.0, "y": 0.4, "a": 0.0, "b": 0.0}], [0.0] * n
+            free = dict(marks[-1])
+            for a in range(start, n):
+                if a % 16 == 0 and a > start: marks.append(dict(free))
+                i = order[a]
                 q = queue[i]
-                t = max(early[i], free[q])
+                t = free[q]
+                if early[i] > t: t = early[i]
                 for j, hard in edges[i]:
-                    e = end[j] + wake if hard or queue[j] != q else end[j]
+                    e = end[j] + (wake if queue[j] != q else own if hard else 0.0)
                     if e > t: t = e
                 c = calls[i]
                 free[q] = t = t + c["ways"][way[i]][1][s]
                 end[i] = t + c["lat"][s]
             total += max(end) + PLAN["mean"] * sum(end) / n
-        return total
+            keep.append((marks, end))
+        return total, keep
 
     state = [PLAN["seed"]]
     def draw(k):
         state[0] = (state[0] * 1103515245 + 12345) % 2147483648
         return (state[0] >> 8) * k >> 23
-    now = best = span(order, way)
-    kept = (list(order), list(way))
+    now, saved = span(order, way, 0, None)
+    best, kept = now, (order, way)
     for trial in range(PLAN["tries"]):
         a = draw(n)
-        i, o, w = order[a], list(order), way
+        i, o, w, b = order[a], order, way, a
         if len(calls[i]["ways"]) > 1 and draw(3) == 0:
             w = list(way)
             w[i] = 1 - w[i]
@@ -160,10 +168,14 @@ def arrange(calls, loaded):
             lo, hi = a, a
             while lo > max(0, a - PLAN["reach"]) and o[lo - 1] not in before[i]: lo -= 1
             while hi < min(n - 1, a + PLAN["reach"]) and i not in before[o[hi + 1]]: hi += 1
-            o.insert(lo + draw(hi - lo + 1), o.pop(a))
-        new = span(o, w)
+            b = lo + draw(hi - lo + 1)
+            q = calls[i]["ways"][way[i]][0]
+            if not any(calls[k]["ways"][way[k]][0] == q for k in (o[b:a] if b < a else o[a + 1:b + 1])) and draw(4): continue
+            o = list(o)
+            o.insert(b, o.pop(a))
+        new, keep = span(o, w, min(a, b) // 16 * 16, saved)
         if new <= now + PLAN["heat"] * (1 - trial / PLAN["tries"]) * draw(1000) / 1000:
-            now, order, way = new, o, w
+            now, order, way, saved = new, o, w, keep
             if new < best: best, kept = new, (o, w)
     LAID.extend((i, kept[1][i]) for i in kept[0])
     return arrange(calls, loaded)
@@ -176,7 +188,9 @@ def rank_program(g, core, T, topo):
 
     def each(f): return tuple(f(p) for p in PACES)
     def cycles(n): return each(lambda p: n * p["cyc"])
-    def put(ways, rd, wr, acc=False, lat=None, kind="c", parts=None): calls.append(dict(ways=ways, rd=rd, wr=wr, acc=acc, lat=lat or cycles(0), kind=kind, parts=parts))
+    def put(ways, rd, wr, acc=False, lat=None, kind="c", sem=None):
+        ways = [(q, tuple(x + (p["act"] * (2 if isinstance(f, tuple) else 1) if q == "s" and kind == "c" else 0.0) for x, p in zip(t, PACES)), f) for q, t, f in ways]
+        calls.append(dict(ways=ways, rd=rd, wr=wr, acc=acc, lat=lat or cycles(0), kind=kind, sem=sem))
 
     def ap(r, p=None):
         name, a, b, st = norm(r)
@@ -191,7 +205,8 @@ def rank_program(g, core, T, topo):
     def sc(s): return ap(s) if isinstance(s, tuple) else s
     def cols(*x): return [s for s in x if isinstance(s, tuple)]
     def real(*x): return all(KIND[r[0]] in ("float32", "bfloat16") for r in x)
-    def plain(n, k=1.0, more=0): return cycles(64 + n * k + more)
+    def plain(n, k=1.0, more=0): return cycles(max(64, n * k) + more)
+    def twice(n): return each(lambda p: 2 * max(64, n) * p["cyc"] + p["own"])
     def narrow(*x): return 0.5 if all(KIND[r[0]] in ("bfloat16", "uint16") for r in x) else 1.0
     def picked(n, q="v"): return each(lambda p: ((60 if q == "v" else 78) + n * p["gat"]) * p["cyc"])
     def tt(out, in0, in1, op, off=None):
@@ -201,21 +216,32 @@ def rank_program(g, core, T, topo):
         t = plain(size(out), narrow(out, in0))
         if op1 is None: put([("v", t, lambda e: e.tensor_scalar(ap(out), ap(in0), sc(s1), None, op0))], [in0] + cols(s1), [out])
         else: put([("v", t, lambda e: e.tensor_scalar(ap(out), ap(in0), sc(s1), sc(s2), op0, op1))], [in0] + cols(s1, s2), [out])
-    def cp(out, in_, p=None):
+    def cp(out, in_, p=None, idle=False):
         ways = [("v", plain(size(out), narrow(out, in_)), lambda e: e.tensor_copy(ap(out, p), ap(in_, p)))]
-        if real(out, in_): ways.append(("s", plain(size(out)), lambda e: e.activation(ap(out, p), ap(in_, p), AF.Copy)))
-        put(ways, [in_], [out])
+        if idle: ways.append(("g", cycles(205 + 2 * size(out)), lambda e: e.affine_select(ap(out), ap(in_), [[0, size(out)]], A.is_ge, 0.0, 0, 0)))
+        elif real(out, in_): ways.append(("s", plain(size(out)), lambda e: e.activation(ap(out, p), ap(in_, p), AF.Copy)))
+        put(ways, [in_], [out], kind="select" if idle else "c")
     def plus(out, in_, bias, scale=1.0):
         ways = [("v", plain(size(out), narrow(out, in_)), lambda e: e.tensor_scalar(ap(out), ap(in_), sc(scale), sc(bias), A.mult, A.add))]
         if real(out, in_): ways.append(("s", plain(size(out)), lambda e: e.activation(ap(out), ap(in_), AF.Identity, bias=sc(bias), scale=sc(scale))))
         put(ways, [in_] + cols(bias, scale), [out])
+    def distance(in_, col): return lambda e: e.activation(ap(("ab", 0, size(in_))), ap(in_), AF.Abs, bias=ap(col), scale=-1.0)
+    def same(out, in_, col, gain=1.0):
+        put([("v", plain(size(out), narrow(out, in_)), lambda e: e.tensor_scalar(ap(out), ap(in_), ap(col), gain, A.is_equal, A.mult)),
+             ("s", twice(size(out)), (distance(in_, col), lambda e: e.activation(ap(out), ap(("ab", 0, size(out))), AF.Relu, bias=gain, scale=-gain)))], [in_, col], [out])
+    def apart(out, in_, col, gain):
+        put([("v", plain(size(out)), lambda e: e.tensor_scalar(ap(out), ap(in_), ap(col), gain, A.not_equal, A.mult)),
+             ("s", twice(size(out)), (distance(in_, col), lambda e: e.activation(ap(out), ap(("ab", 0, size(out))), AF.Copy, scale=gain)))], [in_, col], [out])
+    def nonzero(out, in_):
+        put([("v", plain(size(out)), lambda e: e.tensor_scalar(ap(out), ap(in_), 0.0, None, A.not_equal)), ("s", plain(size(out)), lambda e: e.activation(ap(out), ap(in_), AF.Sign))], [in_], [out])
     def count(out, pattern, base, cm):
         if KIND[out[0]] == "int32": return lambda e: e.iota(ap(out), pattern, base, cm)
         return lambda e: e.iota(ap(out), pattern, base, cm, allow_small_or_imprecise_dtypes=True)
-    def iota(out, pattern, base, cm): put([("g", cycles(200 + 2 * size(out)), count(out, pattern, base, cm))], [], [out], kind="iota")
-    def ms(out, c): put([("v", plain(size(out), narrow(out)), lambda e: e.memset(ap(out), c)), ("g", cycles(200 + 2 * size(out)), count(out, [[0, size(out)]], int(c), 0))], [], [out], kind="iota")
+    def iota(out, pattern, base, cm): put([("g", cycles(157 + 2 * size(out)), count(out, pattern, base, cm))], [], [out], kind="iota")
+    def ms(out, c): put([("v", plain(size(out), narrow(out)), lambda e: e.memset(ap(out), c)), ("g", cycles(157 + 2 * size(out)), count(out, [[0, size(out)]], int(c), 0))], [], [out], kind="iota")
     def within(out, src, cm, base, fill):
-        put([("g", cycles(250 + 2 * size(out)), lambda e: e.affine_select(ap(out), ap(src), [[0, size(out)]], A.is_ge, fill, base, cm))], [src], [out], kind="select")
+        put([("g", cycles(205 + 2 * size(out)), lambda e: e.affine_select(ap(out), ap(src), [[0, size(out)]], A.is_ge, fill, base, cm))], [src], [out], kind="select")
+    def diagonal(out, zeros, c): put([("g", cycles(205 + 256), lambda e: e.affine_select(ap(out), ap(zeros), [[-1, 128]], A.not_equal, c, 0, 1))], [zeros], [out], kind="select")
     def rsum(out, in_, junk):
         put([("v", plain(size(in_)), lambda e: e.tensor_reduce(ap(out), ap(in_), AxisListType.X, A.add)),
              ("s", plain(size(in_), 1, 24), lambda e: e.activation(ap(junk), ap(in_), AF.Copy, accum_out=ap(out)))], [in_], [out, junk])
@@ -236,29 +262,29 @@ def rank_program(g, core, T, topo):
     def mm(b, w, x, start=True, stop=True):
         n = x[2] - x[1]
         wc, ws, xc, xs = (w[0] + "c", w[1], w[2]), (w[0] + "s", w[1], w[2]), (x[0] + "c", x[1], x[2]), (x[0] + "s", x[1], x[2])
-        put([("t", each(lambda p: (n + 16) * p["pe"]), lambda e: e.matmul_mx(ap(("ps%d" % b, 0, n)), ap(wc), ap(ws), ap(xc), ap(xs), start, stop))], [wc, ws, xc, xs], [("ps%d" % b, 0, 512)], acc=not start)
+        put([("t", each(lambda p: (n + 16) * p["pe"] + p["fill"]), lambda e: e.matmul_mx(ap(("ps%d" % b, 0, n)), ap(wc), ap(ws), ap(xc), ap(xs), start, stop))], [wc, ws, xc, xs],
+            [("ps%d" % b, 0, 512)], acc=not start)
     stores = [0]
     def store(q, out, in_, view):
         stores[0] += 16
         put([(q, cycles(50), lambda e: e.dma_start(out, view))], [in_], [], lat=each(lambda p: p["store"]), kind="store")
 
     peer, eng = shares(T, topo, core)
-    incoming = sum(len(shares(T, topo, c)[1][d]) for d, c in peer.items())
+    side = {d: "ab"[topo.chip(c) != topo.chip(core)] for d, c in peer.items()}
+    incoming = {s: sum(len(shares(T, topo, c)[1][d]) for d, c in peer.items() if side[d] == s) for s in "ab"}
     sent = [0]
 
-    def send(way, *parts):
-        made = []
-        for what, sem, lands in parts:
-            tr, rd = [], []
-            for d in eng:
-                src, dst, region = what(d)
-                rid, pid, _s = topo.addr(peer[d])
-                tr.append(RemoteDMATransfer(dst_ids=[DstId(rid=rid, pnc=pid)], dma_engine_mask=sum(1 << e for e in eng[d]), remote_sem=T.sem[sem], src=src, dst=dst))
-                rd.append(region)
-            made.append((tr, rd, sem, lands))
-        put([("g", each(lambda p: p["issue"] * len(parts) + (0.0 if sent[0] else p["first"])), None)], [r for m in made for r in m[1]], [m[3] for m in made],
-            lat=each(lambda p: p["way"][way]), kind="send", parts=made)
-        sent[0] += len(parts) * sum(len(e) for e in eng.values())
+    def send(way, what, sem, lands):
+        tr, rd = [], []
+        for d in eng:
+            src, dst, region = what(d)
+            rid, pid, _s = topo.addr(peer[d])
+            tr.append(RemoteDMATransfer(dst_ids=[DstId(rid=rid, pnc=pid)], dma_engine_mask=sum(1 << e for e in eng[d]), remote_sem=T.sem[sem + side[d]], src=src, dst=dst))
+            rd.append(region)
+        put([("g", each(lambda p: p["issue"] + (0.0 if sent[0] else p["first"])), tr)], rd, [("issue", 0, 1)], kind="send")
+        sent[0] += sum(len(e) for e in eng.values())
+        for s in "ab":
+            put([(s, each(lambda p: p["wire"][way]), None)], [("issue", 0, 1)], [lands(d) for d in eng if side[d] == s], lat=each(lambda p: p["way"]), kind="land", sem=sem + s)
 
     iota(W("pI"), [[0, 1]], 0, 1)
     iota(W("mF"), [[1, 256]], 0, 0)
@@ -283,40 +309,45 @@ def rank_program(g, core, T, topo):
     within(W("b0"), W("nil"), 1, -F0, -HUGE)
     within(W("b1"), W("nil"), -1, F1 - 129, -HUGE)
     within(W("m3"), W("m4"), -1, FAR[3][1] - 129, 0.0)
+    plus(W("away"), W("loc"), 1.0, -1.0)
     ts(W("rI"), W("pI"), 15, A.bitwise_and)
     ts(W("gI"), W("pI"), 4, A.logical_shift_right)
     ts(W("aI"), W("pI"), 96, A.bitwise_and)
     ts(W("bI"), W("pI"), 1, A.bitwise_and)
-    ts(W("uI"), W("pI"), 4, A.logical_shift_right, 1, A.bitwise_and)
     cp(W("rF"), W("rI"))
     cp(W("gF"), W("gI"))
-    cp(W("pF"), W("pI"))
+    iota(W("pF"), [[0, 1]], 0, 1)
     plus(W("r1"), W("rF"), 1.0)
     plus(W("rB"), W("rF"), -OWN)
     plus(W("rT"), W("rF"), GAIN[0])
     plus(W("c6"), W("rF"), W("gF"), 8.0)
-    cp(W("iJ"), W("mF"))
-    ts(W("I"), ("mF", 0, 128), W("pF"), A.is_equal)
     ms(W("hE"), 0.0)
-    plus(("hE", 3, 515, 4), W("I"), 0.0, 0.5)
+    diagonal(W("I"), ("hE", 0, 512, 4), 1.0)
+    diagonal(("hE", 3, 515, 4), ("hE", 3, 515, 4), 0.5)
     def Eb(b): return ("E", 128 * b, 128 * b + 128)
     for b in range(4): quant(Eb(b), ("hE", 3 - b, 515 - b))
-    for i in range(2): ts(("hP", i, 512, 2), W("CR"), W("rF"), A.is_equal, OWN, A.mult)
-    quant(("D", 144, 272), W("hP"))
-    ms(W("hL"), 0.0)
-    quant(("L", 16, 144), W("hL"))
+    for i in range(2): same(("hP", i, 512, 2), W("CR"), W("rF"), OWN)
+    quant(("D", 272, 400), W("hP"))
+    ms(("hL", 384, 896), 0.0)
     ms(W("hM"), 0.0)
     ts(W("NE"), ("mF", 0, 24), -8.0, A.add, W("gF"), A.not_equal)
     plus(W("EQ"), W("NE"), 1.0 / OWN, -1.0 / OWN)
+    plus(W("EB"), W("NE"), 0.0, -HUGE)
+    plus(W("NH"), W("NE"), 0.0, HUGE)
     for k in range(3):
         for h in range(2):
             a = 32 * (2 * k + h) + (16 if k == 2 else 0)
-            plus(("MK", a, a + 16), ("NE", 8 - 8 * h, 24 - 8 * h), 0.0, HUGE if k == 2 else -HUGE)
-    ts(W("KF"), ("CR", 0, 192, 2), W("rF"), A.is_equal)
+            cp(("MK", a, a + 16), ("NH" if k == 2 else "EB", 8 - 8 * h, 24 - 8 * h), None, True)
+    same(W("KF"), ("CR", 0, 192, 2), W("rF"))
     cp(("K96", 0, 64), ("KF", 0, 64))
-    for h in range(2): plus(("K96", 64 + 16 * h, 80 + 16 * h), ("KF", 0, 16), 0.0, C("loc", h))
-    ts(W("S96"), ("CR", 0, 192, 2), 0.0, A.not_equal)
-    ms(("cl", 0, 6), 0.0)
+    within(("K96", 64, 80), ("KF", 0, 16), -1, F0 - 1, 0.0)
+    within(("K96", 80, 96), ("KF", 0, 16), 1, 128 - F1, 0.0)
+    plus(W("KA"), W("K96"), -HUGE, HUGE)
+    ts(W("R96"), ("CR", 0, 192, 2), 0.0, A.is_equal, -HUGE, A.mult)
+    cp(W("lK"), ("mF", 0, 6))
+    nonzero(W("S96"), ("CR", 0, 192, 2))
+    nonzero(W("s48"), W("o48"))
+    ms(W("cl"), 0.0)
     ms(W("D48"), 0.0)
     plus(("D48", 2, 48, 3), ("mF", 0, 256, 16), W("rB"))
     plus(W("T16"), ("mF", 0, 256, 16), W("rT"))
@@ -324,21 +355,18 @@ def rank_program(g, core, T, topo):
     ts(W("lC"), W("bI"), 24.0, A.mult, W("c9"), A.add)
     tt(("tg", 4, 6), W("tq"), W("wc"), A.add)
     ts(W("lG"), W("c6"), 16.0, A.add, 63.0, A.min)
-    ts(W("c8"), W("uI"), 16.0, A.mult, W("rF"), A.add)
-    for i in range(2): ts(("lB", i, 16, 2), ("mF", 0, 256, 32), W("c8"), A.add)
     quant(("X", 0, 256), W("xb"))
     quant(("wq", 0, 128), W("wb"))
 
     for q in range(4): plus(("Fw", 256 * q, 256 * q + 256), W("mF"), 1048576.0 * (q ^ rank), 4096.0 if q < rank else 0.0)
-    ts(W("z48"), W("o48"), W("rF"), A.add, 1.0, A.add)
-    ts(W("zI"), W("z48"), 1.0 / 3.0, A.mult)
-    ts(W("z3"), W("zI"), 3.0, A.mult)
-    tt(W("M48"), W("z3"), W("z48"), A.is_equal)
+    ts(W("zI"), W("rI"), 2.0 / 3.0, A.mult, 1.0 / 3.0, A.add)
+    ts(W("z1"), W("rI"), 2.0, A.mult, 2.0, A.add)
+    ts(W("z3"), W("zI"), -3.0, A.mult, W("z1"), A.add)
+    ts(W("M48"), W("o48"), W("z3"), A.is_equal)
     ts(W("wI"), W("yI"), 3855, A.bitwise_and)
     tt(W("mk"), W("nbT"), W("M48"), A.mult)
-    tt(W("t2a"), ("mk", 0, 48, 3), ("mk", 1, 48, 3), A.add)
-    tt(W("T2"), W("t2a"), ("mk", 2, 48, 3), A.add)
-    cp(W("T2u"), W("T2"))
+    scan(W("t48"), W("s48"), W("mk"), A.mult, A.add)
+    cp(W("T2u"), ("t48", 2, 48, 3))
     tt(W("RK"), W("Fw"), W("wI"), A.add, W("T2u"))
     ts(W("rh"), W("rF"), 3.0, A.mult, 2.0, A.add)
     ts(W("rhoI"), W("rh"), 15, A.bitwise_and)
@@ -353,6 +381,7 @@ def rank_program(g, core, T, topo):
     ts(W("posI"), W("sg"), 0.5, A.mult, 127.5 + F1, A.add)
     ts(("rgI", 0, 2), W("posI"), 15, A.bitwise_and)
     ts(("rgI", 2, 4), W("posI"), 4, A.logical_shift_right, 15, A.bitwise_and)
+    ts(("rgI", 4, 6), W("posI"), 240, A.bitwise_and)
     cp(W("rg"), W("rgI"))
     plus(W("c3"), W("gF"), W("rF"), 6.0)
     ts(W("lNG"), W("c3"), 47.0, A.min)
@@ -369,12 +398,17 @@ def rank_program(g, core, T, topo):
     ts(W("c5"), W("bI"), 32.0, A.mult)
     ts(W("lVR"), W("vr"), W("c5"), A.add)
     gather(W("VR"), W("VT"), W("lVR"))
-    for u in range(2): ts(("mr", 128 * u, 128 * u + 128), ("CR", 0, 128), C("rg", 2 + u), A.is_equal)
-    for u in range(2): ts(("hB", u, 512, 2), W("CR"), C("rg", u), A.is_equal)
+    for u in range(2): same(("mr", 128 * u, 128 * u + 128), ("CR", 0, 128), C("rg", 2 + u))
+    for u in range(2): same(("hB", u, 512, 2), W("CR"), C("rg", u))
     for u in range(2): tt(("hB", 512 + u, 768, 2), ("mr", 128 * u, 128 * u + 128), ("VR", 128 * u, 128 * u + 128), A.mult)
+    for u in range(2):
+        same(("EJ", 16 * u, 16 * u + 16), ("mF", 0, 256, 16), C("VT", 16 * u), 1.0 / OWN)
+        for lo in range(2): plus(("hB", 768 + u + 2 * lo, 832, 4), ("EJ", 16 * u, 16 * u + 16), 0.0, C("rg", u if lo else 4 + u))
     quant(("B", 0, 128), ("hB", 0, 512))
     quant(("B", 128, 256), ("hB", 512, 1024))
     mm(2, ("B", 0, 128), ("B", 128, 256))
+    mm(3, ("D", 272, 400), ("B", 128, 256))
+    cp(W("posU"), ("ps3", 64, 80))
     cp(W("idT"), ("ps2", 0, 64))
     cp(W("idF"), ("ps2", 0, 64))
     cp(("idF", 48 + F0 // 16, 48 + F1 // 16), ("ps2", F0 // 16, F1 // 16))
@@ -382,63 +416,61 @@ def rank_program(g, core, T, topo):
     tt(W("gt0"), W("idF"), W("HB"), A.add, W("lG"))
     cp(W("gU0"), ("gt0", 0, 6))
 
-    put([("v", each(lambda p: (60 + 256 * p["sca"]) * p["cyc"]), lambda e: e.tensor_copy(ap(W("Rp")).indirect(ap(("idT", 0, 16))), ap(W("iJ"))))], [("idT", 0, 16), W("iJ")], [W("Rp")])
+    gather(W("Rp"), W("mF"), W("posU"))
     gather(W("gI0"), W("idF"), W("lG"))
     tt(W("nm"), W("Rp"), W("KF"), A.mult, ("gI0", 0, 6))
     scan(W("np"), W("S96"), W("nm"), A.mult, A.add)
     cp(W("npI"), ("np", 15, 96, 16))
     tt(("gt", 0, 6), ("np", 15, 96, 16), ("HB", 0, 6), A.add)
     cp(W("gU"), ("gt", 0, 6))
-    ts(("nsI", 0, 6), W("npI"), 15, A.bitwise_and)
-    ts(("nsI", 6, 12), W("npI"), 4, A.logical_shift_right)
+    ts(("nsI", 0, 12, 2), W("npI"), 240, A.bitwise_and)
+    ts(("nsI", 1, 12, 2), W("npI"), 15, A.bitwise_and)
     cp(W("ns"), W("nsI"))
-    plus(W("nh"), ("ns", 6, 12), 0.0, 16.0)
-    for i in range(2): tt(("dn", 2 * i, 2 * i + 2), (("ns", "nh")[i], 0, 2), (("ns", "nh")[i], 2, 4), A.subtract)
-    for i in range(4): plus(("MV", 32 * (i % 2) + i // 2, 32 * (i % 2) + 32, 2), ("EQ", 8 - 8 * (i % 2), 24 - 8 * (i % 2)), 0.0, C(("nh", "ns")[i // 2], 4 + i % 2))
-    for i in range(4): ts(("hQ", i, 512, 4), ("CR", 0, 256, 2), C("ns", i), A.is_equal, GAIN[i // 2], A.mult)
+    for i in range(2): tt(("dn", 4 * i, 4 * i + 4), ("ns", 8 * i, 8 * i + 4), ("ns", 4, 8), A.subtract)
+    for h in range(2):
+        for lo in range(2):
+            eq = ("EQ", 8 - 8 * h, 24 - 8 * h)
+            plus(("hL", 512 + h + 2 * lo, 576, 4), eq, 0.0, C("ns", 4 + 2 * h + lo))
+            for i in range(2): plus(("MV", 64 * i + 32 * h + lo, 64 * i + 32 * h + 32, 2), eq, 0.0, C("dn", 4 * i + 2 * h + lo))
+    quant(("D", 144, 272), ("hL", 384, 896))
+    for i in range(4): same(("hQ", i, 512, 4), ("CR", 0, 256, 2), C("ns", 2 * i + 1), GAIN[i // 2])
     quant(("SQ", 0, 128), W("hQ"))
     for i in range(6):
         a = 32 * i + (0 if i >= 4 else 16)
-        ts(("MK", a, a + 16), ("mF", 0, 16), C("ns", 6 + i), A.not_equal, HUGE if i >= 4 else -HUGE, A.mult)
-    for h in range(2): ts(("wR", 32 * h, 32 * h + 17), W("i17"), C("ns", 4 + h), A.is_equal, C("wc", h), A.mult)
-    gather(W("d3"), W("Rp"), W("lB"))
-    tp(W("t3"), W("d3"))
-    cp(W("posU"), ("t3", 0, 256, 16))
-    for i in range(2): plus(("NR", 256 * i, 256 * i + 256), W("mF"), -1.0, 0.0)
+        apart(("MK", a, a + 16), ("mF", 0, 256, 16), C("ns", 2 * i), HUGE if i >= 4 else -HUGE)
+    for h in range(2): ts(("wR", 32 * h, 32 * h + 17), W("i17"), C("ns", 9 + 2 * h), A.is_equal, C("wc", h), A.mult)
+    for i in range(2): ms(("NR", 256 * i, 256 * i + 256), -1.0)
     for k in range(3): gather(("NR", 512 + 256 * k, 768 + 256 * k), W("mF"), ("idT", 16 + 16 * k, 32 + 16 * k), 256.0 * rank)
     for d, (a, b) in FAR.items(): plus(("NR", 256 + a, 256 + b), ("NR", 1024 + a, 1024 + b), 256.0 * ((rank ^ d) - rank))
 
-    def S(i): return C("SL", 100 * i + 99)
-    def SS(k): return ("SL", 200 * k + 99, 200 * k + 200, 100)
+    def S(i): return C("gs", 16 * i + 15)
+    def SS(k): return ("gs", 32 * k + 15, 32 * k + 32, 16)
+    quant(("M", 0, 128), W("hP"))
 
     for t in range(R):
-        w, far, near, m, fl = "W%d" % t, "M%d" % t, "N%d" % t, "m01_%d" % t, "fl%d" % t
-        def columns(kind, view):
-            def what(d):
-                own, there = (w + kind,) + FAR[d], (far + kind, FAR[d][0] - F0, FAR[d][1] - F0)
-                return view(own), view(there), own
-            return what, "x%s%d" % (kind, t), W(far + kind)
-        send(1, columns("c", octets), columns("s", ap))
+        w, near, m, fl, o = "W%d" % t, "N%d" % t, "m01_%d" % t, "fl%d" % t, 128 + 144 * t
+        for way, kind, view in ((2, "c", octets), (1, "s", ap)):
+            def there(d): return ("M" + kind, FAR[d][0] + o - F0, FAR[d][1] + o - F0)
+            send(way, lambda d: (view((w + kind,) + FAR[d]), view(there(d)), (w + kind,) + FAR[d]), "x%s%d" % (kind, t), there)
         for h in range(2): mm(h, (w, 128 * h, 128 * h + 128), (w, 0, 256) if t else ("X", 0, 256))
         for h in range(2): cp(("G", 256 * h, 256 * h + 256), ("ps%d" % h, 0, 256))
-        tt(W("gm"), W("G"), W("K96"), A.mult, W("gU" if t else "gU0"))
-        scan(W("gs"), W("S96"), W("gm"), A.mult, A.add)
-        tt(("SL", 99, 600, 100), ("gs", 15, 96, 16), ("cl", 0, 6), A.add)
+        if t: tt(W("KB"), W("cl"), W("KA"), A.add, W("lK"))
+        tt(W("gm"), W("G"), W("KB" if t else "KA"), A.add, W("gU" if t else "gU0"))
+        scan(W("gs"), W("R96"), W("gm"), A.add, A.max)
+        for h in range(2): ts(C("x2", h), C("cl", 4 + h), C("away", h), A.mult)
+        for h in range(2): plus(C("SL", 499 + 100 * h), S(4 + h), C("x2", h), C("loc", h))
         tt(W(m), SS(0), SS(1), A.max)
-        send(0, (lambda d: (ap(C(m, FAR[d][0] // 128)), ap(C(fl, d)), C(m, FAR[d][0] // 128)), "xm%d" % t, W(fl)))
-        tt(("GL", 0, 2), SS(0), SS(1), A.is_lt)
+        send(0, lambda d: (ap(C(m, FAR[d][0] // 128)), ap(C(fl, 4 * d)), C(m, FAR[d][0] // 128)), "xm%d" % t, lambda d: C(fl, 4 * d))
         tt(("GL", 2, 4), SS(0), SS(1), A.is_ge)
+        plus(("GL", 0, 2), ("GL", 2, 4), 1.0, -1.0)
         for h in range(2): ts(C("e2", h), S(4 + h), C(m, h), A.is_gt, C("loc", h), A.mult)
-        plus(W("n2"), W("e2"), 1.0, -1.0)
-        for i in range(4): plus(C("sel", i), C("GL", 2 + i % 2), C(("ns", "nh")[i // 2], 2 + i % 2), C("dn", i))
+        for h in range(2): ts(C("n2", h), S(4 + h), C(m, h), A.is_le, C("away", h), A.max)
         for i in range(4): plus(C("th", i), C("GL", i), S(i), -HUGE)
-        for h in range(2): plus(("hL", 64 + h, 128, 2), ("MV", 32 * h, 32 * h + 32), 0.0, C("e2", h))
-        for i in range(4):
-            h, lo = i % 2, 1 - i // 2
-            ts(("hL", h + 2 * lo, 64, 4), ("EQ", 8 - 8 * h, 24 - 8 * h), C("sel", i), A.mult, C("n2", h), A.mult)
-        quant(("L", 0, 128), W("hL"))
-        mm(0, ("D", 144, 272), ("L", 0, 128), True, False)
-        mm(0, ("D", 144, 272), ("L", 16, 144), False, True)
+        for h in range(2):
+            ts(("hL", 384 + h, 448, 2), ("MV", 32 * h, 32 * h + 32), C("GL", 2 + h), A.mult, C("n2", h), A.mult)
+            plus(("hL", 448 + h, 512, 2), ("MV", 64 + 32 * h, 96 + 32 * h), 0.0, C("e2", h))
+        quant(("D", 48, 176), ("hL", 0, 512))
+        for i in (2, 0, 1): mm(0, ("D", 272, 400), ("D", 144 + 16 * i, 272 + 16 * i), i == 2, i == 1)
         cp(W("lst"), ("ps0", 0, 16))
         pick((near, 0, 256), (w, 0, 256), W("lst"))
         for b in range(4):
@@ -446,27 +478,25 @@ def rank_program(g, core, T, topo):
             mm(4 + b, Eb(b), (near, 0, 256), False, True)
             cp(("hn", b, 1024, 4), ("ps%d" % (4 + b), 0, 256))
         quant((w, 512, 768), W("hn"))
-        for h in range(2): mm(2 + h, (w, 128 * h, 128 * h + 128), (far, 16 * h, 16 * h + 128))
-        tt(("SL", 451, 499), ("ps2", 0, 48), ("I", F0, 128), A.mult)
+        for h in range(2): mm(2 + h, (w, 128 * h, 128 * h + 128), ("M", o - 80 + 96 * h, o + 48 + 96 * h))
+        tt(("SL", 451, 499), ("ps2", F0, 128), ("I", F0, 128), A.mult)
         tt(("SL", 503, 599), ("ps3", 32, 128), ("I", 0, 96), A.mult)
         for b, k in enumerate((1, 0, 3, 1)):
             mm(k, Eb(b), (w, F0, F1), True, False)
-            mm(k, Eb(b), (far, 0, 144), False, True)
+            mm(k, Eb(b), ("M", o, o + 144), False, True)
             cp(("hf", b, 576, 4), ("ps%d" % k, 0, 144))
         quant((w, 256 + F0, 256 + F1), W("hf"))
         rsum(C("S2", 0), ("SL", 451, 500), ("jr", 0, 49))
         rsum(C("S2", 1), ("SL", 503, 600), ("jr", 128, 225))
         for h in range(2):
-            for k in range(3):
-                a, mk = (192 + h, 198 + h, 8 + h)[k], ("MK", 32 * (2 * k + h), 32 * (2 * k + h) + 32)
-                if k < 2: ts(("hM", a, a + 373, 12), mk, C("th", 2 * k + h), A.add, C("S2", h), A.is_ge)
-                else: ts(("hM", a, a + 373, 12), mk, C(m, h), A.add, C("S2", h), A.is_lt)
+            for k in range(2): ts(("hM", 192 + 6 * k + h, 192 + 6 * k + h + 373, 12), ("MK", 32 * (2 * k + h), 32 * (2 * k + h) + 32), C("th", 2 * k + h), A.add, C("S2", h), A.is_ge)
+            ts(("hM", 8 + h, 8 + h + 373, 12), ("MK", 128 + 32 * h, 160 + 32 * h), C(m, h), A.add, C("S2", h), A.is_lt)
         quant(("D", 0, 144), W("hM"))
-        mm(2, ("D", 144, 272), ("D", 48, 176), True, False)
+        mm(2, ("D", 272, 400), ("D", 48, 176), True, False)
         mm(2, ("SQ", 0, 128), ("D", 96, 224), False, False)
-        plus(W("FX"), W("m2"), W("b1"), C(fl, 2))
-        plus(("FL", 0, 8), W("m1"), W("b0"), C(fl, 1))
-        plus(("FL", 8, 16), W("m3"), W("FX"), C(fl, 3))
+        plus(W("FX"), W("m2"), W("b1"), C(fl, 8))
+        plus(("FL", 0, 8), W("m1"), W("b0"), C(fl, 4))
+        plus(("FL", 8, 16), W("m3"), W("FX"), C(fl, 12))
         for h in range(2): ts(("off", 8 * h, 8 * h + 8), ("FL", 8 * h, 8 * h + 8), C("S2", h), A.is_lt, W("r1"), A.mult)
         for h in range(2): gather(("hB", h, 512, 4), ("wR", 32 * h, 32 * h + 17), ("off", 8 * h, 8 * h + 8))
         quant(("SR", 0, 128), ("hB", 0, 512))
@@ -481,7 +511,7 @@ def rank_program(g, core, T, topo):
             plus(("cl", 6 * t, 6 * t + 6), ("CF", 0, 6), 0.0, -BIG)
         if t == 1: tt(("cl", 0, 6), ("cl", 0, 6), ("cl", 6, 12), A.add)
 
-    pick(("Z", 0, 256), ("H", 0, 256), W("posU"))
+    for h in range(2): pick(("Z", 128 * h, 128 * h + 128), ("H", 0, 256), ("posU", 8 * h, 8 * h + 8))
     store("y", T.oc[:, :], ("Zc", 0, 256), octets(("Zc", 0, 256)))
     for k in range(4): store("y", T.osc[4 * k:4 * k + 4, :], ("Zs", 0, 256), T.Zs[32 * k:32 * k + 4, 0:256])
     for h in range(2):
@@ -496,7 +526,7 @@ def rank_program(g, core, T, topo):
     queues = {"v": g.vector, "s": g.scalar, "t": g.tensor, "g": g, "y": g.sync}
     done = {q: 0 for q in "vstg"}
     known = {q: {} for q in queues}
-    writes, reads, last = {}, {}, [None]
+    writes, reads, last, pair = {}, {}, [None], [0]
 
     def wait(q, evs):
         for sem, val, snap, _q in sorted(evs, key=lambda e: -e[1]):
@@ -516,16 +546,17 @@ def rank_program(g, core, T, topo):
 
     for i in range(8): queues["ys"[i % 2]].dma_start(T.nbT[16 * i:16 * i + 16, :], T.nb[:, :]).then_inc(T.sem.ldn, 16)
     note(("ldn", 128, {}, "d"), [], [W("nbT")])
-    for sem, region, src in (("ldx", W("xb"), T.x[:, :]), ("ldb", ("hB", 768, 1024), T.x[:, 0:256]), ("ldw", W("wb"), T.w[:, :])):
+    for sem, region, src in (("ldx", W("xb"), T.x[:, :]), ("ldb", ("hB", 832, 1024), T.x[:, 0:192]), ("ldc", ("hL", 0, 384), T.x[:, 0:384]), ("ldw", W("wb"), T.w[:, :])):
         g.sync.dma_start(ap(region), src).then_inc(T.sem[sem], 16)
         note((sem, 16, {}, "d"), [], [region])
 
     for c, (q, _t, call) in arrange(calls, {"nbT": PLAN["load"][0], "xb": PLAN["load"][1], "wb": PLAN["load"][1]}):
         if c["kind"] == "send":
-            for tr, rd, sem, lands in c["parts"]:
-                wait("g", made(rd))
-                g.remote_dma_fused(tr, local_sem=T.sem.ls)
-                note((sem, incoming, {}, "d"), [], [lands])
+            wait("g", made(c["rd"]))
+            g.remote_dma_fused(call, local_sem=T.sem.ls)
+            continue
+        if c["kind"] == "land":
+            note((c["sem"], incoming[q], {}, "d"), [], c["wr"])
             continue
         evs = made(c["rd"]) + [e for r in c["rd"] if bank(r) for w, e in reads.get(r[0], []) if e[3] != q]
         for r in map(norm, c["wr"]):
@@ -537,6 +568,12 @@ def rank_program(g, core, T, topo):
         wait(q, evs)
         if c["kind"] == "store": call(queues[q]).then_inc(T.sem.st, 16)
         else:
+            if isinstance(call, tuple):
+                wait(q, [("q" + q, pair[0], {}, q)])
+                done[q] += 1
+                call[0](queues[q]).then_inc(T.sem["q" + q], 1)
+                wait(q, [("q" + q, done[q], {}, q)])
+                call, pair[0] = call[1], done[q] + 1
             done[q] += 1
             call(queues[q]).then_inc(T.sem["q" + q], 1)
             note(("q" + q, done[q], dict(known[q]), q), c["rd"], c["wr"])

from concourse.bass import DstId, RemoteDMATransfer
from concourse.mybir import dt, AluOpType as A, AxisListType, ActivationFunctionType as AF

P, F, R = 256, 48, 3
FAR = {1: (80, 128), 2: (128, 176), 3: (176, 224)}
F0, F1 = 80, 224
BIG = 1e29
HUGE = 5e29
OWN = 2048.0
GAIN = (512.0, 768.0, 1024.0, 256.0)
PACES = [dict(cyc=0.000830, act=0.000, pe=0.00060, fill=0.00, gat=1.56, wake=0.25, own=0.17, issue=0.30, first=0.7, wire=(0.18, 0.35, 0.93), way=0.8, store=1.2),
         dict(cyc=0.000913, act=0.000, pe=0.00042, fill=0.05, gat=1.10, wake=0.24, own=0.15, issue=0.60, first=1.7, wire=(0.18, 0.35, 0.93), way=0.3, store=1.2),
         dict(cyc=0.000830, act=0.020, pe=0.00080, fill=0.02, gat=1.40, wake=0.19, own=0.19, issue=0.45, first=1.5, wire=(0.34, 0.51, 1.09), way=0.9, store=1.4)]
PLAN = dict(load=(1.25, 1.5), seed=1, tries=40000, lean=0.0, reach=25, heat=0.15, mean=0.3)


def _bufs():
    b = {}
    def sb(name, n, d="float32"): b[name] = ("sbuf", [128, n], d)
    def mx(name, n):
        sb(name + "c", n, "float8_e4m3fn_x4")
        sb(name + "s", n, "uint8")
    sb("nbT", 48, "int32"); sb("xb", 1024, "bfloat16"); sb("wb", 512, "bfloat16")
    mx("X", 256); mx("wq", 128); mx("E", 512); mx("H", 256); mx("Z", 256); mx("B", 256); mx("D", 400); mx("SQ", 128); mx("SR", 128); mx("M", 128 + 144 * R)
    for t in range(R):
        mx("W%d" % t, 768); mx("N%d" % t, 256)
        sb("fl%d" % t, 16); sb("m01_%d" % t, 2); sb("U%d" % t, 16, "uint16")
    for name, n in (("hn", 1024), ("hf", 576), ("hE", 516), ("hB", 1024), ("hM", 576), ("hL", 896), ("hP", 512), ("hQ", 512)): sb(name, n, "bfloat16")
    for name, n in (("pI", 1), ("rI", 1), ("gI", 1), ("aI", 1), ("bI", 1), ("yI", 256), ("wI", 256), ("rhoI", 1), ("rh", 1), ("zI", 1),
                    ("nbG", 16), ("nbH", 12), ("posI", 2), ("rgI", 6), ("npI", 6), ("nsI", 12)): sb(name, n, "int32")
    for name, n in (("pF", 1), ("mF", 256), ("rF", 1), ("gF", 1), ("o48", 48), ("s48", 48), ("t48", 48), ("z1", 1), ("z3", 1), ("M48", 48), ("Fw", 1024), ("mk", 48),
                    ("RK", 256), ("KG", 32), ("KT", 32), ("sg", 2), ("jk", 512), ("rg", 6), ("ns", 12), ("dn", 8), ("c1", 1), ("c2", 1), ("c3", 1), ("c4", 1), ("c5", 1), ("c6", 1),
                    ("c9", 1), ("EJ", 32), ("r1", 1), ("rB", 1), ("rT", 1), ("vr", 16), ("HB", 16), ("gt", 16), ("gt0", 16), ("NE", 24), ("EQ", 24), ("EB", 24), ("NH", 24), ("MK", 192),
                    ("D48", 48), ("T16", 16), ("tg", 16), ("tq", 2), ("one", 8), ("nil", 1), ("top", 1), ("loc", 2), ("wc", 2), ("m1", 8), ("m3", 8), ("m4", 8), ("m2", 1), ("b0", 1), ("b1", 1),
                    ("i17", 17), ("wR", 64), ("K96", 96), ("KA", 96), ("KB", 96), ("R96", 96), ("x2", 2), ("KF", 96), ("S96", 96), ("nm", 96), ("np", 96), ("MV", 128), ("G", 512), ("gm", 96),
                    ("gs", 96), ("SL", 600), ("jr", 256), ("ab", 256), ("S2", 2), ("GL", 4), ("e2", 2), ("th", 4), ("n2", 2), ("away", 2), ("cl", 12), ("CF", 16), ("ls", 48), ("lu", 16),
                    ("NR", 1280), ("PRp", 256), ("PRn", 256), ("yo", 256), ("FX", 1), ("FL", 16)): sb(name, n)
    for name, n in (("CR", 256), ("I", 128), ("GN", 192), ("VT", 256), ("VR", 256), ("mr", 256), ("idF", 64), ("Rp", 256)): sb(name, n, "bfloat16")
    for name, n in (("T2u", 16), ("lKG", 2), ("lNG", 1), ("nbO", 12), ("lVR", 16), ("idT", 64), ("lG", 1), ("gI0", 16), ("gU0", 6), ("gU", 6), ("lC", 1), ("lK", 6), ("posU", 16),
                    ("lst", 16), ("UA", 16), ("off", 16)): sb(name, n, "uint16")
    for i in range(8): b["ps%d" % i] = ("psum", [128, 512], "float32")
    return b


def _pack(b):
    out, place, fill = {}, {}, {"float32": 0, "int32": 0, "uint16": 0, "bfloat16": 0}
    fixed = ("nbT", "xb", "wb", "hn", "hf", "hE", "hB", "hM", "hL", "hP", "hQ", "fl0", "fl1", "fl2", "m01_0", "m01_1", "m01_2", "FX", "FL", "off", "yo")
    for name, (where, shape, d) in b.items():
        place[name] = (name, 0)
        if where != "sbuf" or d not in fill or name in fixed: out[name] = (where, shape, d)
        else:
            place[name] = ("pool_" + d, fill[d])
            fill[d] += (shape[1] + 31) // 32 * 32
    for d, n in fill.items(): out["pool_" + d] = ("sbuf", [128, n], d)
    return out, place


SCRATCH, PLACE = _pack(_bufs())
WIDTH = {k: v[1][1] for k, v in _bufs().items()}
KIND = {k: v[2] for k, v in _bufs().items()}
SEMAPHORES = ["qv", "qs", "qt", "qg", "ldn", "ldx", "ldb", "ldc", "ldw", "ls", "st"] + ["x%s%d%s" % (k, t, s) for k in "csm" for t in range(R) for s in "ab"]


def shares(T, topo, core):
    peer = {d: T.cores[T.rank_of(core) ^ d] for d in FAR}
    may = {d: topo.engines(core, c) for d, c in peer.items()}
    away = [d for d in FAR if topo.chip(peer[d]) != topo.chip(core)]
    eng, used = {}, []
    for d in sorted(FAR, key=lambda d: (d not in away, d)):
        free = [e for e in may[d] if e not in used]
        eng[d] = free[:len(may[d]) // len(away)] if d in away else free[::2]
        used += eng[d]
    return peer, eng


def norm(r): return (r[0], r[1], r[2], r[3] if len(r) > 3 else 1)
def size(r): return len(range(*norm(r)[1:]))
def bank(r): return r[0][:2] == "ps"


def clash(x, y):
    if x[2] <= y[1] or y[2] <= x[1]: return False
    return x[3] == y[3] == 1 or not set(range(*x[1:])).isdisjoint(range(*y[1:]))


LAID = []


def arrange(calls, loaded):
    if LAID: return [(calls[i], calls[i]["ways"][w]) for i, w in LAID]
    n = len(calls)
    before, seen = [dict() for _ in calls], {}
    for i, c in enumerate(calls):
        for r, w in [(norm(r), False) for r in c["rd"]] + [(norm(r), True) for r in c["wr"]]:
            for j, s, v in seen.get(r[0], ()):
                if j == i or r[0] == "issue" and w and not v: continue
                if (w or v) and clash(r, s): before[i][j] = not (c["acc"] and v and bank(r)) or before[i].get(j, False)
                elif bank(r): before[i].setdefault(j, False)
            seen.setdefault(r[0], []).append((i, r, w))
    above = [set() for _ in calls]
    for i in range(n):
        for j in before[i]: above[i] |= above[j] | {j}
        for j in [j for j in before[i] if any(j in above[k] for k in before[i])]: del before[i][j]
    after = [[] for _ in calls]
    for i in range(n):
        for j in before[i]: after[j].append(i)
    wake, chain = PACES[0]["wake"], [0.0] * n
    for i in reversed(range(n)): chain[i] = min(w[1][0] for w in calls[i]["ways"]) + calls[i]["lat"][0] + max([wake + chain[k] for k in after[i]] + [0.0])
    early = [max([loaded.get(r[0], 0.0) for r in c["rd"]] + [0.0]) for c in calls]
    left, ready, busy, at = [len(b) for b in before], [i for i in range(n) if not before[i]], {"s": [(0.0, 0.25)], "y": [(0.0, 0.4)]}, [None] * n
    while ready:
        i = max(ready, key=lambda k: chain[k])
        ready.remove(i)
        pick = None
        for x, w in enumerate(calls[i]["ways"]):
            t = max([early[i]] + [at[j][1] + calls[j]["lat"][0] + (wake if at[j][2] != w[0] else PACES[0]["own"] if hard else 0.0) for j, hard in before[i].items()])
            for a, b in busy.setdefault(w[0], []):
                if t + w[1][0] <= a: break
                t = max(t, b)
            e = t + w[1][0] + (PLAN["lean"] if w[0] == "v" else 0.0)
            if pick is None or e < pick[4]: pick = (t, t + w[1][0], w[0], x, e)
        at[i] = pick
        busy[pick[2]].append(pick[:2])
        busy[pick[2]].sort()
        for k in after[i]:
            left[k] -= 1
            if not left[k]: ready.append(k)
    order, way = sorted(range(n), key=lambda i: (at[i][0], i)), [a[3] for a in at]
    edges = [tuple(b.items()) for b in before]

    def span(order, way, start, saved):
        total, keep = 0.0, []
        queue = [calls[i]["ways"][way[i]][0] for i in range(n)]
        for s, pace in enumerate(PACES):
            wake, own = pace["wake"], pace["own"]
            if start: marks, end = saved[s][0][:start // 16 + 1], list(saved[s][1])
            else: marks, end = [{"v": 0.0, "s": 0.25, "t": 0.0, "g": 0.0, "y": 0.4, "a": 0.0, "b": 0.0}], [0.0] * n
            free = dict(marks[-1])
            for a in range(start, n):
                if a % 16 == 0 and a > start: marks.append(dict(free))
                i = order[a]
                q = queue[i]
                t = free[q]
                if early[i] > t: t = early[i]
                for j, hard in edges[i]:
                    e = end[j] + (wake if queue[j] != q else own if hard else 0.0)
                    if e > t: t = e
                c = calls[i]
                free[q] = t = t + c["ways"][way[i]][1][s]
                end[i] = t + c["lat"][s]
            total += max(end) + PLAN["mean"] * sum(end) / n
            keep.append((marks, end))
        return total, keep

    state = [PLAN["seed"]]
    def draw(k):
        state[0] = (state[0] * 1103515245 + 12345) % 2147483648
        return (state[0] >> 8) * k >> 23
    now, saved = span(order, way, 0, None)
    best, kept = now, (order, way)
    for trial in range(PLAN["tries"]):
        a = draw(n)
        i, o, w, b = order[a], order, way, a
        if len(calls[i]["ways"]) > 1 and draw(3) == 0:
            w = list(way)
            w[i] = 1 - w[i]
        else:
            lo, hi = a, a
            while lo > max(0, a - PLAN["reach"]) and o[lo - 1] not in before[i]: lo -= 1
            while hi < min(n - 1, a + PLAN["reach"]) and i not in before[o[hi + 1]]: hi += 1
            b = lo + draw(hi - lo + 1)
            q = calls[i]["ways"][way[i]][0]
            if not any(calls[k]["ways"][way[k]][0] == q for k in (o[b:a] if b < a else o[a + 1:b + 1])) and draw(4): continue
            o = list(o)
            o.insert(b, o.pop(a))
        new, keep = span(o, w, min(a, b) // 16 * 16, saved)
        if new <= now + PLAN["heat"] * (1 - trial / PLAN["tries"]) * draw(1000) / 1000:
            now, order, way, saved = new, o, w, keep
            if new < best: best, kept = new, (o, w)
    LAID.extend((i, kept[1][i]) for i in kept[0])
    return arrange(calls, loaded)


def rank_program(g, core, T, topo):
    rank = T.rank_of(core)
    if rank is None: return
    calls = []

    def each(f): return tuple(f(p) for p in PACES)
    def cycles(n): return each(lambda p: n * p["cyc"])
    def put(ways, rd, wr, acc=False, lat=None, kind="c", sem=None):
        ways = [(q, tuple(x + (p["act"] * (2 if isinstance(f, tuple) else 1) if q == "s" and kind == "c" else 0.0) for x, p in zip(t, PACES)), f) for q, t, f in ways]
        calls.append(dict(ways=ways, rd=rd, wr=wr, acc=acc, lat=lat or cycles(0), kind=kind, sem=sem))

    def ap(r, p=None):
        name, a, b, st = norm(r)
        buf, o = PLACE[name]
        rows = slice(p[0], p[1]) if p else slice(None)
        return T[buf][rows, o + a:o + b:st] if st != 1 else T[buf][rows, o + a:o + b]

    def words(r): return ap(r).bitcast(dt.uint32)
    def octets(r): return ap(r).bitcast(dt.uint8)
    def W(n): return (n, 0, WIDTH[n])
    def C(n, i): return (n, i, i + 1)
    def sc(s): return ap(s) if isinstance(s, tuple) else s
    def cols(*x): return [s for s in x if isinstance(s, tuple)]
    def real(*x): return all(KIND[r[0]] in ("float32", "bfloat16") for r in x)
    def plain(n, k=1.0, more=0): return cycles(max(64, n * k) + more)
    def twice(n): return each(lambda p: 2 * max(64, n) * p["cyc"] + p["own"])
    def narrow(*x): return 0.5 if all(KIND[r[0]] in ("bfloat16", "uint16") for r in x) else 1.0
    def picked(n, q="v"): return each(lambda p: ((60 if q == "v" else 78) + n * p["gat"]) * p["cyc"])
    def tt(out, in0, in1, op, off=None):
        if off is None: put([("v", plain(size(out), 1 if bank(in0) else 2), lambda e: e.tensor_tensor(ap(out), ap(in0), ap(in1), op))], [in0, in1], [out])
        else: put([("v", picked(size(out)), lambda e: e.tensor_tensor(ap(out), ap(in0).indirect(ap(off)), ap(in1), op))], [in0, off, in1], [out])
    def ts(out, in0, s1, op0, s2=None, op1=None):
        t = plain(size(out), narrow(out, in0))
        if op1 is None: put([("v", t, lambda e: e.tensor_scalar(ap(out), ap(in0), sc(s1), None, op0))], [in0] + cols(s1), [out])
        else: put([("v", t, lambda e: e.tensor_scalar(ap(out), ap(in0), sc(s1), sc(s2), op0, op1))], [in0] + cols(s1, s2), [out])
    def cp(out, in_, p=None, idle=False):
        ways = [("v", plain(size(out), narrow(out, in_)), lambda e: e.tensor_copy(ap(out, p), ap(in_, p)))]
        if idle: ways.append(("g", cycles(205 + 2 * size(out)), lambda e: e.affine_select(ap(out), ap(in_), [[0, size(out)]], A.is_ge, 0.0, 0, 0)))
        elif real(out, in_): ways.append(("s", plain(size(out)), lambda e: e.activation(ap(out, p), ap(in_, p), AF.Copy)))
        put(ways, [in_], [out], kind="select" if idle else "c")
    def plus(out, in_, bias, scale=1.0):
        ways = [("v", plain(size(out), narrow(out, in_)), lambda e: e.tensor_scalar(ap(out), ap(in_), sc(scale), sc(bias), A.mult, A.add))]
        if real(out, in_): ways.append(("s", plain(size(out)), lambda e: e.activation(ap(out), ap(in_), AF.Identity, bias=sc(bias), scale=sc(scale))))
        put(ways, [in_] + cols(bias, scale), [out])
    def distance(in_, col): return lambda e: e.activation(ap(("ab", 0, size(in_))), ap(in_), AF.Abs, bias=ap(col), scale=-1.0)
    def same(out, in_, col, gain=1.0):
        put([("v", plain(size(out), narrow(out, in_)), lambda e: e.tensor_scalar(ap(out), ap(in_), ap(col), gain, A.is_equal, A.mult)),
             ("s", twice(size(out)), (distance(in_, col), lambda e: e.activation(ap(out), ap(("ab", 0, size(out))), AF.Relu, bias=gain, scale=-gain)))], [in_, col], [out])
    def apart(out, in_, col, gain):
        put([("v", plain(size(out)), lambda e: e.tensor_scalar(ap(out), ap(in_), ap(col), gain, A.not_equal, A.mult)),
             ("s", twice(size(out)), (distance(in_, col), lambda e: e.activation(ap(out), ap(("ab", 0, size(out))), AF.Copy, scale=gain)))], [in_, col], [out])
    def nonzero(out, in_):
        put([("v", plain(size(out)), lambda e: e.tensor_scalar(ap(out), ap(in_), 0.0, None, A.not_equal)), ("s", plain(size(out)), lambda e: e.activation(ap(out), ap(in_), AF.Sign))], [in_], [out])
    def count(out, pattern, base, cm):
        if KIND[out[0]] == "int32": return lambda e: e.iota(ap(out), pattern, base, cm)
        return lambda e: e.iota(ap(out), pattern, base, cm, allow_small_or_imprecise_dtypes=True)
    def iota(out, pattern, base, cm): put([("g", cycles(157 + 2 * size(out)), count(out, pattern, base, cm))], [], [out], kind="iota")
    def ms(out, c): put([("v", plain(size(out), narrow(out)), lambda e: e.memset(ap(out), c)), ("g", cycles(157 + 2 * size(out)), count(out, [[0, size(out)]], int(c), 0))], [], [out], kind="iota")
    def within(out, src, cm, base, fill):
        put([("g", cycles(205 + 2 * size(out)), lambda e: e.affine_select(ap(out), ap(src), [[0, size(out)]], A.is_ge, fill, base, cm))], [src], [out], kind="select")
    def diagonal(out, zeros, c): put([("g", cycles(205 + 256), lambda e: e.affine_select(ap(out), ap(zeros), [[-1, 128]], A.not_equal, c, 0, 1))], [zeros], [out], kind="select")
    def rsum(out, in_, junk):
        put([("v", plain(size(in_)), lambda e: e.tensor_reduce(ap(out), ap(in_), AxisListType.X, A.add)),
             ("s", plain(size(in_), 1, 24), lambda e: e.activation(ap(junk), ap(in_), AF.Copy, accum_out=ap(out)))], [in_], [out, junk])
    def tp(out, in_): put([("v", plain(size(out), narrow(out, in_)), lambda e: e.transpose(ap(out), ap(in_)))], [in_], [out])
    def scan(out, d0, d1, op0, op1): put([("v", plain(size(out)), lambda e: e.tensor_tensor_scan(ap(out), ap(d0), ap(d1), 0.0, op0, op1))], [d0, d1], [out])
    def gather(out, win, off, bias=None):
        if bias is None: ways = [("v", picked(size(out)), lambda e: e.tensor_copy(ap(out), ap(win).indirect(ap(off)))), ("s", picked(size(out), "s"), lambda e: e.activation(ap(out), ap(win).indirect(ap(off)), AF.Copy))]
        else: ways = [("v", picked(size(out)), lambda e: e.tensor_scalar(ap(out), ap(win).indirect(ap(off)), bias, None, A.add)),
                      ("s", picked(size(out), "s"), lambda e: e.activation(ap(out), ap(win).indirect(ap(off)), AF.Identity, bias=bias))]
        put(ways if real(out, win) else ways[:1], [win, off], [out])
    def pick(out, win, off):
        oc, wc, os_, ws = [(r[0] + x, r[1], r[2]) for x in "cs" for r in (out, win)]
        put([("v", picked(size(oc)), lambda e: e.tensor_copy(words(oc), words(wc).indirect(ap(off))))], [wc, off], [oc])
        put([("s", picked(size(oc), "s"), lambda e: e.activation(ap(os_), ap(ws).indirect(ap(off)), AF.Copy))], [ws, off], [os_])
    def quant(out, in_):
        c, s = (out[0] + "c", out[1], out[2]), (out[0] + "s", out[1], out[2])
        put([("v", cycles(15 + 0.265 * size(in_)), lambda e: e.quantize_mx(ap(c), ap(s), ap(in_)))], [in_], [c, s])
    def mm(b, w, x, start=True, stop=True):
        n = x[2] - x[1]
        wc, ws, xc, xs = (w[0] + "c", w[1], w[2]), (w[0] + "s", w[1], w[2]), (x[0] + "c", x[1], x[2]), (x[0] + "s", x[1], x[2])
        put([("t", each(lambda p: (n + 16) * p["pe"] + p["fill"]), lambda e: e.matmul_mx(ap(("ps%d" % b, 0, n)), ap(wc), ap(ws), ap(xc), ap(xs), start, stop))], [wc, ws, xc, xs],
            [("ps%d" % b, 0, 512)], acc=not start)
    stores = [0]
    def store(q, out, in_, view):
        stores[0] += 16
        put([(q, cycles(50), lambda e: e.dma_start(out, view))], [in_], [], lat=each(lambda p: p["store"]), kind="store")

    peer, eng = shares(T, topo, core)
    side = {d: "ab"[topo.chip(c) != topo.chip(core)] for d, c in peer.items()}
    incoming = {s: sum(len(shares(T, topo, c)[1][d]) for d, c in peer.items() if side[d] == s) for s in "ab"}
    sent = [0]

    def send(way, what, sem, lands):
        tr, rd = [], []
        for d in eng:
            src, dst, region = what(d)
            rid, pid, _s = topo.addr(peer[d])
            tr.append(RemoteDMATransfer(dst_ids=[DstId(rid=rid, pnc=pid)], dma_engine_mask=sum(1 << e for e in eng[d]), remote_sem=T.sem[sem + side[d]], src=src, dst=dst))
            rd.append(region)
        put([("g", each(lambda p: p["issue"] + (0.0 if sent[0] else p["first"])), tr)], rd, [("issue", 0, 1)], kind="send")
        sent[0] += sum(len(e) for e in eng.values())
        for s in "ab":
            put([(s, each(lambda p: p["wire"][way]), None)], [("issue", 0, 1)], [lands(d) for d in eng if side[d] == s], lat=each(lambda p: p["way"]), kind="land", sem=sem + s)

    iota(W("pI"), [[0, 1]], 0, 1)
    iota(W("mF"), [[1, 256]], 0, 0)
    iota(W("o48"), [[0, 16], [1, 3]], 0, 0)
    iota(W("yI"), [[256, 16], [11, 16]], 10, 0)
    iota(W("vr"), [[16, 2], [64, 4], [0, 2]], 0, 0)
    iota(W("CR"), [[0, 8], [1, 16], [0, 2]], 0, 0)
    iota(W("HB"), [[0, 8], [256, 2]], 0, 0)
    iota(W("i17"), [[1, 17]], -1, 0)
    iota(W("tg"), [[128, 16]], int(GAIN[0]), 1)
    iota(W("tq"), [[128, 2]], 0, 1)
    ms(W("one"), 1.0)
    ms(W("nil"), 0.0)
    ms(W("top"), GAIN[2])
    within(C("loc", 0), C("one", 0), -1, F0 - 1, 0.0)
    within(C("loc", 1), C("one", 0), 1, 128 - F1, 0.0)
    within(C("wc", 0), W("top"), -1, F0 - 1, GAIN[3])
    within(C("wc", 1), W("top"), 1, 128 - F1, GAIN[3])
    within(W("m1"), W("one"), 1, -FAR[1][0], 0.0)
    within(W("m4"), W("one"), 1, 128 - FAR[3][0], 0.0)
    within(W("m2"), C("one", 0), -1, FAR[2][1] - 129, 0.0)
    within(W("b0"), W("nil"), 1, -F0, -HUGE)
    within(W("b1"), W("nil"), -1, F1 - 129, -HUGE)
    within(W("m3"), W("m4"), -1, FAR[3][1] - 129, 0.0)
    plus(W("away"), W("loc"), 1.0, -1.0)
    ts(W("rI"), W("pI"), 15, A.bitwise_and)
    ts(W("gI"), W("pI"), 4, A.logical_shift_right)
    ts(W("aI"), W("pI"), 96, A.bitwise_and)
    ts(W("bI"), W("pI"), 1, A.bitwise_and)
    cp(W("rF"), W("rI"))
    cp(W("gF"), W("gI"))
    iota(W("pF"), [[0, 1]], 0, 1)
    plus(W("r1"), W("rF"), 1.0)
    plus(W("rB"), W("rF"), -OWN)
    plus(W("rT"), W("rF"), GAIN[0])
    plus(W("c6"), W("rF"), W("gF"), 8.0)
    ms(W("hE"), 0.0)
    diagonal(W("I"), ("hE", 0, 512, 4), 1.0)
    diagonal(("hE", 3, 515, 4), ("hE", 3, 515, 4), 0.5)
    def Eb(b): return ("E", 128 * b, 128 * b + 128)
    for b in range(4): quant(Eb(b), ("hE", 3 - b, 515 - b))
    for i in range(2): same(("hP", i, 512, 2), W("CR"), W("rF"), OWN)
    quant(("D", 272, 400), W("hP"))
    ms(("hL", 384, 896), 0.0)
    ms(W("hM"), 0.0)
    ts(W("NE"), ("mF", 0, 24), -8.0, A.add, W("gF"), A.not_equal)
    plus(W("EQ"), W("NE"), 1.0 / OWN, -1.0 / OWN)
    plus(W("EB"), W("NE"), 0.0, -HUGE)
    plus(W("NH"), W("NE"), 0.0, HUGE)
    for k in range(3):
        for h in range(2):
            a = 32 * (2 * k + h) + (16 if k == 2 else 0)
            cp(("MK", a, a + 16), ("NH" if k == 2 else "EB", 8 - 8 * h, 24 - 8 * h), None, True)
    same(W("KF"), ("CR", 0, 192, 2), W("rF"))
    cp(("K96", 0, 64), ("KF", 0, 64))
    within(("K96", 64, 80), ("KF", 0, 16), -1, F0 - 1, 0.0)
    within(("K96", 80, 96), ("KF", 0, 16), 1, 128 - F1, 0.0)
    plus(W("KA"), W("K96"), -HUGE, HUGE)
    ts(W("R96"), ("CR", 0, 192, 2), 0.0, A.is_equal, -HUGE, A.mult)
    cp(W("lK"), ("mF", 0, 6))
    nonzero(W("S96"), ("CR", 0, 192, 2))
    nonzero(W("s48"), W("o48"))
    ms(W("cl"), 0.0)
    ms(W("D48"), 0.0)
    plus(("D48", 2, 48, 3), ("mF", 0, 256, 16), W("rB"))
    plus(W("T16"), ("mF", 0, 256, 16), W("rT"))
    plus(W("c9"), W("gF"), 2.0, 3.0)
    ts(W("lC"), W("bI"), 24.0, A.mult, W("c9"), A.add)
    tt(("tg", 4, 6), W("tq"), W("wc"), A.add)
    ts(W("lG"), W("c6"), 16.0, A.add, 63.0, A.min)
    quant(("X", 0, 256), W("xb"))
    quant(("wq", 0, 128), W("wb"))

    for q in range(4): plus(("Fw", 256 * q, 256 * q + 256), W("mF"), 1048576.0 * (q ^ rank), 4096.0 if q < rank else 0.0)
    ts(W("zI"), W("rI"), 2.0 / 3.0, A.mult, 1.0 / 3.0, A.add)
    ts(W("z1"), W("rI"), 2.0, A.mult, 2.0, A.add)
    ts(W("z3"), W("zI"), -3.0, A.mult, W("z1"), A.add)
    ts(W("M48"), W("o48"), W("z3"), A.is_equal)
    ts(W("wI"), W("yI"), 3855, A.bitwise_and)
    tt(W("mk"), W("nbT"), W("M48"), A.mult)
    scan(W("t48"), W("s48"), W("mk"), A.mult, A.add)
    cp(W("T2u"), ("t48", 2, 48, 3))
    tt(W("RK"), W("Fw"), W("wI"), A.add, W("T2u"))
    ts(W("rh"), W("rF"), 3.0, A.mult, 2.0, A.add)
    ts(W("rhoI"), W("rh"), 15, A.bitwise_and)
    plus(W("c2"), W("gF"), 0.0, 32.0)
    ts(W("c1"), W("rhoI"), W("c2"), A.add)
    ts(W("lKG"), ("mF", 0, 32, 16), W("c1"), A.add)
    gather(W("KG"), W("RK"), W("lKG"))
    tp(W("KT"), W("KG"))
    for u in range(2):
        def sign(jk, b, o): put([("s", plain(256, 1, 24), lambda e: e.activation(ap(jk), ap(W("RK")), AF.Sign, bias=ap(b), scale=-1.0, accum_out=ap(o)))], [W("RK"), b], [jk, o])
        sign(("jk", 256 * u, 256 * u + 256), C("KT", 16 * u), C("sg", u))
    ts(W("posI"), W("sg"), 0.5, A.mult, 127.5 + F1, A.add)
    ts(("rgI", 0, 2), W("posI"), 15, A.bitwise_and)
    ts(("rgI", 2, 4), W("posI"), 4, A.logical_shift_right, 15, A.bitwise_and)
    ts(("rgI", 4, 6), W("posI"), 240, A.bitwise_and)
    cp(W("rg"), W("rgI"))
    plus(W("c3"), W("gF"), W("rF"), 6.0)
    ts(W("lNG"), W("c3"), 47.0, A.min)
    gather(W("nbG"), W("nbT"), W("lNG"))
    ts(("nbH", 0, 6), ("nbG", 0, 6), 240, A.bitwise_and)
    ts(("nbH", 6, 12), ("nbG", 0, 6), 15, A.bitwise_and)
    cp(W("nbO"), W("nbH"))
    gather(W("GN"), W("mF"), W("nbO"))
    ms(("VT", 0, 64), 0.0)
    ts(W("c4"), W("aI"), W("pF"), A.add, W("rF"), A.subtract)
    plus(("VT", 0, 32, 16), ("mF", 0, 64, 32), W("c4"))
    plus(("VT", 32, 64, 16), ("mF", 0, 2), W("rF"), 0.0)
    for k in range(3): tp(("VT", 64 * k + 64, 64 * k + 128), ("GN", k, 192, 3))
    ts(W("c5"), W("bI"), 32.0, A.mult)
    ts(W("lVR"), W("vr"), W("c5"), A.add)
    gather(W("VR"), W("VT"), W("lVR"))
    for u in range(2): same(("mr", 128 * u, 128 * u + 128), ("CR", 0, 128), C("rg", 2 + u))
    for u in range(2): same(("hB", u, 512, 2), W("CR"), C("rg", u))
    for u in range(2): tt(("hB", 512 + u, 768, 2), ("mr", 128 * u, 128 * u + 128), ("VR", 128 * u, 128 * u + 128), A.mult)
    for u in range(2):
        same(("EJ", 16 * u, 16 * u + 16), ("mF", 0, 256, 16), C("VT", 16 * u), 1.0 / OWN)
        for lo in range(2): plus(("hB", 768 + u + 2 * lo, 832, 4), ("EJ", 16 * u, 16 * u + 16), 0.0, C("rg", u if lo else 4 + u))
    quant(("B", 0, 128), ("hB", 0, 512))
    quant(("B", 128, 256), ("hB", 512, 1024))
    mm(2, ("B", 0, 128), ("B", 128, 256))
    mm(3, ("D", 272, 400), ("B", 128, 256))
    cp(W("posU"), ("ps3", 64, 80))
    cp(W("idT"), ("ps2", 0, 64))
    cp(W("idF"), ("ps2", 0, 64))
    cp(("idF", 48 + F0 // 16, 48 + F1 // 16), ("ps2", F0 // 16, F1 // 16))
    pick(("W0", 0, 256), ("X", 0, 256), ("idT", 0, 16))
    tt(W("gt0"), W("idF"), W("HB"), A.add, W("lG"))
    cp(W("gU0"), ("gt0", 0, 6))

    gather(W("Rp"), W("mF"), W("posU"))
    gather(W("gI0"), W("idF"), W("lG"))
    tt(W("nm"), W("Rp"), W("KF"), A.mult, ("gI0", 0, 6))
    scan(W("np"), W("S96"), W("nm"), A.mult, A.add)
    cp(W("npI"), ("np", 15, 96, 16))
    tt(("gt", 0, 6), ("np", 15, 96, 16), ("HB", 0, 6), A.add)
    cp(W("gU"), ("gt", 0, 6))
    ts(("nsI", 0, 12, 2), W("npI"), 240, A.bitwise_and)
    ts(("nsI", 1, 12, 2), W("npI"), 15, A.bitwise_and)
    cp(W("ns"), W("nsI"))
    for i in range(2): tt(("dn", 4 * i, 4 * i + 4), ("ns", 8 * i, 8 * i + 4), ("ns", 4, 8), A.subtract)
    for h in range(2):
        for lo in range(2):
            eq = ("EQ", 8 - 8 * h, 24 - 8 * h)
            plus(("hL", 512 + h + 2 * lo, 576, 4), eq, 0.0, C("ns", 4 + 2 * h + lo))
            for i in range(2): plus(("MV", 64 * i + 32 * h + lo, 64 * i + 32 * h + 32, 2), eq, 0.0, C("dn", 4 * i + 2 * h + lo))
    quant(("D", 144, 272), ("hL", 384, 896))
    for i in range(4): same(("hQ", i, 512, 4), ("CR", 0, 256, 2), C("ns", 2 * i + 1), GAIN[i // 2])
    quant(("SQ", 0, 128), W("hQ"))
    for i in range(6):
        a = 32 * i + (0 if i >= 4 else 16)
        apart(("MK", a, a + 16), ("mF", 0, 256, 16), C("ns", 2 * i), HUGE if i >= 4 else -HUGE)
    for h in range(2): ts(("wR", 32 * h, 32 * h + 17), W("i17"), C("ns", 9 + 2 * h), A.is_equal, C("wc", h), A.mult)
    for i in range(2): ms(("NR", 256 * i, 256 * i + 256), -1.0)
    for k in range(3): gather(("NR", 512 + 256 * k, 768 + 256 * k), W("mF"), ("idT", 16 + 16 * k, 32 + 16 * k), 256.0 * rank)
    for d, (a, b) in FAR.items(): plus(("NR", 256 + a, 256 + b), ("NR", 1024 + a, 1024 + b), 256.0 * ((rank ^ d) - rank))

    def S(i): return C("gs", 16 * i + 15)
    def SS(k): return ("gs", 32 * k + 15, 32 * k + 32, 16)
    quant(("M", 0, 128), W("hP"))

    for t in range(R):
        w, near, m, fl, o = "W%d" % t, "N%d" % t, "m01_%d" % t, "fl%d" % t, 128 + 144 * t
        for way, kind, view in ((2, "c", octets), (1, "s", ap)):
            def there(d): return ("M" + kind, FAR[d][0] + o - F0, FAR[d][1] + o - F0)
            send(way, lambda d: (view((w + kind,) + FAR[d]), view(there(d)), (w + kind,) + FAR[d]), "x%s%d" % (kind, t), there)
        for h in range(2): mm(h, (w, 128 * h, 128 * h + 128), (w, 0, 256) if t else ("X", 0, 256))
        for h in range(2): cp(("G", 256 * h, 256 * h + 256), ("ps%d" % h, 0, 256))
        if t: tt(W("KB"), W("cl"), W("KA"), A.add, W("lK"))
        tt(W("gm"), W("G"), W("KB" if t else "KA"), A.add, W("gU" if t else "gU0"))
        scan(W("gs"), W("R96"), W("gm"), A.add, A.max)
        for h in range(2): ts(C("x2", h), C("cl", 4 + h), C("away", h), A.mult)
        for h in range(2): plus(C("SL", 499 + 100 * h), S(4 + h), C("x2", h), C("loc", h))
        tt(W(m), SS(0), SS(1), A.max)
        send(0, lambda d: (ap(C(m, FAR[d][0] // 128)), ap(C(fl, 4 * d)), C(m, FAR[d][0] // 128)), "xm%d" % t, lambda d: C(fl, 4 * d))
        tt(("GL", 2, 4), SS(0), SS(1), A.is_ge)
        plus(("GL", 0, 2), ("GL", 2, 4), 1.0, -1.0)
        for h in range(2): ts(C("e2", h), S(4 + h), C(m, h), A.is_gt, C("loc", h), A.mult)
        for h in range(2): ts(C("n2", h), S(4 + h), C(m, h), A.is_le, C("away", h), A.max)
        for i in range(4): plus(C("th", i), C("GL", i), S(i), -HUGE)
        for h in range(2):
            ts(("hL", 384 + h, 448, 2), ("MV", 32 * h, 32 * h + 32), C("GL", 2 + h), A.mult, C("n2", h), A.mult)
            plus(("hL", 448 + h, 512, 2), ("MV", 64 + 32 * h, 96 + 32 * h), 0.0, C("e2", h))
        quant(("D", 48, 176), ("hL", 0, 512))
        for i in (2, 0, 1): mm(0, ("D", 272, 400), ("D", 144 + 16 * i, 272 + 16 * i), i == 2, i == 1)
        cp(W("lst"), ("ps0", 0, 16))
        pick((near, 0, 256), (w, 0, 256), W("lst"))
        for b in range(4):
            mm(4 + b, Eb(b), (w, 0, 256), True, False)
            mm(4 + b, Eb(b), (near, 0, 256), False, True)
            cp(("hn", b, 1024, 4), ("ps%d" % (4 + b), 0, 256))
        quant((w, 512, 768), W("hn"))
        for h in range(2): mm(2 + h, (w, 128 * h, 128 * h + 128), ("M", o - 80 + 96 * h, o + 48 + 96 * h))
        tt(("SL", 451, 499), ("ps2", F0, 128), ("I", F0, 128), A.mult)
        tt(("SL", 503, 599), ("ps3", 32, 128), ("I", 0, 96), A.mult)
        for b, k in enumerate((1, 0, 3, 1)):
            mm(k, Eb(b), (w, F0, F1), True, False)
            mm(k, Eb(b), ("M", o, o + 144), False, True)
            cp(("hf", b, 576, 4), ("ps%d" % k, 0, 144))
        quant((w, 256 + F0, 256 + F1), W("hf"))
        rsum(C("S2", 0), ("SL", 451, 500), ("jr", 0, 49))
        rsum(C("S2", 1), ("SL", 503, 600), ("jr", 128, 225))
        for h in range(2):
            for k in range(2): ts(("hM", 192 + 6 * k + h, 192 + 6 * k + h + 373, 12), ("MK", 32 * (2 * k + h), 32 * (2 * k + h) + 32), C("th", 2 * k + h), A.add, C("S2", h), A.is_ge)
            ts(("hM", 8 + h, 8 + h + 373, 12), ("MK", 128 + 32 * h, 160 + 32 * h), C(m, h), A.add, C("S2", h), A.is_lt)
        quant(("D", 0, 144), W("hM"))
        mm(2, ("D", 272, 400), ("D", 48, 176), True, False)
        mm(2, ("SQ", 0, 128), ("D", 96, 224), False, False)
        plus(W("FX"), W("m2"), W("b1"), C(fl, 8))
        plus(("FL", 0, 8), W("m1"), W("b0"), C(fl, 4))
        plus(("FL", 8, 16), W("m3"), W("FX"), C(fl, 12))
        for h in range(2): ts(("off", 8 * h, 8 * h + 8), ("FL", 8 * h, 8 * h + 8), C("S2", h), A.is_lt, W("r1"), A.mult)
        for h in range(2): gather(("hB", h, 512, 4), ("wR", 32 * h, 32 * h + 17), ("off", 8 * h, 8 * h + 8))
        quant(("SR", 0, 128), ("hB", 0, 512))
        mm(2, ("SR", 0, 128), ("D", 0, 128), False, True)
        scan(W("ls"), ("ps2", 0, 48), W("D48"), A.max, A.add)
        tt(W("lu"), ("ls", 2, 48, 3), W("T16"), A.min)
        cp(W("U%d" % t), W("lu"))
        pick(("W%d" % (t + 1) if t < R - 1 else "H", 0, 256), (w, 0, 768), W("U%d" % t))
        cp(W("UA"), ("ls", 2, 48, 3), ((0, 32), (32, 64), (64, 128))[t])
        if t < R - 1:
            tt(W("CF"), W("ls"), W("tg"), A.is_equal, W("lC"))
            plus(("cl", 6 * t, 6 * t + 6), ("CF", 0, 6), 0.0, -BIG)
        if t == 1: tt(("cl", 0, 6), ("cl", 0, 6), ("cl", 6, 12), A.add)

    for h in range(2): pick(("Z", 128 * h, 128 * h + 128), ("H", 0, 256), ("posU", 8 * h, 8 * h + 8))
    store("y", T.oc[:, :], ("Zc", 0, 256), octets(("Zc", 0, 256)))
    for k in range(4): store("y", T.osc[4 * k:4 * k + 4, :], ("Zs", 0, 256), T.Zs[32 * k:32 * k + 4, 0:256])
    for h in range(2):
        half = ("yo", 128 * h, 128 * h + 128)
        mm(h, ("wq", 0, 128), ("Z", 128 * h, 128 * h + 128))
        cp(half, ("ps%d" % h, 0, 128))
        store("sy"[h], T.y[:, 128 * h:128 * h + 128], half, ap(half))
    gather(W("PRp"), W("NR"), W("UA"))
    gather(W("PRn"), W("PRp"), W("posU"))
    for i in range(R): store("y", T.pr[i:i + 1, :], W("PRn"), ap(W("PRn"), (32 * i, 32 * i + 1)))

    queues = {"v": g.vector, "s": g.scalar, "t": g.tensor, "g": g, "y": g.sync}
    done = {q: 0 for q in "vstg"}
    known = {q: {} for q in queues}
    writes, reads, last, pair = {}, {}, [None], [0]

    def wait(q, evs):
        for sem, val, snap, _q in sorted(evs, key=lambda e: -e[1]):
            if known[q].get(sem, 0) >= val: continue
            queues[q].wait_ge(T.sem[sem], val)
            known[q][sem] = val
            for k, v in snap.items(): known[q][k] = max(known[q].get(k, 0), v)

    def made(rd): return [e for r in map(norm, rd) for w, e in writes.get(r[0], []) if clash(w, r)]

    def note(ev, rd, wr):
        for r in rd: reads.setdefault(r[0], []).append((norm(r), ev))
        for r in map(norm, wr):
            inside = lambda w: w == r or w[1] >= r[1] and w[2] <= r[2] and r[3] == 1
            writes[r[0]] = [(w, e) for w, e in writes.get(r[0], []) if not inside(w)] + [(r, ev)]
            reads[r[0]] = [(w, e) for w, e in reads.get(r[0], []) if not inside(w)]

    for i in range(8): queues["ys"[i % 2]].dma_start(T.nbT[16 * i:16 * i + 16, :], T.nb[:, :]).then_inc(T.sem.ldn, 16)
    note(("ldn", 128, {}, "d"), [], [W("nbT")])
    for sem, region, src in (("ldx", W("xb"), T.x[:, :]), ("ldb", ("hB", 832, 1024), T.x[:, 0:192]), ("ldc", ("hL", 0, 384), T.x[:, 0:384]), ("ldw", W("wb"), T.w[:, :])):
        g.sync.dma_start(ap(region), src).then_inc(T.sem[sem], 16)
        note((sem, 16, {}, "d"), [], [region])

    for c, (q, _t, call) in arrange(calls, {"nbT": PLAN["load"][0], "xb": PLAN["load"][1], "wb": PLAN["load"][1]}):
        if c["kind"] == "send":
            wait("g", made(c["rd"]))
            g.remote_dma_fused(call, local_sem=T.sem.ls)
            continue
        if c["kind"] == "land":
            note((c["sem"], incoming[q], {}, "d"), [], c["wr"])
            continue
        evs = made(c["rd"]) + [e for r in c["rd"] if bank(r) for w, e in reads.get(r[0], []) if e[3] != q]
        for r in map(norm, c["wr"]):
            evs += [e for w, e in writes.get(r[0], []) if clash(w, r) and not (c["acc"] and e[3] == "t")]
            evs += [e for w, e in reads.get(r[0], []) if clash(w, r)]
        if q == "g":
            if last[0] not in (None, c["kind"]): evs.append(("qg", done["g"], {}, "g"))
            last[0] = c["kind"]
        wait(q, evs)
        if c["kind"] == "store": call(queues[q]).then_inc(T.sem.st, 16)
        else:
            if isinstance(call, tuple):
                wait(q, [("q" + q, pair[0], {}, q)])
                done[q] += 1
                call[0](queues[q]).then_inc(T.sem["q" + q], 1)
                wait(q, [("q" + q, done[q], {}, q)])
                call, pair[0] = call[1], done[q] + 1
            done[q] += 1
            call(queues[q]).then_inc(T.sem["q" + q], 1)
            note(("q" + q, done[q], dict(known[q]), q), c["rd"], c["wr"])
    g.sync.wait_ge(T.sem.st, stores[0])
    g.wait_ge(T.sem.ls, sent[0])
    wait("g", [("q" + q, done[q], {}, q) for q in done])
